import numpy as np
import ml_dtypes


def mxq(x, axis, fmt="e4m3"):
    dtype, down = {"e4m3": (ml_dtypes.float8_e4m3fn, 7), "e5m2": (ml_dtypes.float8_e5m2, 14)}[fmt]
    v = np.moveaxis(np.asarray(x, np.float32).astype(ml_dtypes.bfloat16).astype(np.float64), axis, -1)
    blocks = v.reshape(v.shape[:-1] + (-1, 32))
    amax = np.abs(blocks).max(-1, keepdims=True)
    byte = np.maximum(np.where(amax > 0, np.frexp(amax)[1] - 1 + 127, 0) - down, 1)
    scale = np.exp2(byte - 127.0)
    codes = (blocks / scale).astype(np.float32).astype(dtype).astype(np.float64)
    return np.moveaxis((codes * scale).reshape(v.shape), -1, axis)


WIDE = False


def mx_kscale(k):
    if not WIDE:
        return np.ones(k)
    levels = np.array([10, -10, 5, -5, 0])
    if k % 512:
        return np.exp2(np.random.permutation(np.resize(levels, k // 32))).repeat(32)
    a = np.empty((k // 512, 16))
    for p in range(k // 512):
        a[p, :8] = np.random.permutation(np.resize(levels, 8))
        for g in range(8):
            far = levels[np.abs(levels - a[p, g]) >= 10]
            a[p, g + 8] = far[np.random.randint(len(far))]
    return np.exp2(a.ravel()).repeat(32)


def f64(x):
    return np.asarray(x).astype(np.float64)


def striped(idx):
    return np.tile(idx.reshape(-1, 16).T, (8, 1)).astype(np.uint16)


def unstriped(offs):
    return offs[:16].T.reshape(-1).astype(np.int64)


E2M1 = np.array([0.0, 0.5, 1.0, 1.5, 2.0, 3.0, 4.0, 6.0, -0.0, -0.5, -1.0, -1.5, -2.0, -3.0, -4.0, -6.0])


def pack_weight(w, fmt):
    k, n = w.shape
    w = f64(np.asarray(w, np.float32).astype(ml_dtypes.bfloat16)).reshape(k // 32, 32, n)
    amax = np.abs(w).max(1)
    if fmt == "e4m3":
        byte = np.frexp(amax)[1] - 1 + 127 - 7
    else:
        mant, ex = np.frexp(amax / 6.0)
        byte = np.where(mant > 0.5, ex, ex - 1) + 127
    byte = np.clip(np.where(amax > 0, byte, 1), 1, 254)
    scaled = (w * np.exp2(127.0 - byte)[:, None, :]).reshape(k, n).astype(np.float32)
    by_word = np.ascontiguousarray(scaled.reshape(k // 512, 128, 4, n).transpose(0, 1, 3, 2))
    if fmt == "e4m3":
        words = by_word.astype(ml_dtypes.float8_e4m3fn).view(np.uint8)
    else:
        c = by_word.astype(ml_dtypes.float4_e2m1fn).view(np.uint8) & 0xF
        words = (c[..., 0::2] | (c[..., 1::2] << 4)).reshape(k // 512, 128, 2 * n)
    return np.ascontiguousarray(words), np.ascontiguousarray(byte.astype(np.uint8).reshape(k // 512, 16, n))


def unpack_weight(words, scales, fmt):
    g, _, n = scales.shape
    words = np.ascontiguousarray(words).reshape(g, 128, n, -1)
    if fmt == "e4m3":
        vals = words.view(ml_dtypes.float8_e4m3fn).astype(np.float64)
    else:
        nib = np.empty((g, 128, n, 4), np.uint8)
        nib[..., 0::2] = words & 0xF
        nib[..., 1::2] = words >> 4
        vals = E2M1[nib]
    vals = vals * np.repeat(np.exp2(scales.astype(np.float64) - 127.0), 8, axis=1)[..., None]
    return vals.transpose(0, 1, 3, 2).reshape(g * 512, n)


def gelu(v):
    return 0.5 * v * (1.0 + np.tanh(np.sqrt(2.0 / np.pi) * (v + 0.044715 * v**3)))


K, T, S, P, H, N = 1024, 4096, 1024, 512, 1024, 768

def setup_inputs():
    n = np.random.standard_normal
    s = mx_kscale(K)[:, None]
    u = mx_kscale(H)[:, None]
    tab_words, tab_scales = pack_weight(n((K, T)) * s, "e4m3")
    w1 = (n((K, H)) / np.sqrt(K) / s * u.T).astype(np.float32)
    b1 = (0.4 * n(H) * u[:, 0]).astype(np.float32)
    w2_words, w2_scales = pack_weight(n((H, N)) / np.sqrt(H) / u, "e2m1")
    b2 = (0.4 * n(N)).astype(np.float32)
    offs = striped(np.random.permutation(T)[:S])
    pos1 = striped(np.random.permutation(S)[:P])
    pos2 = striped(np.random.permutation(S)[:P])
    return {"tab_words": tab_words, "tab_scales": tab_scales, "w1": w1, "b1": b1,
            "w2_words": w2_words, "w2_scales": w2_scales, "b2": b2,
            "offs": offs, "pos1": pos1, "pos2": pos2}

def reference(tab_words, tab_scales, w1, b1, w2_words, w2_scales, b2, offs, pos1, pos2):
    v = unpack_weight(tab_words, tab_scales, "e4m3")[:, unstriped(offs)]
    w1q = mxq(f64(w1), 0, "e4m3")
    h = (w1q.T @ v) + f64(b1)[:, None]
    a = h[:, unstriped(pos1)]
    b = h[:, unstriped(pos2)]
    z = np.maximum(np.maximum(a, b), 0.0)
    zq = mxq(z, 0, "e4m3")
    w2 = unpack_weight(w2_words, w2_scales, "e2m1")
    return (w2.T @ zq) + f64(b2)[:, None]

@@ -1,0 +1,279 @@
+from contextlib import ExitStack
+
+import concourse.mybir as mybir
+
+K, T, S, PAIRS, H, N = 1024, 4096, 1024, 512, 1024, 768
+FLOPS = 2 * K * H * S + 2 * H * N * PAIRS
+
+F32 = mybir.dt.float32
+BF16 = mybir.dt.bfloat16
+I32 = mybir.dt.int32
+U32 = mybir.dt.uint32
+U16 = mybir.dt.uint16
+U8 = mybir.dt.uint8
+FP8X4 = mybir.dt.float8_e4m3fn_x4
+FP4X4 = mybir.dt.float4_e2m1fn_x4
+ACT = mybir.ActivationFunctionType
+ALU = mybir.AluOpType
+
+P = 128
+PACK = 4
+K_PASS = P * PACK
+BANK = 512
+LIST_ROWS = 16
+N_TILES = N // P
+GROUP = 128
+LAST_PASS_PARTS = [(0, 256), (256, 128), (384, 128)]
+
+
+def tile_list_point_pair_max_kernel(
+    tc, tab_words, tab_scales, w1, b1, w2_words, w2_scales, b2, offs, pos1, pos2, out
+):
+    nc = tc.nc
+    with ExitStack() as ctx:
+        lists = ctx.enter_context(tc.tile_pool(name="lists", bufs=1))
+        keep = ctx.enter_context(tc.tile_pool(name="keep", bufs=1))
+        psum = ctx.enter_context(tc.psum_pool(name="psum", bufs=1))
+
+        def sb(shape, dtype, name):
+            return keep.tile(shape, dtype, name=name, align_bytes=64)
+
+        def bank(i, name):
+            return psum.tile([P, BANK], F32, name=name, tag="bank%d" % i)
+
+        offs_sb = lists.tile([P, S // LIST_ROWS], U16, name="offs_sb")
+        pos_sb = [lists.tile([P, PAIRS // LIST_ROWS], U16, name="pos%d_sb" % i) for i in (1, 2)]
+
+        tab_w = [sb([P, T], I32, "tab_w%d" % a) for a in range(2)]
+        tab_s = sb([P, T], U8, "tab_s")
+        w2_w = sb([P, 2, 2 * N], U8, "w2_w")
+        w2_s = sb([P, 2, N], U8, "w2_s")
+        b1_sb = sb([P, 2, PACK], F32, "b1_sb")
+        b2_sb = sb([P, N_TILES], F32, "b2_sb")
+
+        nc.vector.memset(tab_s[:].bitcast(I32), 0)
+        nc.vector.memset(w2_s[:].rearrange("p b n -> p (b n)").bitcast(I32), 0)
+
+        def load_table_scales(a):
+            for q in range(4):
+                nc.sync.dma_start(
+                    out=tab_s[32 * q + 4 * a : 32 * q + 4 * a + 4, :].bitcast(I32),
+                    in_=tab_scales[a, 4 * q : 4 * q + 4, :].bitcast(I32),
+                )
+
+        def load_table(a):
+            nc.sync.dma_start(out=tab_w[a][:], in_=tab_words[a].rearrange("p t i -> p (t i)").bitcast(I32))
+
+        raw = {}
+
+        def load_w1(a, b, m0, mn):
+            t_raw = sb([P, PACK, PACK * mn], F32, "w1_raw_%d_%d_%d" % (a, b, m0))
+            cols = slice(b * K_PASS + PACK * m0, b * K_PASS + PACK * (m0 + mn))
+            nc.sync.dma_start(
+                out=t_raw[:],
+                in_=w1[a * K_PASS : (a + 1) * K_PASS, cols].rearrange("(p j) c -> p j c", j=PACK),
+            )
+            raw.setdefault((a, b), []).append((t_raw, m0, mn))
+
+        nc.sync.dma_start(offs_sb[:], offs)
+        load_table(0)
+        nc.sync.dma_start(pos_sb[0][:], pos1)
+        nc.sync.dma_start(pos_sb[1][:], pos2)
+        load_table_scales(0)
+        load_w1(0, 0, 0, P)
+        load_table_scales(1)
+        load_table(1)
+        nc.sync.dma_start(out=b1_sb[:], in_=b1.rearrange("(b p t) -> p b t", b=2, t=PACK))
+        load_w1(1, 0, 0, P // 2)
+        load_w1(1, 0, P // 2, P // 2)
+        load_w1(0, 1, 0, P)
+        load_w1(1, 1, 0, P)
+        nc.sync.dma_start(out=w2_w[:].bitcast(I32), in_=w2_words.rearrange("b p n -> p b n").bitcast(I32))
+        for q in range(4):
+            nc.sync.dma_start(
+                out=w2_s[32 * q : 32 * q + 4, :, :].bitcast(I32),
+                in_=w2_scales[:, 4 * q : 4 * q + 4, :].rearrange("b r n -> r b n").bitcast(I32),
+            )
+        with nc.allow_non_contiguous_dma(reason="one bias value to a partition"):
+            nc.sync.dma_start(out=b2_sb[:], in_=b2.rearrange("(c p) -> p c", p=P))
+
+        v_w = [sb([P, S], U32, "v_w%d" % a) for a in range(2)]
+        v_s = sb([P, S], U8, "v_s")
+
+        def gather_words(a, j0, jn):
+            nc.vector.tensor_copy(
+                v_w[a][:, j0 : j0 + jn],
+                tab_w[a][:].bitcast(U32).indirect(offs_sb[:, j0 // LIST_ROWS : (j0 + jn) // LIST_ROWS]),
+            )
+
+        grouped, w1_c, w1_s = {}, {}, {}
+
+        def cast_w1(a, b, u):
+            g = sb([P, 2, P, PACK], BF16, "w1_g_%d_%d_%d" % (a, b, u))
+            grouped[a, b, u] = g
+            for t_raw, m0, mn in raw[a, b]:
+                nc.scalar.copy(
+                    out=g[:, :, m0 : m0 + mn, :].rearrange("p t m j -> p m j t"),
+                    in_=t_raw[:].rearrange("p j (m t) -> p m j t", t=PACK)[:, :, :, 2 * u : 2 * u + 2],
+                )
+
+        def quantize_w1(a, b, u):
+            w1_c[a, b, u] = sb([P, 2 * P], U32, "w1_c_%d_%d_%d" % (a, b, u))
+            w1_s[a, b, u] = sb([P, 2 * P], U8, "w1_s_%d_%d_%d" % (a, b, u))
+            nc.vector.quantize_mx(
+                out=w1_c[a, b, u][:].bitcast(FP8X4),
+                scales=w1_s[a, b, u][:],
+                in_=grouped[a, b, u][:].rearrange("p t m j -> p (t m j)"),
+            )
+
+        h_ps = {}
+
+        def h_pass(a, b, t, half):
+            if a == 0:
+                h_ps[b, t, half] = bank(2 * t + half, "h_ps_%d_%d_%d" % (b, t, half))
+            m_cols = slice((t % 2) * P, (t % 2 + 1) * P)
+            j_cols = slice(half * BANK, (half + 1) * BANK)
+            nc.tensor.matmul_mx(
+                out=h_ps[b, t, half][:],
+                lhsT=w1_c[a, b, t // 2][:, m_cols].bitcast(FP8X4),
+                lhsT_scale=w1_s[a, b, t // 2][:, m_cols],
+                rhs=v_w[a][:, j_cols].bitcast(FP8X4),
+                rhs_scale=v_s[4 * a :, j_cols],
+                start=(a == 0),
+                stop=(a == 1),
+            )
+
+        h = {(b, t): sb([P, S], F32, "h_%d_%d" % (b, t)) for b in range(2) for t in range(PACK)}
+
+        def h_out(b, t, half, on_vector=False):
+            dst = h[b, t][:, half * BANK : (half + 1) * BANK]
+            bias = b1_sb[:, b, t : t + 1]
+            if on_vector:
+                nc.vector.tensor_scalar(dst, h_ps[b, t, half][:], bias, 0.0, ALU.add, ALU.max)
+            else:
+                nc.scalar.activation(dst, h_ps[b, t, half][:], ACT.Relu, bias=bias)
+
+        picked, z_g, z_c, z_s = {}, {}, {}, {}
+
+        def gather_h(b, t, q0, qn):
+            for i in range(2):
+                if t == 0:
+                    picked[b, q0, i] = sb([P, PACK, qn], F32, "picked_%d_%d_%d" % (b, q0, i))
+                nc.vector.tensor_copy(
+                    picked[b, q0, i][:, t, :],
+                    h[b, t][:].indirect(pos_sb[i][:, q0 // LIST_ROWS : (q0 + qn) // LIST_ROWS]),
+                )
+
+        def pair_max(b, q0, qn):
+            z_g[b, q0] = sb([P, qn, PACK], BF16, "z_g_%d_%d" % (b, q0))
+            nc.vector.tensor_tensor(
+                z_g[b, q0][:].rearrange("p (c i) t -> p c t i", i=2),
+                picked[b, q0, 0][:].rearrange("p t (c i) -> p c t i", i=2),
+                picked[b, q0, 1][:].rearrange("p t (c i) -> p c t i", i=2),
+                ALU.max,
+            )
+
+        def quantize_z(b, q0, qn):
+            z_c[b, q0] = sb([P, qn], U32, "z_c_%d_%d" % (b, q0))
+            z_s[b, q0] = sb([P, qn], U8, "z_s_%d_%d" % (b, q0))
+            nc.vector.quantize_mx(
+                out=z_c[b, q0][:].bitcast(FP8X4),
+                scales=z_s[b, q0][:],
+                in_=z_g[b, q0][:].rearrange("p q t -> p (q t)"),
+            )
+
+        def out_pass(b, c, q, z0):
+            z_cols = slice(q - z0, q - z0 + GROUP)
+            nc.tensor.matmul_mx(
+                out=o_ps[c][:, q : q + GROUP],
+                lhsT=w2_w[:, b, 2 * P * c : 2 * P * (c + 1)].bitcast(FP4X4),
+                lhsT_scale=w2_s[:, b, P * c : P * (c + 1)],
+                rhs=z_c[b, z0][:, z_cols].bitcast(FP8X4),
+                rhs_scale=z_s[b, z0][:, z_cols],
+                start=(b == 0),
+                stop=(b == 1),
+            )
+
+        gather_words(0, 0, S)
+        for u in range(2):
+            cast_w1(0, 0, u)
+        nc.vector.tensor_copy(v_s[:], tab_s[:].indirect(offs_sb[:]))
+        for u in range(2):
+            quantize_w1(0, 0, u)
+        for t in range(PACK):
+            for half in range(2):
+                h_pass(0, 0, t, half)
+        gather_words(1, 0, BANK)
+        gather_words(1, BANK, BANK)
+        for u in range(2):
+            cast_w1(1, 0, u)
+            quantize_w1(1, 0, u)
+            for t in (2 * u, 2 * u + 1):
+                for half in range(2):
+                    h_pass(1, 0, t, half)
+        h_out(0, 0, 0)
+        h_out(0, 0, 1, on_vector=True)
+        for half in range(2):
+            h_out(0, 1, half)
+
+        gather_h(0, 0, 0, PAIRS)
+        cast_w1(0, 1, 0)
+        for half in range(2):
+            h_out(0, 2, half)
+        gather_h(0, 1, 0, PAIRS)
+        cast_w1(1, 1, 0)
+        for half in range(2):
+            h_out(0, 3, half)
+        quantize_w1(0, 1, 0)
+        quantize_w1(1, 1, 0)
+        gather_h(0, 2, 0, PAIRS)
+        cast_w1(0, 1, 1)
+        cast_w1(1, 1, 1)
+        for t in range(2):
+            for half in range(2):
+                for a in range(2):
+                    h_pass(a, 1, t, half)
+                h_out(1, t, half)
+        quantize_w1(0, 1, 1)
+        quantize_w1(1, 1, 1)
+        gather_h(0, 3, 0, PAIRS)
+        for t in range(2, PACK):
+            for half in range(2):
+                for a in range(2):
+                    h_pass(a, 1, t, half)
+                h_out(1, t, half)
+        pair_max(0, 0, PAIRS)
+
+        o_ps = [bank(c, "o_ps_%d" % c) for c in range(N_TILES)]
+        out_v = out.rearrange("(c p) q -> p c q", p=P)
+
+        def finish(q0, qn, last):
+            quantize_z(1, q0, qn)
+            staged = sb([P, N_TILES, qn], F32, "staged_%d" % q0)
+            for c in range(N_TILES):
+                for q in range(q0, q0 + qn, GROUP):
+                    if q > q0:
+                        out_pass(0, c, q, 0)
+                    out_pass(1, c, q, q0)
+                if last and c % 2 == 1:
+                    nc.vector.tensor_scalar_add(staged[:, c, :], o_ps[c][:, q0 : q0 + qn], b2_sb[:, c : c + 1])
+                else:
+                    nc.scalar.activation(
+                        staged[:, c, :], o_ps[c][:, q0 : q0 + qn], ACT.Identity, bias=b2_sb[:, c : c + 1]
+                    )
+            nc.sync.dma_start(out=out_v[:, :, q0 : q0 + qn], in_=staged[:])
+
+        pending = None
+        for q0, qn in LAST_PASS_PARTS:
+            gather_h(1, 0, q0, qn)
+            if pending is None:
+                quantize_z(0, 0, PAIRS)
+            else:
+                finish(pending[0], pending[1], False)
+            for c in range(N_TILES):
+                out_pass(0, c, q0, 0)
+            for t in range(1, PACK):
+                gather_h(1, t, q0, qn)
+            pair_max(1, q0, qn)
+            pending = (q0, qn)
+        finish(pending[0], pending[1], True)

@@ -35,8 +35,8 @@ def tile_list_point_pair_max_kernel(
         keep = ctx.enter_context(tc.tile_pool(name="keep", bufs=1))
         psum = ctx.enter_context(tc.psum_pool(name="psum", bufs=1))
 
-        def sb(shape, dtype, name):
-            return keep.tile(shape, dtype, name=name, align_bytes=64)
+        def sb(shape, dtype, name, tag=""):
+            return keep.tile(shape, dtype, name=name, tag=tag or name, align_bytes=64)
 
         def bank(i, name):
             return psum.tile([P, BANK], F32, name=name, tag="bank%d" % i)
@@ -61,29 +61,30 @@ def tile_list_point_pair_max_kernel(
                     in_=tab_scales[a, 4 * q : 4 * q + 4, :].bitcast(I32),
                 )
 
-        def load_table(a):
-            nc.sync.dma_start(out=tab_w[a][:], in_=tab_words[a].rearrange("p t i -> p (t i)").bitcast(I32))
+        def load_table(a, cols=slice(0, T)):
+            nc.sync.dma_start(
+                out=tab_w[a][:, cols], in_=tab_words[a].rearrange("p t i -> p (t i)").bitcast(I32)[:, cols]
+            )
 
         raw = {}
 
         def load_w1(a, b, m0, mn):
-            t_raw = sb([P, PACK, PACK * mn], F32, "w1_raw_%d_%d_%d" % (a, b, m0))
-            cols = slice(b * K_PASS + PACK * m0, b * K_PASS + PACK * (m0 + mn))
-            nc.sync.dma_start(
-                out=t_raw[:],
-                in_=w1[a * K_PASS : (a + 1) * K_PASS, cols].rearrange("(p j) c -> p j c", j=PACK),
-            )
-            raw.setdefault((a, b), []).append((t_raw, m0, mn))
+            raw[a, b, m0] = sb([P, PACK, PACK * mn], F32, "w1_raw_%d_%d_%d" % (a, b, m0))
+            c0 = b * K_PASS + PACK * m0
+            block = w1[a * K_PASS : (a + 1) * K_PASS, c0 : c0 + PACK * mn]
+            nc.sync.dma_start(out=raw[a, b, m0][:], in_=block.rearrange("(p j) c -> p j c", j=PACK))
 
+        load_table(0, slice(0, T // 2))
         nc.sync.dma_start(offs_sb[:], offs)
-        load_table(0)
         nc.sync.dma_start(pos_sb[0][:], pos1)
         nc.sync.dma_start(pos_sb[1][:], pos2)
-        load_table_scales(0)
-        load_w1(0, 0, 0, P)
-        load_table_scales(1)
-        load_table(1)
         nc.sync.dma_start(out=b1_sb[:], in_=b1.rearrange("(b p t) -> p b t", b=2, t=PACK))
+        load_table(0, slice(T // 2, T))
+        load_table_scales(0)
+        load_w1(0, 0, 0, P // 2)
+        load_table_scales(1)
+        load_w1(0, 0, P // 2, P // 2)
+        load_table(1)
         load_w1(1, 0, 0, P // 2)
         load_w1(1, 0, P // 2, P // 2)
         load_w1(0, 1, 0, P)
@@ -97,10 +98,12 @@ def tile_list_point_pair_max_kernel(
         with nc.allow_non_contiguous_dma(reason="one bias value to a partition"):
             nc.sync.dma_start(out=b2_sb[:], in_=b2.rearrange("(c p) -> p c", p=P))
 
-        v_w = [sb([P, S], U32, "v_w%d" % a) for a in range(2)]
+        v_w = {}
         v_s = sb([P, S], U8, "v_s")
 
-        def gather_words(a, j0, jn):
+        def gather_words(a, j0, jn, tag=""):
+            if j0 == 0:
+                v_w[a] = sb([P, S], U32, "v_w%d" % a, tag)
             nc.vector.tensor_copy(
                 v_w[a][:, j0 : j0 + jn],
                 tab_w[a][:].bitcast(U32).indirect(offs_sb[:, j0 // LIST_ROWS : (j0 + jn) // LIST_ROWS]),
@@ -108,14 +111,13 @@ def tile_list_point_pair_max_kernel(
 
         grouped, w1_c, w1_s = {}, {}, {}
 
-        def cast_w1(a, b, u):
-            g = sb([P, 2, P, PACK], BF16, "w1_g_%d_%d_%d" % (a, b, u))
-            grouped[a, b, u] = g
-            for t_raw, m0, mn in raw[a, b]:
-                nc.scalar.copy(
-                    out=g[:, :, m0 : m0 + mn, :].rearrange("p t m j -> p m j t"),
-                    in_=t_raw[:].rearrange("p j (m t) -> p m j t", t=PACK)[:, :, :, 2 * u : 2 * u + 2],
-                )
+        def cast_w1(a, b, u, m0=0, mn=P, tag=""):
+            if m0 == 0:
+                grouped[a, b, u] = sb([P, 2, P, PACK], BF16, "w1_g_%d_%d_%d" % (a, b, u), tag)
+            nc.scalar.copy(
+                out=grouped[a, b, u][:, :, m0 : m0 + mn, :].rearrange("p t m j -> p m j t"),
+                in_=raw[a, b, m0][:].rearrange("p j (m t) -> p m j t", t=PACK)[:, :, :, 2 * u : 2 * u + 2],
+            )
 
         def quantize_w1(a, b, u):
             w1_c[a, b, u] = sb([P, 2 * P], U32, "w1_c_%d_%d_%d" % (a, b, u))
@@ -154,11 +156,17 @@ def tile_list_point_pair_max_kernel(
                 nc.scalar.activation(dst, h_ps[b, t, half][:], ACT.Relu, bias=bias)
 
         picked, z_g, z_c, z_s = {}, {}, {}, {}
+        reuse = {
+            (1, 256, 0): "w1_c_1_1_1",
+            (1, 256, 1): "picked_1_0_0",
+            (1, 384, 0): "picked_1_0_1",
+            (1, 384, 1): "w1_c_1_1_1",
+        }
 
-        def gather_h(b, t, q0, qn):
-            for i in range(2):
+        def gather_h(b, t, q0, qn, sides=(0, 1)):
+            for i in sides:
                 if t == 0:
-                    picked[b, q0, i] = sb([P, PACK, qn], F32, "picked_%d_%d_%d" % (b, q0, i))
+                    picked[b, q0, i] = sb([P, PACK, qn], F32, "picked_%d_%d_%d" % (b, q0, i), reuse.get((b, q0, i), ""))
                 nc.vector.tensor_copy(
                     picked[b, q0, i][:, t, :],
                     h[b, t][:].indirect(pos_sb[i][:, q0 // LIST_ROWS : (q0 + qn) // LIST_ROWS]),
@@ -195,53 +203,55 @@ def tile_list_point_pair_max_kernel(
             )
 
         gather_words(0, 0, S)
-        for u in range(2):
-            cast_w1(0, 0, u)
+        for m0 in (0, P // 2):
+            for u in range(2):
+                cast_w1(0, 0, u, m0, P // 2)
         nc.vector.tensor_copy(v_s[:], tab_s[:].indirect(offs_sb[:]))
         for u in range(2):
             quantize_w1(0, 0, u)
-        for t in range(PACK):
-            for half in range(2):
-                h_pass(0, 0, t, half)
-        gather_words(1, 0, BANK)
-        gather_words(1, BANK, BANK)
-        for u in range(2):
-            cast_w1(1, 0, u)
-            quantize_w1(1, 0, u)
-            for t in (2 * u, 2 * u + 1):
-                for half in range(2):
-                    h_pass(1, 0, t, half)
-        h_out(0, 0, 0)
-        h_out(0, 0, 1, on_vector=True)
-        for half in range(2):
-            h_out(0, 1, half)
-
-        gather_h(0, 0, 0, PAIRS)
-        cast_w1(0, 1, 0)
-        for half in range(2):
-            h_out(0, 2, half)
-        gather_h(0, 1, 0, PAIRS)
-        cast_w1(1, 1, 0)
-        for half in range(2):
-            h_out(0, 3, half)
-        quantize_w1(0, 1, 0)
-        quantize_w1(1, 1, 0)
-        gather_h(0, 2, 0, PAIRS)
-        cast_w1(0, 1, 1)
-        cast_w1(1, 1, 1)
         for t in range(2):
             for half in range(2):
-                for a in range(2):
-                    h_pass(a, 1, t, half)
-                h_out(1, t, half)
-        quantize_w1(0, 1, 1)
-        quantize_w1(1, 1, 1)
-        gather_h(0, 3, 0, PAIRS)
-        for t in range(2, PACK):
+                h_pass(0, 0, t, half)
+        gather_words(1, 0, BANK, "w1_g_0_0_1")
+        gather_words(1, BANK, BANK)
+        for m0 in (0, P // 2):
+            for u in range(2):
+                cast_w1(1, 0, u, m0, P // 2)
+        quantize_w1(1, 0, 0)
+        for half in range(2):
+            h_pass(1, 0, 0, half)
+        h_out(0, 0, 0)
+        h_out(0, 0, 1, on_vector=True)
+
+        def h_tile(b, t):
             for half in range(2):
                 for a in range(2):
-                    h_pass(a, 1, t, half)
-                h_out(1, t, half)
+                    h_pass(a, b, t, half)
+                h_out(b, t, half)
+
+        for half in range(2):
+            h_pass(1, 0, 1, half)
+            h_out(0, 1, half)
+        quantize_w1(1, 0, 1)
+        gather_h(0, 0, 0, PAIRS)
+        h_tile(0, 2)
+        h_tile(0, 3)
+        cast_w1(0, 1, 0, tag="w1_c_1_0_0")
+        cast_w1(1, 1, 0, tag="w1_c_1_0_1")
+        cast_w1(0, 1, 1, tag="w1_s_1_0_0")
+        cast_w1(1, 1, 1, tag="w1_s_1_0_1")
+        gather_h(0, 1, 0, PAIRS)
+        gather_h(0, 2, 0, PAIRS)
+        gather_h(0, 3, 0, PAIRS, (0,))
+        quantize_w1(0, 1, 0)
+        quantize_w1(1, 1, 0)
+        h_tile(1, 0)
+        h_tile(1, 1)
+        gather_h(0, 3, 0, PAIRS, (1,))
+        quantize_w1(0, 1, 1)
+        quantize_w1(1, 1, 1)
+        h_tile(1, 2)
+        h_tile(1, 3)
         pair_max(0, 0, PAIRS)
 
         o_ps = [bank(c, "o_ps_%d" % c) for c in range(N_TILES)]
@@ -261,7 +271,9 @@ def tile_list_point_pair_max_kernel(
                     nc.scalar.activation(
                         staged[:, c, :], o_ps[c][:, q0 : q0 + qn], ACT.Identity, bias=b2_sb[:, c : c + 1]
                     )
-            nc.sync.dma_start(out=out_v[:, :, q0 : q0 + qn], in_=staged[:])
+                if c == N_TILES - 1 or (last and c == N_TILES // 2 - 1):
+                    c0 = N_TILES // 2 if last and c == N_TILES - 1 else 0
+                    nc.sync.dma_start(out=out_v[:, c0 : c + 1, q0 : q0 + qn], in_=staged[:, c0 : c + 1, :])
 
         pending = None
         for q0, qn in LAST_PASS_PARTS:

@@ -54,17 +54,14 @@ def tile_list_point_pair_max_kernel(
         nc.vector.memset(tab_s[:].bitcast(I32), 0)
         nc.vector.memset(w2_s[:].rearrange("p b n -> p (b n)").bitcast(I32), 0)
 
-        def load_table_scales(a):
-            for q in range(4):
-                nc.sync.dma_start(
-                    out=tab_s[32 * q + 4 * a : 32 * q + 4 * a + 4, :].bitcast(I32),
-                    in_=tab_scales[a, 4 * q : 4 * q + 4, :].bitcast(I32),
-                )
-
-        def load_table(a, cols=slice(0, T)):
-            nc.sync.dma_start(
-                out=tab_w[a][:, cols], in_=tab_words[a].rearrange("p t i -> p (t i)").bitcast(I32)[:, cols]
+        for q in (0, 2, 1, 3):
+            nc.gpsimd.dma_start(
+                out=tab_s[32 * q : 32 * q + 8, :].bitcast(I32),
+                in_=tab_scales[:, 4 * q : 4 * q + 4, :].bitcast(I32),
             )
+
+        def load_table(a):
+            nc.sync.dma_start(out=tab_w[a][:], in_=tab_words[a].rearrange("p t i -> p (t i)").bitcast(I32))
 
         raw = {}
 
@@ -74,19 +71,15 @@ def tile_list_point_pair_max_kernel(
             block = w1[a * K_PASS : (a + 1) * K_PASS, c0 : c0 + PACK * mn]
             nc.sync.dma_start(out=raw[a, b, m0][:], in_=block.rearrange("(p j) c -> p j c", j=PACK))
 
-        load_table(0, slice(0, T // 2))
+        load_table(0)
         nc.sync.dma_start(offs_sb[:], offs)
-        nc.sync.dma_start(pos_sb[0][:], pos1)
-        nc.sync.dma_start(pos_sb[1][:], pos2)
-        nc.sync.dma_start(out=b1_sb[:], in_=b1.rearrange("(b p t) -> p b t", b=2, t=PACK))
-        load_table(0, slice(T // 2, T))
-        load_table_scales(0)
-        load_w1(0, 0, 0, P // 2)
-        load_table_scales(1)
-        load_w1(0, 0, P // 2, P // 2)
+        load_w1(0, 0, 0, P)
         load_table(1)
         load_w1(1, 0, 0, P // 2)
         load_w1(1, 0, P // 2, P // 2)
+        nc.sync.dma_start(out=b1_sb[:], in_=b1.rearrange("(b p t) -> p b t", b=2, t=PACK))
+        nc.sync.dma_start(pos_sb[0][:], pos1)
+        nc.sync.dma_start(pos_sb[1][:], pos2)
         load_w1(0, 1, 0, P)
         load_w1(1, 1, 0, P)
         nc.sync.dma_start(out=w2_w[:].bitcast(I32), in_=w2_words.rearrange("b p n -> p b n").bitcast(I32))
@@ -119,8 +112,8 @@ def tile_list_point_pair_max_kernel(
                 in_=raw[a, b, m0][:].rearrange("p j (m t) -> p m j t", t=PACK)[:, :, :, 2 * u : 2 * u + 2],
             )
 
-        def quantize_w1(a, b, u):
-            w1_c[a, b, u] = sb([P, 2 * P], U32, "w1_c_%d_%d_%d" % (a, b, u))
+        def quantize_w1(a, b, u, tag=""):
+            w1_c[a, b, u] = sb([P, 2 * P], U32, "w1_c_%d_%d_%d" % (a, b, u), tag)
             w1_s[a, b, u] = sb([P, 2 * P], U8, "w1_s_%d_%d_%d" % (a, b, u))
             nc.vector.quantize_mx(
                 out=w1_c[a, b, u][:].bitcast(FP8X4),
@@ -203,21 +196,20 @@ def tile_list_point_pair_max_kernel(
             )
 
         gather_words(0, 0, S)
-        for m0 in (0, P // 2):
-            for u in range(2):
-                cast_w1(0, 0, u, m0, P // 2)
+        for u in range(2):
+            cast_w1(0, 0, u)
         nc.vector.tensor_copy(v_s[:], tab_s[:].indirect(offs_sb[:]))
         for u in range(2):
             quantize_w1(0, 0, u)
         for t in range(2):
             for half in range(2):
                 h_pass(0, 0, t, half)
-        gather_words(1, 0, BANK, "w1_g_0_0_1")
+        gather_words(1, 0, BANK, "tab_s")
         gather_words(1, BANK, BANK)
         for m0 in (0, P // 2):
             for u in range(2):
                 cast_w1(1, 0, u, m0, P // 2)
-        quantize_w1(1, 0, 0)
+        quantize_w1(1, 0, 0, "tab_w1")
         for half in range(2):
             h_pass(1, 0, 0, half)
         h_out(0, 0, 0)
@@ -232,12 +224,12 @@ def tile_list_point_pair_max_kernel(
         for half in range(2):
             h_pass(1, 0, 1, half)
             h_out(0, 1, half)
-        quantize_w1(1, 0, 1)
+        quantize_w1(1, 0, 1, "w1_g_1_0_0")
         gather_h(0, 0, 0, PAIRS)
         h_tile(0, 2)
         h_tile(0, 3)
-        cast_w1(0, 1, 0, tag="w1_c_1_0_0")
-        cast_w1(1, 1, 0, tag="w1_c_1_0_1")
+        cast_w1(0, 1, 0, tag="tab_w1")
+        cast_w1(1, 1, 0, tag="w1_g_1_0_0")
         cast_w1(0, 1, 1, tag="w1_s_1_0_0")
         cast_w1(1, 1, 1, tag="w1_s_1_0_1")
         gather_h(0, 1, 0, PAIRS)

@@ -168,9 +168,9 @@ def tile_list_point_pair_max_kernel(
         def pair_max(b, q0, qn):
             z_g[b, q0] = sb([P, qn, PACK], BF16, "z_g_%d_%d" % (b, q0))
             nc.vector.tensor_tensor(
-                z_g[b, q0][:].rearrange("p (c i) t -> p c t i", i=2),
-                picked[b, q0, 0][:].rearrange("p t (c i) -> p c t i", i=2),
-                picked[b, q0, 1][:].rearrange("p t (c i) -> p c t i", i=2),
+                z_g[b, q0][:].rearrange("p (c i) t -> p c t i", i=4),
+                picked[b, q0, 0][:].rearrange("p t (c i) -> p c t i", i=4),
+                picked[b, q0, 1][:].rearrange("p t (c i) -> p c t i", i=4),
                 ALU.max,
             )
 

@@ -23,7 +23,7 @@ BANK = 512
 LIST_ROWS = 16
 N_TILES = N // P
 GROUP = 128
-LAST_PASS_PARTS = [(0, 256), (256, 128), (384, 128)]
+QUAD = 32
 
 
 def tile_list_point_pair_max_kernel(
@@ -54,11 +54,12 @@ def tile_list_point_pair_max_kernel(
         nc.vector.memset(tab_s[:].bitcast(I32), 0)
         nc.vector.memset(w2_s[:].rearrange("p b n -> p (b n)").bitcast(I32), 0)
 
-        for q in (0, 2, 1, 3):
-            nc.gpsimd.dma_start(
-                out=tab_s[32 * q : 32 * q + 8, :].bitcast(I32),
-                in_=tab_scales[:, 4 * q : 4 * q + 4, :].bitcast(I32),
-            )
+        def load_scales():
+            for q in (0, 2, 1, 3):
+                nc.gpsimd.dma_start(
+                    out=tab_s[QUAD * q : QUAD * q + 8, :].bitcast(I32),
+                    in_=tab_scales[:, 4 * q : 4 * q + 4, :].bitcast(I32),
+                )
 
         def load_table(a):
             nc.sync.dma_start(out=tab_w[a][:], in_=tab_words[a].rearrange("p t i -> p (t i)").bitcast(I32))
@@ -67,10 +68,12 @@ def tile_list_point_pair_max_kernel(
 
         def load_w1(a, b, m0, mn):
             raw[a, b, m0] = sb([P, PACK, PACK * mn], F32, "w1_raw_%d_%d_%d" % (a, b, m0))
+            piece = raw[a, b, m0]
             c0 = b * K_PASS + PACK * m0
             block = w1[a * K_PASS : (a + 1) * K_PASS, c0 : c0 + PACK * mn]
-            nc.sync.dma_start(out=raw[a, b, m0][:], in_=block.rearrange("(p j) c -> p j c", j=PACK))
+            nc.sync.dma_start(out=piece[:], in_=block.rearrange("(p j) c -> p j c", j=PACK))
 
+        load_scales()
         load_table(0)
         nc.sync.dma_start(offs_sb[:], offs)
         load_w1(0, 0, 0, P)
@@ -85,7 +88,7 @@ def tile_list_point_pair_max_kernel(
         nc.sync.dma_start(out=w2_w[:].bitcast(I32), in_=w2_words.rearrange("b p n -> p b n").bitcast(I32))
         for q in range(4):
             nc.sync.dma_start(
-                out=w2_s[32 * q : 32 * q + 4, :, :].bitcast(I32),
+                out=w2_s[QUAD * q : QUAD * q + 4, :, :].bitcast(I32),
                 in_=w2_scales[:, 4 * q : 4 * q + 4, :].rearrange("b r n -> r b n").bitcast(I32),
             )
         with nc.allow_non_contiguous_dma(reason="one bias value to a partition"):
@@ -102,23 +105,31 @@ def tile_list_point_pair_max_kernel(
                 tab_w[a][:].bitcast(U32).indirect(offs_sb[:, j0 // LIST_ROWS : (j0 + jn) // LIST_ROWS]),
             )
 
-        grouped, w1_c, w1_s = {}, {}, {}
+        grouped, codes, planes, where = {}, {}, {}, {}
 
-        def cast_w1(a, b, u, m0=0, mn=P, tag=""):
-            if m0 == 0:
-                grouped[a, b, u] = sb([P, 2, P, PACK], BF16, "w1_g_%d_%d_%d" % (a, b, u), tag)
+        def open_batch(name, operands, tag=""):
+            grouped[name] = sb([P, len(operands), P, PACK], BF16, "w1_g_" + name, tag)
+            for i, operand in enumerate(operands):
+                where[operand] = (name, i)
+
+        def cast_w1(a, b, u, m0=0, mn=P):
+            name, i = where[a, b, 2 * u]
             nc.scalar.copy(
-                out=grouped[a, b, u][:, :, m0 : m0 + mn, :].rearrange("p t m j -> p m j t"),
+                out=grouped[name][:, i : i + 2, m0 : m0 + mn, :].rearrange("p t m j -> p m j t"),
                 in_=raw[a, b, m0][:].rearrange("p j (m t) -> p m j t", t=PACK)[:, :, :, 2 * u : 2 * u + 2],
             )
 
-        def quantize_w1(a, b, u, tag=""):
-            w1_c[a, b, u] = sb([P, 2 * P], U32, "w1_c_%d_%d_%d" % (a, b, u), tag)
-            w1_s[a, b, u] = sb([P, 2 * P], U8, "w1_s_%d_%d_%d" % (a, b, u))
+        def quantize_w1(name, i0=0, n=0, tag=""):
+            count = grouped[name].shape[1]
+            n = n or count
+            if i0 == 0:
+                codes[name] = sb([P, count * P], U32, "w1_c_" + name, tag)
+                planes[name] = sb([P, count * P], U8, "w1_s_" + name)
+            cols = slice(i0 * P, (i0 + n) * P)
             nc.vector.quantize_mx(
-                out=w1_c[a, b, u][:].bitcast(FP8X4),
-                scales=w1_s[a, b, u][:],
-                in_=grouped[a, b, u][:].rearrange("p t m j -> p (t m j)"),
+                out=codes[name][:, cols].bitcast(FP8X4),
+                scales=planes[name][:, cols],
+                in_=grouped[name][:, i0 : i0 + n, :, :].rearrange("p t m j -> p (t m j)"),
             )
 
         h_ps = {}
@@ -126,12 +137,13 @@ def tile_list_point_pair_max_kernel(
         def h_pass(a, b, t, half):
             if a == 0:
                 h_ps[b, t, half] = bank(2 * t + half, "h_ps_%d_%d_%d" % (b, t, half))
-            m_cols = slice((t % 2) * P, (t % 2 + 1) * P)
+            name, i = where[a, b, t]
+            m_cols = slice(i * P, (i + 1) * P)
             j_cols = slice(half * BANK, (half + 1) * BANK)
             nc.tensor.matmul_mx(
                 out=h_ps[b, t, half][:],
-                lhsT=w1_c[a, b, t // 2][:, m_cols].bitcast(FP8X4),
-                lhsT_scale=w1_s[a, b, t // 2][:, m_cols],
+                lhsT=codes[name][:, m_cols].bitcast(FP8X4),
+                lhsT_scale=planes[name][:, m_cols],
                 rhs=v_w[a][:, j_cols].bitcast(FP8X4),
                 rhs_scale=v_s[4 * a :, j_cols],
                 start=(a == 0),
@@ -148,34 +160,39 @@ def tile_list_point_pair_max_kernel(
             else:
                 nc.scalar.activation(dst, h_ps[b, t, half][:], ACT.Relu, bias=bias)
 
+        def h_tile(b, t):
+            for half in range(2):
+                for a in range(2):
+                    h_pass(a, b, t, half)
+                h_out(b, t, half)
+
+        def pick(dst, b, t, side, q0, qn):
+            nc.vector.tensor_copy(
+                dst, h[b, t][:].indirect(pos_sb[side][:, q0 // LIST_ROWS : (q0 + qn) // LIST_ROWS])
+            )
+
         picked, z_g, z_c, z_s = {}, {}, {}, {}
-        reuse = {
-            (1, 256, 0): "w1_c_1_1_1",
-            (1, 256, 1): "picked_1_0_0",
-            (1, 384, 0): "picked_1_0_1",
-            (1, 384, 1): "w1_c_1_1_1",
-        }
 
-        def gather_h(b, t, q0, qn, sides=(0, 1)):
-            for i in sides:
-                if t == 0:
-                    picked[b, q0, i] = sb([P, PACK, qn], F32, "picked_%d_%d_%d" % (b, q0, i), reuse.get((b, q0, i), ""))
-                nc.vector.tensor_copy(
-                    picked[b, q0, i][:, t, :],
-                    h[b, t][:].indirect(pos_sb[i][:, q0 // LIST_ROWS : (q0 + qn) // LIST_ROWS]),
-                )
+        def open_picked(b, q0, qn, tags=("", "")):
+            for side in range(2):
+                tile = sb([P, PACK, qn], F32, "picked_%d_%d_%d" % (b, q0, side), tags[side])
+                for q in range(q0, q0 + qn, GROUP):
+                    picked[b, q, side] = tile[:, :, q - q0 :]
 
-        def pair_max(b, q0, qn):
-            z_g[b, q0] = sb([P, qn, PACK], BF16, "z_g_%d_%d" % (b, q0))
+        def pick_pairs(b, t, side, q0, qn):
+            pick(picked[b, q0, side][:, t, 0:qn], b, t, side, q0, qn)
+
+        def pair_max(b, q0, qn, tag=""):
+            z_g[b, q0] = sb([P, qn, PACK], BF16, "z_g_%d_%d" % (b, q0), tag)
             nc.vector.tensor_tensor(
                 z_g[b, q0][:].rearrange("p (c i) t -> p c t i", i=4),
-                picked[b, q0, 0][:].rearrange("p t (c i) -> p c t i", i=4),
-                picked[b, q0, 1][:].rearrange("p t (c i) -> p c t i", i=4),
+                picked[b, q0, 0][:, :, 0:qn].rearrange("p t (c i) -> p c t i", i=4),
+                picked[b, q0, 1][:, :, 0:qn].rearrange("p t (c i) -> p c t i", i=4),
                 ALU.max,
             )
 
-        def quantize_z(b, q0, qn):
-            z_c[b, q0] = sb([P, qn], U32, "z_c_%d_%d" % (b, q0))
+        def quantize_z(b, q0, qn, tag=""):
+            z_c[b, q0] = sb([P, qn], U32, "z_c_%d_%d" % (b, q0), tag)
             z_s[b, q0] = sb([P, qn], U8, "z_s_%d_%d" % (b, q0))
             nc.vector.quantize_mx(
                 out=z_c[b, q0][:].bitcast(FP8X4),
@@ -196,11 +213,14 @@ def tile_list_point_pair_max_kernel(
             )
 
         gather_words(0, 0, S)
+        for a in range(2):
+            for u in range(2):
+                open_batch("%d_0_%d" % (a, u), [(a, 0, 2 * u), (a, 0, 2 * u + 1)])
         for u in range(2):
             cast_w1(0, 0, u)
         nc.vector.tensor_copy(v_s[:], tab_s[:].indirect(offs_sb[:]))
         for u in range(2):
-            quantize_w1(0, 0, u)
+            quantize_w1("0_0_%d" % u)
         for t in range(2):
             for half in range(2):
                 h_pass(0, 0, t, half)
@@ -209,48 +229,44 @@ def tile_list_point_pair_max_kernel(
         for m0 in (0, P // 2):
             for u in range(2):
                 cast_w1(1, 0, u, m0, P // 2)
-        quantize_w1(1, 0, 0, "tab_w1")
+        quantize_w1("1_0_0", tag="tab_w1")
         for half in range(2):
             h_pass(1, 0, 0, half)
         h_out(0, 0, 0)
         h_out(0, 0, 1, on_vector=True)
-
-        def h_tile(b, t):
-            for half in range(2):
-                for a in range(2):
-                    h_pass(a, b, t, half)
-                h_out(b, t, half)
-
         for half in range(2):
             h_pass(1, 0, 1, half)
             h_out(0, 1, half)
-        quantize_w1(1, 0, 1, "w1_g_1_0_0")
-        gather_h(0, 0, 0, PAIRS)
+        quantize_w1("1_0_1", tag="w1_g_1_0_0")
+        open_picked(0, 0, PAIRS)
+        for side in range(2):
+            pick_pairs(0, 0, side, 0, PAIRS)
         h_tile(0, 2)
         h_tile(0, 3)
-        cast_w1(0, 1, 0, tag="tab_w1")
-        cast_w1(1, 1, 0, tag="w1_g_1_0_0")
-        cast_w1(0, 1, 1, tag="w1_s_1_0_0")
-        cast_w1(1, 1, 1, tag="w1_s_1_0_1")
-        gather_h(0, 1, 0, PAIRS)
-        gather_h(0, 2, 0, PAIRS)
-        gather_h(0, 3, 0, PAIRS, (0,))
-        quantize_w1(0, 1, 0)
-        quantize_w1(1, 1, 0)
+        open_batch("u0", [(a, 1, t) for a in range(2) for t in (0, 1)], "w1_g_1_0_0")
+        open_batch("u1", [(a, 1, t) for a in range(2) for t in (2, 3)], "w1_s_1_0_1")
+        for u in range(2):
+            for a in range(2):
+                cast_w1(a, 1, u)
+        for t in range(1, PACK):
+            for side in range(2):
+                pick_pairs(0, t, side, 0, PAIRS)
+        quantize_w1("u0")
         h_tile(1, 0)
         h_tile(1, 1)
-        gather_h(0, 3, 0, PAIRS, (1,))
-        quantize_w1(0, 1, 1)
-        quantize_w1(1, 1, 1)
+        quantize_w1("u1")
         h_tile(1, 2)
         h_tile(1, 3)
-        pair_max(0, 0, PAIRS)
+        pair_max(0, 0, PAIRS, "w1_s_1_0_1")
 
         o_ps = [bank(c, "o_ps_%d" % c) for c in range(N_TILES)]
         out_v = out.rearrange("(c p) q -> p c q", p=P)
 
+        def open_part(q0):
+            for c in range(N_TILES):
+                out_pass(0, c, q0, 0)
+
         def finish(q0, qn, last):
-            quantize_z(1, q0, qn)
             staged = sb([P, N_TILES, qn], F32, "staged_%d" % q0)
             for c in range(N_TILES):
                 for q in range(q0, q0 + qn, GROUP):
@@ -267,17 +283,31 @@ def tile_list_point_pair_max_kernel(
                     c0 = N_TILES // 2 if last and c == N_TILES - 1 else 0
                     nc.sync.dma_start(out=out_v[:, c0 : c + 1, q0 : q0 + qn], in_=staged[:, c0 : c + 1, :])
 
-        pending = None
-        for q0, qn in LAST_PASS_PARTS:
-            gather_h(1, 0, q0, qn)
-            if pending is None:
-                quantize_z(0, 0, PAIRS)
-            else:
-                finish(pending[0], pending[1], False)
-            for c in range(N_TILES):
-                out_pass(0, c, q0, 0)
-            for t in range(1, PACK):
-                gather_h(1, t, q0, qn)
-            pair_max(1, q0, qn)
-            pending = (q0, qn)
-        finish(pending[0], pending[1], True)
+        open_picked(1, 0, 256)
+        for side in range(2):
+            pick_pairs(1, 0, side, 0, 256)
+        quantize_z(0, 0, PAIRS)
+        open_part(0)
+        for t in range(1, PACK):
+            for side in range(2):
+                pick_pairs(1, t, side, 0, 256)
+        open_picked(1, 256, 256, ("w1_c_u1", "picked_1_0_1"))
+        for t in range(3):
+            pick_pairs(1, t, 0, 256, 256)
+        pair_max(1, 0, 256)
+        pick_pairs(1, 3, 0, 256, GROUP)
+        quantize_z(1, 0, 256)
+        finish(0, 256, False)
+        open_part(256)
+        for t in range(3):
+            pick_pairs(1, t, 1, 256, 256)
+        pick_pairs(1, 3, 1, 256, GROUP)
+        pick_pairs(1, 3, 0, 384, GROUP)
+        pair_max(1, 256, GROUP)
+        pick_pairs(1, 3, 1, 384, GROUP)
+        quantize_z(1, 256, GROUP)
+        finish(256, GROUP, False)
+        open_part(384)
+        pair_max(1, 384, GROUP)
+        quantize_z(1, 384, GROUP)
+        finish(384, GROUP, True)

@@ -173,11 +173,10 @@ def tile_list_point_pair_max_kernel(
 
         picked, z_g, z_c, z_s = {}, {}, {}, {}
 
-        def open_picked(b, q0, qn, tags=("", "")):
-            for side in range(2):
-                tile = sb([P, PACK, qn], F32, "picked_%d_%d_%d" % (b, q0, side), tags[side])
-                for q in range(q0, q0 + qn, GROUP):
-                    picked[b, q, side] = tile[:, :, q - q0 :]
+        def open_picked(b, side, q0, qn, tag=""):
+            tile = sb([P, PACK, qn], F32, "picked_%d_%d_%d" % (b, q0, side), tag)
+            for q in range(q0, q0 + qn, GROUP):
+                picked[b, q, side] = tile[:, :, q - q0 :]
 
         def pick_pairs(b, t, side, q0, qn):
             pick(picked[b, q0, side][:, t, 0:qn], b, t, side, q0, qn)
@@ -200,16 +199,16 @@ def tile_list_point_pair_max_kernel(
                 in_=z_g[b, q0][:].rearrange("p q t -> p (q t)"),
             )
 
-        def out_pass(b, c, q, z0):
+        def out_pass(b, c, q, z0, start, stop):
             z_cols = slice(q - z0, q - z0 + GROUP)
             nc.tensor.matmul_mx(
-                out=o_ps[c][:, q : q + GROUP],
+                out=o_ps[c, q],
                 lhsT=w2_w[:, b, 2 * P * c : 2 * P * (c + 1)].bitcast(FP4X4),
                 lhsT_scale=w2_s[:, b, P * c : P * (c + 1)],
                 rhs=z_c[b, z0][:, z_cols].bitcast(FP8X4),
                 rhs_scale=z_s[b, z0][:, z_cols],
-                start=(b == 0),
-                stop=(b == 1),
+                start=start,
+                stop=stop,
             )
 
         gather_words(0, 0, S)
@@ -229,7 +228,8 @@ def tile_list_point_pair_max_kernel(
         for m0 in (0, P // 2):
             for u in range(2):
                 cast_w1(1, 0, u, m0, P // 2)
-        quantize_w1("1_0_0", tag="tab_w1")
+        quantize_w1("1_0_0", 0, 1, "tab_w1")
+        quantize_w1("1_0_0", 1, 1)
         for half in range(2):
             h_pass(1, 0, 0, half)
         h_out(0, 0, 0)
@@ -238,8 +238,8 @@ def tile_list_point_pair_max_kernel(
             h_pass(1, 0, 1, half)
             h_out(0, 1, half)
         quantize_w1("1_0_1", tag="w1_g_1_0_0")
-        open_picked(0, 0, PAIRS)
         for side in range(2):
+            open_picked(0, side, 0, PAIRS)
             pick_pairs(0, 0, side, 0, PAIRS)
         h_tile(0, 2)
         h_tile(0, 3)
@@ -259,55 +259,74 @@ def tile_list_point_pair_max_kernel(
         h_tile(1, 3)
         pair_max(0, 0, PAIRS, "w1_s_1_0_1")
 
-        o_ps = [bank(c, "o_ps_%d" % c) for c in range(N_TILES)]
+        own = [bank(c, "o_own_%d" % c) for c in range(N_TILES)]
+        shared = [bank(N_TILES + i, "o_shared_%d" % i) for i in range(2)]
+        o_ps = {}
+        for c in range(N_TILES):
+            for q in (0, 128, 384):
+                o_ps[c, q] = own[c][:, q : q + GROUP]
+            o_ps[c, 256] = shared[c // 3][:, (c % 3) * GROUP : (c % 3 + 1) * GROUP]
         out_v = out.rearrange("(c p) q -> p c q", p=P)
 
-        def open_part(q0):
-            for c in range(N_TILES):
-                out_pass(0, c, q0, 0)
+        def add_bias(dst, src, c, on_vector=False):
+            if on_vector:
+                nc.vector.tensor_scalar_add(dst, src, b2_sb[:, c : c + 1])
+            else:
+                nc.scalar.activation(dst, src, ACT.Identity, bias=b2_sb[:, c : c + 1])
 
-        def finish(q0, qn, last):
-            staged = sb([P, N_TILES, qn], F32, "staged_%d" % q0)
-            for c in range(N_TILES):
-                for q in range(q0, q0 + qn, GROUP):
-                    if q > q0:
-                        out_pass(0, c, q, 0)
-                    out_pass(1, c, q, q0)
-                if last and c % 2 == 1:
-                    nc.vector.tensor_scalar_add(staged[:, c, :], o_ps[c][:, q0 : q0 + qn], b2_sb[:, c : c + 1])
-                else:
-                    nc.scalar.activation(
-                        staged[:, c, :], o_ps[c][:, q0 : q0 + qn], ACT.Identity, bias=b2_sb[:, c : c + 1]
-                    )
-                if c == N_TILES - 1 or (last and c == N_TILES // 2 - 1):
-                    c0 = N_TILES // 2 if last and c == N_TILES - 1 else 0
-                    nc.sync.dma_start(out=out_v[:, c0 : c + 1, q0 : q0 + qn], in_=staged[:, c0 : c + 1, :])
+        def store(staged, c0, cn, q0, qn):
+            nc.sync.dma_start(out=out_v[:, c0 : c0 + cn, q0 : q0 + qn], in_=staged[:, c0 : c0 + cn, :])
 
-        open_picked(1, 0, 256)
-        for side in range(2):
-            pick_pairs(1, 0, side, 0, 256)
+        open_picked(1, 0, 0, PAIRS)
+        open_picked(1, 1, 0, 256)
+        pick_pairs(1, 0, 0, 0, PAIRS)
         quantize_z(0, 0, PAIRS)
-        open_part(0)
-        for t in range(1, PACK):
-            for side in range(2):
-                pick_pairs(1, t, side, 0, 256)
-        open_picked(1, 256, 256, ("w1_c_u1", "picked_1_0_1"))
-        for t in range(3):
-            pick_pairs(1, t, 0, 256, 256)
-        pair_max(1, 0, 256)
+        for c in range(N_TILES):
+            out_pass(0, c, 0, 0, True, False)
+            out_pass(0, c, 128, 0, False, False)
+        for c in range(N_TILES):
+            out_pass(0, c, 256, 0, c % 3 == 0, False)
+        pick_pairs(1, 0, 1, 0, 256)
+        for t in (1, 2):
+            pick_pairs(1, t, 0, 0, PAIRS)
+            pick_pairs(1, t, 1, 0, 256)
+        pick_pairs(1, 3, 0, 0, 256)
+        pick_pairs(1, 3, 1, 0, 256)
         pick_pairs(1, 3, 0, 256, GROUP)
-        quantize_z(1, 0, 256)
-        finish(0, 256, False)
-        open_part(256)
-        for t in range(3):
-            pick_pairs(1, t, 1, 256, 256)
-        pick_pairs(1, 3, 1, 256, GROUP)
+        pair_max(1, 0, 256)
         pick_pairs(1, 3, 0, 384, GROUP)
+        quantize_z(1, 0, 256)
+        staged = sb([P, N_TILES, 256], F32, "staged_first")
+        for c in range(N_TILES):
+            out_pass(1, c, 0, 0, False, False)
+            out_pass(1, c, 128, 0, False, True)
+            add_bias(staged[:, c, :], own[c][:, 0:256], c)
+            if c % 2 == 1:
+                store(staged, c - 1, 2, 0, 256)
+        for c in range(N_TILES):
+            out_pass(0, c, 384, 0, True, False)
+        open_picked(1, 1, 256, GROUP, "picked_1_0_1")
+        open_picked(1, 1, 384, GROUP, "z_g_1_0")
+        for t in range(PACK):
+            pick_pairs(1, t, 1, 256, GROUP)
+        pick_pairs(1, 0, 1, 384, GROUP)
         pair_max(1, 256, GROUP)
-        pick_pairs(1, 3, 1, 384, GROUP)
+        pick_pairs(1, 1, 1, 384, GROUP)
         quantize_z(1, 256, GROUP)
-        finish(256, GROUP, False)
-        open_part(384)
+        staged = sb([P, N_TILES, GROUP], F32, "staged_middle")
+        for c in range(N_TILES):
+            out_pass(1, c, 256, 256, False, c % 3 == 2)
+            if c % 3 == 2:
+                for done in range(c - 2, c + 1):
+                    add_bias(staged[:, done, :], o_ps[done, 256], done)
+                store(staged, c - 2, 3, 256, GROUP)
+        for t in (2, 3):
+            pick_pairs(1, t, 1, 384, GROUP)
         pair_max(1, 384, GROUP)
         quantize_z(1, 384, GROUP)
-        finish(384, GROUP, True)
+        staged = sb([P, N_TILES, GROUP], F32, "staged_last")
+        for c in range(N_TILES):
+            out_pass(1, c, 384, 384, False, True)
+            add_bias(staged[:, c, :], o_ps[c, 384], c, on_vector=(c % 2 == 1))
+            if c % 3 == 2:
+                store(staged, c - 2, 3, 384, GROUP)

@@ -33,6 +33,7 @@ def tile_list_point_pair_max_kernel(
     with ExitStack() as ctx:
         lists = ctx.enter_context(tc.tile_pool(name="lists", bufs=1))
         keep = ctx.enter_context(tc.tile_pool(name="keep", bufs=1))
+        late = ctx.enter_context(tc.tile_pool(name="late", bufs=1))
         psum = ctx.enter_context(tc.psum_pool(name="psum", bufs=1))
 
         def sb(shape, dtype, name, tag=""):
@@ -46,45 +47,64 @@ def tile_list_point_pair_max_kernel(
 
         tab_w = [sb([P, T], I32, "tab_w%d" % a) for a in range(2)]
         tab_s = sb([P, T], U8, "tab_s")
-        w2_w = sb([P, 2, 2 * N], U8, "w2_w")
-        w2_s = sb([P, 2, N], U8, "w2_s")
-        b1_sb = sb([P, 2, PACK], F32, "b1_sb")
-        b2_sb = sb([P, N_TILES], F32, "b2_sb")
+        v_s = sb([P, S], U8, "v_s")
 
-        nc.vector.memset(tab_s[:].bitcast(I32), 0)
-        nc.vector.memset(w2_s[:].rearrange("p b n -> p (b n)").bitcast(I32), 0)
+        def placed(shape, dtype, name, offset):
+            return late.tile(shape, dtype, name=name, tag=name, offset=offset, align_bytes=64)
+
+        g_s = placed([P, 4864], U8, "g_s", 8128)
+
+        nc.vector.memset(tab_s[QUAD : 2 * QUAD, :].bitcast(I32), 0)
+        nc.vector.memset(tab_s[2 * QUAD :, :].bitcast(I32), 0)
+        nc.vector.memset(v_s[:].bitcast(I32), 0)
 
         def load_scales():
-            for q in (0, 2, 1, 3):
-                nc.gpsimd.dma_start(
-                    out=tab_s[QUAD * q : QUAD * q + 8, :].bitcast(I32),
-                    in_=tab_scales[:, 4 * q : 4 * q + 4, :].bitcast(I32),
-                )
+            nc.sync.dma_start(
+                out=tab_s[0:QUAD, :].bitcast(I32),
+                in_=tab_scales.rearrange("a q t -> (a q) t").bitcast(I32),
+            )
+
+        def move_scales(queue, a, q):
+            queue.dma_start(
+                out=v_s[QUAD * q + 4 * a : QUAD * q + 4 * a + 4, :].bitcast(I32),
+                in_=g_s[16 * a + 4 * q : 16 * a + 4 * q + 4, 0:S].bitcast(I32),
+            )
 
         def load_table(a):
             nc.sync.dma_start(out=tab_w[a][:], in_=tab_words[a].rearrange("p t i -> p (t i)").bitcast(I32))
 
         raw = {}
 
-        def load_w1(a, b, m0, mn):
-            raw[a, b, m0] = sb([P, PACK, PACK * mn], F32, "w1_raw_%d_%d_%d" % (a, b, m0))
-            piece = raw[a, b, m0]
-            c0 = b * K_PASS + PACK * m0
-            block = w1[a * K_PASS : (a + 1) * K_PASS, c0 : c0 + PACK * mn]
+        def load_w1(a, b, piece):
+            raw[a, b] = piece
+            block = w1[a * K_PASS : (a + 1) * K_PASS, b * K_PASS : (b + 1) * K_PASS]
             nc.sync.dma_start(out=piece[:], in_=block.rearrange("(p j) c -> p j c", j=PACK))
 
         load_scales()
-        load_table(0)
         nc.sync.dma_start(offs_sb[:], offs)
-        load_w1(0, 0, 0, P)
+        load_table(0)
+        load_w1(0, 0, sb([P, PACK, K_PASS], F32, "w1_raw_0_0"))
         load_table(1)
-        load_w1(1, 0, 0, P // 2)
-        load_w1(1, 0, P // 2, P // 2)
-        nc.sync.dma_start(out=b1_sb[:], in_=b1.rearrange("(b p t) -> p b t", b=2, t=PACK))
+        load_w1(1, 0, sb([P, PACK, K_PASS], F32, "w1_raw_1_0"))
         nc.sync.dma_start(pos_sb[0][:], pos1)
         nc.sync.dma_start(pos_sb[1][:], pos2)
-        load_w1(0, 1, 0, P)
-        load_w1(1, 1, 0, P)
+
+        nc.vector.tensor_copy(g_s[:, 0:S], tab_s[:].indirect(offs_sb[:]))
+        for q in (0, 2):
+            move_scales(nc.gpsimd, 1, q)
+        for q in (0, 2, 1, 3):
+            move_scales(nc.scalar, 0, q)
+        for q in (1, 3):
+            move_scales(nc.scalar, 1, q)
+
+        b1_sb = placed([P, 2, PACK], F32, "b1_sb", 12864)
+        w2_w = placed([P, 2, 2 * N], U8, "w2_w", 8192)
+        w2_s = placed([P, 2, N], U8, "w2_s", 11264)
+        b2_sb = placed([P, N_TILES], F32, "b2_sb", 12800)
+        nc.gpsimd.memset(w2_s[:].rearrange("p b n -> p (b n)").bitcast(I32), 0)
+        nc.sync.dma_start(out=b1_sb[:], in_=b1.rearrange("(b p t) -> p b t", b=2, t=PACK))
+        load_w1(0, 1, placed([P, PACK, K_PASS], F32, "w1_raw_0_1", 0))
+        load_w1(1, 1, placed([P, PACK, K_PASS], F32, "w1_raw_1_1", 12928))
         nc.sync.dma_start(out=w2_w[:].bitcast(I32), in_=w2_words.rearrange("b p n -> p b n").bitcast(I32))
         for q in range(4):
             nc.sync.dma_start(
@@ -95,7 +115,6 @@ def tile_list_point_pair_max_kernel(
             nc.sync.dma_start(out=b2_sb[:], in_=b2.rearrange("(c p) -> p c", p=P))
 
         v_w = {}
-        v_s = sb([P, S], U8, "v_s")
 
         def gather_words(a, j0, jn, tag=""):
             if j0 == 0:
@@ -112,12 +131,28 @@ def tile_list_point_pair_max_kernel(
             for i, operand in enumerate(operands):
                 where[operand] = (name, i)
 
-        def cast_w1(a, b, u, m0=0, mn=P):
+        def cast_w1(a, b, u):
             name, i = where[a, b, 2 * u]
             nc.scalar.copy(
-                out=grouped[name][:, i : i + 2, m0 : m0 + mn, :].rearrange("p t m j -> p m j t"),
-                in_=raw[a, b, m0][:].rearrange("p j (m t) -> p m j t", t=PACK)[:, :, :, 2 * u : 2 * u + 2],
+                out=grouped[name][:, i : i + 2, :, :].rearrange("p t m j -> p m j t"),
+                in_=raw[a, b][:].rearrange("p j (m t) -> p m j t", t=PACK)[:, :, :, 2 * u : 2 * u + 2],
             )
+
+        def cast_all(a, b):
+            name, i = where[a, b, 0]
+            nc.scalar.copy(
+                out=grouped[name][:].rearrange("p t m j -> p m j t"),
+                in_=raw[a, b][:].rearrange("p j (m t) -> p m j t", t=PACK),
+            )
+
+        def cast_one(a, b, t, m0, m1, on_vector):
+            name, i = where[a, b, t]
+            dst = grouped[name][:, i, m0:m1, :]
+            src = raw[a, b][:].rearrange("p j (m t) -> p m j t", t=PACK)[:, m0:m1, :, t]
+            if on_vector:
+                nc.vector.tensor_copy(dst, src)
+            else:
+                nc.scalar.copy(out=dst, in_=src)
 
         def quantize_w1(name, i0=0, n=0, tag=""):
             count = grouped[name].shape[1]
@@ -150,7 +185,7 @@ def tile_list_point_pair_max_kernel(
                 stop=(a == 1),
             )
 
-        h = {(b, t): sb([P, S], F32, "h_%d_%d" % (b, t)) for b in range(2) for t in range(PACK)}
+        h = {(b, t): sb([P, S], F32, "h_%d_%d" % (b, t)) for b in range(2) for t in range(PACK) if (b, t) != (0, 3)}
 
         def h_out(b, t, half, on_vector=False):
             dst = h[b, t][:, half * BANK : (half + 1) * BANK]
@@ -217,18 +252,17 @@ def tile_list_point_pair_max_kernel(
                 open_batch("%d_0_%d" % (a, u), [(a, 0, 2 * u), (a, 0, 2 * u + 1)])
         for u in range(2):
             cast_w1(0, 0, u)
-        nc.vector.tensor_copy(v_s[:], tab_s[:].indirect(offs_sb[:]))
         for u in range(2):
             quantize_w1("0_0_%d" % u)
         for t in range(2):
             for half in range(2):
                 h_pass(0, 0, t, half)
-        gather_words(1, 0, BANK, "tab_s")
-        gather_words(1, BANK, BANK)
-        for m0 in (0, P // 2):
-            for u in range(2):
-                cast_w1(1, 0, u, m0, P // 2)
-        quantize_w1("1_0_0", 0, 1, "tab_w1")
+        gather_words(1, 0, S)
+        cast_one(1, 0, 0, 0, 48, False)
+        cast_one(1, 0, 0, 48, P, True)
+        quantize_w1("1_0_0", 0, 1)
+        cast_w1(1, 0, 1)
+        cast_one(1, 0, 1, 0, P, True)
         quantize_w1("1_0_0", 1, 1)
         for half in range(2):
             h_pass(1, 0, 0, half)
@@ -242,13 +276,21 @@ def tile_list_point_pair_max_kernel(
             open_picked(0, side, 0, PAIRS)
             pick_pairs(0, 0, side, 0, PAIRS)
         h_tile(0, 2)
-        h_tile(0, 3)
-        open_batch("u0", [(a, 1, t) for a in range(2) for t in (0, 1)], "w1_g_1_0_0")
-        open_batch("u1", [(a, 1, t) for a in range(2) for t in (2, 3)], "w1_s_1_0_1")
-        for u in range(2):
+        for half in range(2):
             for a in range(2):
-                cast_w1(a, 1, u)
+                h_pass(a, 0, 3, half)
+        open_batch("a0", [(0, 1, t) for t in range(PACK)], "w1_g_1_0_0")
+        cast_all(0, 1)
+        h[0, 3] = placed([P, S], F32, "h_0_3", 0)
+        for half in range(2):
+            h_out(0, 3, half)
+        open_batch("u0", [(1, 1, t) for t in (0, 1)])
+        open_batch("u1", [(1, 1, t) for t in (2, 3)], "w1_s_1_0_1")
+        for u in range(2):
+            cast_w1(1, 1, u)
         for t in range(1, PACK):
+            if t == 3:
+                quantize_w1("a0")
             for side in range(2):
                 pick_pairs(0, t, side, 0, PAIRS)
         quantize_w1("u0")

@@ -83,19 +83,19 @@ def tile_list_point_pair_max_kernel(
         load_scales()
         nc.sync.dma_start(offs_sb[:], offs)
         load_table(0)
-        load_w1(0, 0, sb([P, PACK, K_PASS], F32, "w1_raw_0_0"))
-        load_table(1)
         load_w1(1, 0, sb([P, PACK, K_PASS], F32, "w1_raw_1_0"))
+        load_table(1)
+        load_w1(0, 0, sb([P, PACK, K_PASS], F32, "w1_raw_0_0"))
         nc.sync.dma_start(pos_sb[0][:], pos1)
         nc.sync.dma_start(pos_sb[1][:], pos2)
 
         nc.vector.tensor_copy(g_s[:, 0:S], tab_s[:].indirect(offs_sb[:]))
         for q in (0, 2):
-            move_scales(nc.gpsimd, 1, q)
+            move_scales(nc.gpsimd, 0, q)
         for q in (0, 2, 1, 3):
-            move_scales(nc.scalar, 0, q)
-        for q in (1, 3):
             move_scales(nc.scalar, 1, q)
+        for q in (1, 3):
+            move_scales(nc.scalar, 0, q)
 
         b1_sb = placed([P, 2, PACK], F32, "b1_sb", 12864)
         w2_w = placed([P, 2, 2 * N], U8, "w2_w", 8192)
@@ -170,8 +170,10 @@ def tile_list_point_pair_max_kernel(
         h_ps = {}
 
         def h_pass(a, b, t, half):
-            if a == 0:
-                h_ps[b, t, half] = bank(2 * t + half, "h_ps_%d_%d_%d" % (b, t, half))
+            opens = a == 1 - b
+            if opens:
+                first_bank = 2 * (t % 2) if b == 0 else (2 * t + 4) % 8
+                h_ps[b, t, half] = bank(first_bank + half, "h_ps_%d_%d_%d" % (b, t, half))
             name, i = where[a, b, t]
             m_cols = slice(i * P, (i + 1) * P)
             j_cols = slice(half * BANK, (half + 1) * BANK)
@@ -181,11 +183,15 @@ def tile_list_point_pair_max_kernel(
                 lhsT_scale=planes[name][:, m_cols],
                 rhs=v_w[a][:, j_cols].bitcast(FP8X4),
                 rhs_scale=v_s[4 * a :, j_cols],
-                start=(a == 0),
-                stop=(a == 1),
+                start=opens,
+                stop=not opens,
             )
 
-        h = {(b, t): sb([P, S], F32, "h_%d_%d" % (b, t)) for b in range(2) for t in range(PACK) if (b, t) != (0, 3)}
+        own_tile = [(0, 0), (0, 1), (0, 2), (1, 0), (1, 1)]
+        h = {(b, t): sb([P, S], F32, "h_%d_%d" % (b, t)) for b, t in own_tile}
+        row = sb([P, 6528], F32, "tail_row")
+        h[1, 2] = row[:, 2304:3328]
+        h[1, 3] = row[:, 3328:4352]
 
         def h_out(b, t, half, on_vector=False):
             dst = h[b, t][:, half * BANK : (half + 1) * BANK]
@@ -197,13 +203,13 @@ def tile_list_point_pair_max_kernel(
 
         def h_tile(b, t):
             for half in range(2):
-                for a in range(2):
+                for a in (1 - b, b):
                     h_pass(a, b, t, half)
                 h_out(b, t, half)
 
         def pick(dst, b, t, side, q0, qn):
             nc.vector.tensor_copy(
-                dst, h[b, t][:].indirect(pos_sb[side][:, q0 // LIST_ROWS : (q0 + qn) // LIST_ROWS])
+                dst, h[b, t][:, 0:S].indirect(pos_sb[side][:, q0 // LIST_ROWS : (q0 + qn) // LIST_ROWS])
             )
 
         picked, z_g, z_c, z_s = {}, {}, {}, {}
@@ -217,9 +223,11 @@ def tile_list_point_pair_max_kernel(
             pick(picked[b, q0, side][:, t, 0:qn], b, t, side, q0, qn)
 
         def pair_max(b, q0, qn, tag=""):
-            z_g[b, q0] = sb([P, qn, PACK], BF16, "z_g_%d_%d" % (b, q0), tag)
+            if (b, q0) not in z_g:
+                rounded = sb([P, qn, PACK], BF16, "z_g_%d_%d" % (b, q0), tag)
+                z_g[b, q0] = rounded[:]
             nc.vector.tensor_tensor(
-                z_g[b, q0][:].rearrange("p (c i) t -> p c t i", i=4),
+                z_g[b, q0].rearrange("p (c i) t -> p c t i", i=4),
                 picked[b, q0, 0][:, :, 0:qn].rearrange("p t (c i) -> p c t i", i=4),
                 picked[b, q0, 1][:, :, 0:qn].rearrange("p t (c i) -> p c t i", i=4),
                 ALU.max,
@@ -231,7 +239,7 @@ def tile_list_point_pair_max_kernel(
             nc.vector.quantize_mx(
                 out=z_c[b, q0][:].bitcast(FP8X4),
                 scales=z_s[b, q0][:],
-                in_=z_g[b, q0][:].rearrange("p q t -> p (q t)"),
+                in_=z_g[b, q0].rearrange("p q t -> p (q t)"),
             )
 
         def out_pass(b, c, q, z0, start, stop):
@@ -251,41 +259,41 @@ def tile_list_point_pair_max_kernel(
             for u in range(2):
                 open_batch("%d_0_%d" % (a, u), [(a, 0, 2 * u), (a, 0, 2 * u + 1)])
         for u in range(2):
-            cast_w1(0, 0, u)
+            cast_w1(1, 0, u)
         for u in range(2):
-            quantize_w1("0_0_%d" % u)
-        for t in range(2):
-            for half in range(2):
-                h_pass(0, 0, t, half)
-        gather_words(1, 0, S)
-        cast_one(1, 0, 0, 0, 48, False)
-        cast_one(1, 0, 0, 48, P, True)
-        quantize_w1("1_0_0", 0, 1)
-        cast_w1(1, 0, 1)
-        cast_one(1, 0, 1, 0, P, True)
-        quantize_w1("1_0_0", 1, 1)
+            quantize_w1("1_0_%d" % u)
         for half in range(2):
-            h_pass(1, 0, 0, half)
-        h_out(0, 0, 0)
-        h_out(0, 0, 1, on_vector=True)
+            gather_words(1, half * BANK, BANK)
+            for t in range(2):
+                h_pass(1, 0, t, half)
+        cast_one(0, 0, 0, 0, P // 2, False)
+        cast_one(0, 0, 0, P // 2, P, True)
+        quantize_w1("0_0_0", 0, 1)
+        cast_w1(0, 0, 1)
+        cast_one(0, 0, 1, 0, P, True)
         for half in range(2):
-            h_pass(1, 0, 1, half)
+            h_pass(0, 0, 0, half)
+        h_out(0, 0, 0, on_vector=True)
+        h_out(0, 0, 1)
+        quantize_w1("0_0_0", 1, 1)
+        for half in range(2):
+            h_pass(0, 0, 1, half)
             h_out(0, 1, half)
-        quantize_w1("1_0_1", tag="w1_g_1_0_0")
+        quantize_w1("0_0_1", tag="w1_g_0_0_0")
         for side in range(2):
             open_picked(0, side, 0, PAIRS)
             pick_pairs(0, 0, side, 0, PAIRS)
         h_tile(0, 2)
         for half in range(2):
-            for a in range(2):
+            for a in (1, 0):
                 h_pass(a, 0, 3, half)
-        open_batch("a0", [(0, 1, t) for t in range(PACK)], "w1_g_1_0_0")
+        open_batch("a0", [(0, 1, t) for t in range(PACK)], "w1_g_0_0_0")
         cast_all(0, 1)
         h[0, 3] = placed([P, S], F32, "h_0_3", 0)
         for half in range(2):
             h_out(0, 3, half)
         open_batch("u0", [(1, 1, t) for t in (0, 1)])
-        open_batch("u1", [(1, 1, t) for t in (2, 3)], "w1_s_1_0_1")
+        open_batch("u1", [(1, 1, t) for t in (2, 3)], "w1_s_0_0_1")
         for u in range(2):
             cast_w1(1, 1, u)
         for t in range(1, PACK):
@@ -299,7 +307,7 @@ def tile_list_point_pair_max_kernel(
         quantize_w1("u1")
         h_tile(1, 2)
         h_tile(1, 3)
-        pair_max(0, 0, PAIRS, "w1_s_1_0_1")
+        pair_max(0, 0, PAIRS, "w1_s_0_0_1")
 
         own = [bank(c, "o_own_%d" % c) for c in range(N_TILES)]
         shared = [bank(N_TILES + i, "o_shared_%d" % i) for i in range(2)]
@@ -319,9 +327,15 @@ def tile_list_point_pair_max_kernel(
         def store(staged, c0, cn, q0, qn):
             nc.sync.dma_start(out=out_v[:, c0 : c0 + cn, q0 : q0 + qn], in_=staged[:, c0 : c0 + cn, :])
 
-        open_picked(1, 0, 0, PAIRS)
-        open_picked(1, 1, 0, 256)
-        pick_pairs(1, 0, 0, 0, PAIRS)
+        picked[1, 0, 0] = row[:, 0:1024].rearrange("p (t q) -> p t q", t=PACK)
+        picked[1, 256, 0] = row[:, 256:1280].rearrange("p (t q) -> p t q", t=PACK)
+        picked[1, 384, 0] = picked[1, 256, 0][:, :, GROUP:]
+        picked[1, 0, 1] = row[:, 1280:2304].rearrange("p (t q) -> p t q", t=PACK)
+        picked[1, 256, 1] = row[:, 128:6528].rearrange("p (r q) -> p r q", q=256)[:, ::8, :]
+        picked[1, 384, 1] = picked[1, 256, 1][:, :, GROUP:]
+        z_g[1, 0] = row[:, 4352:4864].bitcast(BF16).rearrange("p (q t) -> p q t", t=PACK)
+
+        pick_pairs(1, 0, 0, 0, 256)
         quantize_z(0, 0, PAIRS)
         for c in range(N_TILES):
             out_pass(0, c, 0, 0, True, False)
@@ -330,13 +344,13 @@ def tile_list_point_pair_max_kernel(
             out_pass(0, c, 256, 0, c % 3 == 0, False)
         pick_pairs(1, 0, 1, 0, 256)
         for t in (1, 2):
-            pick_pairs(1, t, 0, 0, PAIRS)
-            pick_pairs(1, t, 1, 0, 256)
-        pick_pairs(1, 3, 0, 0, 256)
+            for side in range(2):
+                pick_pairs(1, t, side, 0, 256)
+        pick(row[:, 768:1280], 1, 3, 0, 0, PAIRS)
         pick_pairs(1, 3, 1, 0, 256)
-        pick_pairs(1, 3, 0, 256, GROUP)
+        pick_pairs(1, 3, 1, 256, 256)
         pair_max(1, 0, 256)
-        pick_pairs(1, 3, 0, 384, GROUP)
+        pick_pairs(1, 2, 1, 256, GROUP)
         quantize_z(1, 0, 256)
         staged = sb([P, N_TILES, 256], F32, "staged_first")
         for c in range(N_TILES):
@@ -347,11 +361,11 @@ def tile_list_point_pair_max_kernel(
                 store(staged, c - 1, 2, 0, 256)
         for c in range(N_TILES):
             out_pass(0, c, 384, 0, True, False)
-        open_picked(1, 1, 256, GROUP, "picked_1_0_1")
-        open_picked(1, 1, 384, GROUP, "z_g_1_0")
-        for t in range(PACK):
+        for t in range(3):
+            pick_pairs(1, t, 0, 256, 256)
+        for t in range(2):
             pick_pairs(1, t, 1, 256, GROUP)
-        pick_pairs(1, 0, 1, 384, GROUP)
+        pick_pairs(1, 2, 1, 384, GROUP)
         pair_max(1, 256, GROUP)
         pick_pairs(1, 1, 1, 384, GROUP)
         quantize_z(1, 256, GROUP)
@@ -362,13 +376,13 @@ def tile_list_point_pair_max_kernel(
                 for done in range(c - 2, c + 1):
                     add_bias(staged[:, done, :], o_ps[done, 256], done)
                 store(staged, c - 2, 3, 256, GROUP)
-        for t in (2, 3):
-            pick_pairs(1, t, 1, 384, GROUP)
+        pick_pairs(1, 0, 1, 384, GROUP)
         pair_max(1, 384, GROUP)
         quantize_z(1, 384, GROUP)
         staged = sb([P, N_TILES, GROUP], F32, "staged_last")
         for c in range(N_TILES):
             out_pass(1, c, 384, 384, False, True)
             add_bias(staged[:, c, :], o_ps[c, 384], c, on_vector=(c % 2 == 1))
-            if c % 3 == 2:
-                store(staged, c - 2, 3, 384, GROUP)
+        store(staged, 0, 3, 384, GROUP)
+        store(staged, 3, 2, 384, GROUP)
+        store(staged, 5, 1, 384, GROUP)

@@ -138,17 +138,10 @@ def tile_list_point_pair_max_kernel(
                 in_=raw[a, b][:].rearrange("p j (m t) -> p m j t", t=PACK)[:, :, :, 2 * u : 2 * u + 2],
             )
 
-        def cast_all(a, b):
+        def cast_all(a, b, m0=0, m1=P, on_vector=False):
             name, i = where[a, b, 0]
-            nc.scalar.copy(
-                out=grouped[name][:].rearrange("p t m j -> p m j t"),
-                in_=raw[a, b][:].rearrange("p j (m t) -> p m j t", t=PACK),
-            )
-
-        def cast_one(a, b, t, m0, m1, on_vector):
-            name, i = where[a, b, t]
-            dst = grouped[name][:, i, m0:m1, :]
-            src = raw[a, b][:].rearrange("p j (m t) -> p m j t", t=PACK)[:, m0:m1, :, t]
+            dst = grouped[name][:].rearrange("p t m j -> p m j t")[:, m0:m1, :, :]
+            src = raw[a, b][:].rearrange("p j (m t) -> p m j t", t=PACK)[:, m0:m1, :, :]
             if on_vector:
                 nc.vector.tensor_copy(dst, src)
             else:
@@ -233,13 +226,14 @@ def tile_list_point_pair_max_kernel(
                 ALU.max,
             )
 
-        def quantize_z(b, q0, qn, tag=""):
+        def quantize_z(b, q0, qn, tag="", z0=-1):
+            z0 = q0 if z0 < 0 else z0
             z_c[b, q0] = sb([P, qn], U32, "z_c_%d_%d" % (b, q0), tag)
             z_s[b, q0] = sb([P, qn], U8, "z_s_%d_%d" % (b, q0))
             nc.vector.quantize_mx(
                 out=z_c[b, q0][:].bitcast(FP8X4),
                 scales=z_s[b, q0][:],
-                in_=z_g[b, q0].rearrange("p q t -> p (q t)"),
+                in_=z_g[b, z0][:, q0 - z0 : q0 - z0 + qn, :].rearrange("p q t -> p (q t)"),
             )
 
         def out_pass(b, c, q, z0, start, stop):
@@ -256,30 +250,25 @@ def tile_list_point_pair_max_kernel(
 
         gather_words(0, 0, S)
         for a in range(2):
-            for u in range(2):
-                open_batch("%d_0_%d" % (a, u), [(a, 0, 2 * u), (a, 0, 2 * u + 1)])
-        for u in range(2):
-            cast_w1(1, 0, u)
-        for u in range(2):
-            quantize_w1("1_0_%d" % u)
+            open_batch("%d_0" % a, [(a, 0, t) for t in range(PACK)])
+        cast_all(1, 0)
+        quantize_w1("1_0")
         for half in range(2):
             gather_words(1, half * BANK, BANK)
             for t in range(2):
                 h_pass(1, 0, t, half)
-        cast_one(0, 0, 0, 0, P // 2, False)
-        cast_one(0, 0, 0, P // 2, P, True)
-        quantize_w1("0_0_0", 0, 1)
-        cast_w1(0, 0, 1)
-        cast_one(0, 0, 1, 0, P, True)
+        cast_all(0, 0, 0, 48)
+        cast_all(0, 0, 48, P, True)
+        quantize_w1("0_0", 0, 1)
+        quantize_w1("0_0", 1, 1)
         for half in range(2):
             h_pass(0, 0, 0, half)
         h_out(0, 0, 0, on_vector=True)
         h_out(0, 0, 1)
-        quantize_w1("0_0_0", 1, 1)
+        quantize_w1("0_0", 2, 2)
         for half in range(2):
             h_pass(0, 0, 1, half)
             h_out(0, 1, half)
-        quantize_w1("0_0_1", tag="w1_g_0_0_0")
         for side in range(2):
             open_picked(0, side, 0, PAIRS)
             pick_pairs(0, 0, side, 0, PAIRS)
@@ -287,13 +276,13 @@ def tile_list_point_pair_max_kernel(
         for half in range(2):
             for a in (1, 0):
                 h_pass(a, 0, 3, half)
-        open_batch("a0", [(0, 1, t) for t in range(PACK)], "w1_g_0_0_0")
+        open_batch("a0", [(0, 1, t) for t in range(PACK)], "w1_s_0_0")
         cast_all(0, 1)
         h[0, 3] = placed([P, S], F32, "h_0_3", 0)
         for half in range(2):
             h_out(0, 3, half)
         open_batch("u0", [(1, 1, t) for t in (0, 1)])
-        open_batch("u1", [(1, 1, t) for t in (2, 3)], "w1_s_0_0_1")
+        open_batch("u1", [(1, 1, t) for t in (2, 3)], "w1_c_0_0")
         for u in range(2):
             cast_w1(1, 1, u)
         for t in range(1, PACK):
@@ -307,7 +296,7 @@ def tile_list_point_pair_max_kernel(
         quantize_w1("u1")
         h_tile(1, 2)
         h_tile(1, 3)
-        pair_max(0, 0, PAIRS, "w1_s_0_0_1")
+        pair_max(0, 0, PAIRS, "w1_c_0_0")
 
         own = [bank(c, "o_own_%d" % c) for c in range(N_TILES)]
         shared = [bank(N_TILES + i, "o_shared_%d" % i) for i in range(2)]
@@ -336,12 +325,13 @@ def tile_list_point_pair_max_kernel(
         z_g[1, 0] = row[:, 4352:4864].bitcast(BF16).rearrange("p (q t) -> p q t", t=PACK)
 
         pick_pairs(1, 0, 0, 0, 256)
-        quantize_z(0, 0, PAIRS)
+        quantize_z(0, 0, 256)
+        quantize_z(0, 256, GROUP, z0=0)
         for c in range(N_TILES):
             out_pass(0, c, 0, 0, True, False)
             out_pass(0, c, 128, 0, False, False)
         for c in range(N_TILES):
-            out_pass(0, c, 256, 0, c % 3 == 0, False)
+            out_pass(0, c, 256, 256, c % 3 == 0, False)
         pick_pairs(1, 0, 1, 0, 256)
         for t in (1, 2):
             for side in range(2):
@@ -359,8 +349,6 @@ def tile_list_point_pair_max_kernel(
             add_bias(staged[:, c, :], own[c][:, 0:256], c)
             if c % 2 == 1:
                 store(staged, c - 1, 2, 0, 256)
-        for c in range(N_TILES):
-            out_pass(0, c, 384, 0, True, False)
         for t in range(3):
             pick_pairs(1, t, 0, 256, 256)
         for t in range(2):
@@ -377,6 +365,9 @@ def tile_list_point_pair_max_kernel(
                     add_bias(staged[:, done, :], o_ps[done, 256], done)
                 store(staged, c - 2, 3, 256, GROUP)
         pick_pairs(1, 0, 1, 384, GROUP)
+        quantize_z(0, 384, GROUP, "z_g_1_256", z0=0)
+        for c in range(N_TILES):
+            out_pass(0, c, 384, 384, True, False)
         pair_max(1, 384, GROUP)
         quantize_z(1, 384, GROUP)
         staged = sb([P, N_TILES, GROUP], F32, "staged_last")

@@ -22,8 +22,10 @@ K_PASS = P * PACK
 BANK = 512
 LIST_ROWS = 16
 N_TILES = N // P
-GROUP = 128
 QUAD = 32
+HALF = 64
+NARROW = 256
+PARTS = {"A": (0, 256), "B": (256, 128), "C": (384, 128)}
 
 
 def tile_list_point_pair_max_kernel(
@@ -33,11 +35,14 @@ def tile_list_point_pair_max_kernel(
     with ExitStack() as ctx:
         lists = ctx.enter_context(tc.tile_pool(name="lists", bufs=1))
         keep = ctx.enter_context(tc.tile_pool(name="keep", bufs=1))
-        late = ctx.enter_context(tc.tile_pool(name="late", bufs=1))
+        reused = ctx.enter_context(tc.tile_pool(name="reused", bufs=1))
         psum = ctx.enter_context(tc.psum_pool(name="psum", bufs=1))
 
         def sb(shape, dtype, name, tag=""):
             return keep.tile(shape, dtype, name=name, tag=tag or name, align_bytes=64)
+
+        def placed(shape, dtype, name, kib):
+            return reused.tile(shape, dtype, name=name, tag=name, offset=kib * 1024, align_bytes=64)
 
         def bank(i, name):
             return psum.tile([P, BANK], F32, name=name, tag="bank%d" % i)
@@ -45,66 +50,200 @@ def tile_list_point_pair_max_kernel(
         offs_sb = lists.tile([P, S // LIST_ROWS], U16, name="offs_sb")
         pos_sb = [lists.tile([P, PAIRS // LIST_ROWS], U16, name="pos%d_sb" % i) for i in (1, 2)]
 
-        tab_w = [sb([P, T], I32, "tab_w%d" % a) for a in range(2)]
-        tab_s = sb([P, T], U8, "tab_s")
+        tab_w = {}
+        tab_s = placed([P, T], U8, "tab_s", 30)
+        g_s = sb([P, S], U8, "g_s")
         v_s = sb([P, S], U8, "v_s")
-
-        def placed(shape, dtype, name, offset):
-            return late.tile(shape, dtype, name=name, tag=name, offset=offset, align_bytes=64)
-
-        g_s = placed([P, 4864], U8, "g_s", 8128)
 
         nc.vector.memset(tab_s[QUAD : 2 * QUAD, :].bitcast(I32), 0)
         nc.vector.memset(tab_s[2 * QUAD :, :].bitcast(I32), 0)
         nc.vector.memset(v_s[:].bitcast(I32), 0)
 
-        def load_scales():
-            nc.sync.dma_start(
-                out=tab_s[0:QUAD, :].bitcast(I32),
-                in_=tab_scales.rearrange("a q t -> (a q) t").bitcast(I32),
-            )
-
         def move_scales(queue, a, q):
             queue.dma_start(
                 out=v_s[QUAD * q + 4 * a : QUAD * q + 4 * a + 4, :].bitcast(I32),
-                in_=g_s[16 * a + 4 * q : 16 * a + 4 * q + 4, 0:S].bitcast(I32),
+                in_=g_s[16 * a + 4 * q : 16 * a + 4 * q + 4, :].bitcast(I32),
             )
 
         def load_table(a):
+            tab_w[a] = placed([P, T], I32, "tab_w%d" % a, 16 * a)
             nc.sync.dma_start(out=tab_w[a][:], in_=tab_words[a].rearrange("p t i -> p (t i)").bitcast(I32))
 
         raw = {}
 
-        def load_w1(a, b, piece):
-            raw[a, b] = piece
-            block = w1[a * K_PASS : (a + 1) * K_PASS, b * K_PASS : (b + 1) * K_PASS]
-            nc.sync.dma_start(out=piece[:], in_=block.rearrange("(p j) c -> p j c", j=PACK))
+        def load_w1(a, c0, cn, kib):
+            raw[a, c0] = placed([P, PACK, cn], F32, "w1_raw_%d_%d" % (a, c0), kib)
+            block = w1[a * K_PASS : (a + 1) * K_PASS, c0 : c0 + cn]
+            nc.sync.dma_start(out=raw[a, c0][:], in_=block.rearrange("(p j) c -> p j c", j=PACK))
 
-        load_scales()
+        nc.sync.dma_start(
+            out=tab_s[0:QUAD, :].bitcast(I32), in_=tab_scales.rearrange("a q t -> (a q) t").bitcast(I32)
+        )
         nc.sync.dma_start(offs_sb[:], offs)
-        load_table(0)
-        load_w1(1, 0, sb([P, PACK, K_PASS], F32, "w1_raw_1_0"))
-        load_table(1)
-        load_w1(0, 0, sb([P, PACK, K_PASS], F32, "w1_raw_0_0"))
         nc.sync.dma_start(pos_sb[0][:], pos1)
         nc.sync.dma_start(pos_sb[1][:], pos2)
+        b1_lo = sb([P, 2, 2], F32, "b1_lo")
+        nc.sync.dma_start(out=b1_lo[:], in_=b1[0:K_PASS].rearrange("(g m u) -> m g u", g=2, u=2))
+        load_table(0)
+        load_w1(0, 0, NARROW, 36)
 
-        nc.vector.tensor_copy(g_s[:, 0:S], tab_s[:].indirect(offs_sb[:]))
-        for q in (0, 2):
-            move_scales(nc.gpsimd, 0, q)
-        for q in (0, 2, 1, 3):
-            move_scales(nc.scalar, 1, q)
-        for q in (1, 3):
-            move_scales(nc.scalar, 0, q)
+        nc.vector.tensor_copy(g_s[:], tab_s[:].indirect(offs_sb[:]))
+        moves = [(a, q) for a in range(2) for q in range(4)]
+        for a, q in moves[:5]:
+            move_scales(nc.sync, a, q)
+        load_table(1)
+        for a, q in moves[5:]:
+            move_scales(nc.sync, a, q)
+        load_w1(1, 0, NARROW, 32)
 
-        b1_sb = placed([P, 2, PACK], F32, "b1_sb", 12864)
-        w2_w = placed([P, 2, 2 * N], U8, "w2_w", 8192)
-        w2_s = placed([P, 2, N], U8, "w2_s", 11264)
-        b2_sb = placed([P, N_TILES], F32, "b2_sb", 12800)
-        nc.gpsimd.memset(w2_s[:].rearrange("p b n -> p (b n)").bitcast(I32), 0)
-        nc.sync.dma_start(out=b1_sb[:], in_=b1.rearrange("(b p t) -> p b t", b=2, t=PACK))
-        load_w1(0, 1, placed([P, PACK, K_PASS], F32, "w1_raw_0_1", 0))
-        load_w1(1, 1, placed([P, PACK, K_PASS], F32, "w1_raw_1_1", 12928))
+        v_w = [sb([P, S], U32, "v_w%d" % a) for a in range(2)]
+
+        def gather_words(a, j0, jn):
+            nc.vector.tensor_copy(
+                v_w[a][:, j0 : j0 + jn],
+                tab_w[a][:].bitcast(U32).indirect(offs_sb[:, j0 // LIST_ROWS : (j0 + jn) // LIST_ROWS]),
+            )
+
+        grouped, codes, planes = {}, {}, {}
+
+        def grouped_of(a, g):
+            if (a, g) not in grouped:
+                grouped[a, g] = sb([P, (2, 2, PACK)[g] * K_PASS], BF16, "w1_g_%d_%d" % (a, g))
+            return grouped[a, g][:]
+
+        def cast_narrow(a, g, u0=0, un=2):
+            dst = grouped_of(a, g).rearrange("p (u w e j) -> p w j e u", u=2, e=2, j=PACK)
+            src = raw[a, g * NARROW][:].rearrange("p j (w e u) -> p w j e u", e=2, u=2)
+            if un == 1:
+                nc.scalar.copy(out=dst[:, :, :, :, u0], in_=src[:, :, :, :, u0])
+            else:
+                nc.scalar.copy(out=dst, in_=src)
+
+        def cast_wide(a):
+            nc.scalar.copy(
+                out=grouped_of(a, 2).rearrange("p (t m j) -> p m j t", t=PACK, j=PACK),
+                in_=raw[a, K_PASS][:].rearrange("p j (m t) -> p m j t", t=PACK),
+            )
+
+        def quantize_w1(a, g, u0=0, un=2):
+            if u0 == 0:
+                count = (2, 2, PACK)[g]
+                codes[a, g] = sb([P, count * P], U32, "w1_c_%d_%d" % (a, g))
+                planes[a, g] = sb([P, count * P], U8, "w1_s_%d_%d" % (a, g))
+            cols = slice(u0 * P, (u0 + un) * P)
+            nc.vector.quantize_mx(
+                out=codes[a, g][:, cols].bitcast(FP8X4),
+                scales=planes[a, g][:, cols],
+                in_=grouped[a, g][:, u0 * K_PASS : (u0 + un) * K_PASS],
+            )
+
+        h_ps = {}
+        first_bank = [0, 2, 4, 6, 0, 2, 0, 2]
+
+        def h_pass(a, r, half, opens):
+            if opens:
+                h_ps[r, half] = bank(first_bank[r] + half, "h_ps_%d_%d" % (r, half))
+            g = min(r // 2, 2)
+            m_cols = slice((r - 2 * g) * P, (r - 2 * g + 1) * P)
+            j_cols = slice(half * BANK, (half + 1) * BANK)
+            nc.tensor.matmul_mx(
+                out=h_ps[r, half][:],
+                lhsT=codes[a, g][:, m_cols].bitcast(FP8X4),
+                lhsT_scale=planes[a, g][:, m_cols],
+                rhs=v_w[a][:, j_cols].bitcast(FP8X4),
+                rhs_scale=v_s[4 * a :, j_cols],
+                start=opens,
+                stop=not opens,
+            )
+
+        h = {}
+        h_place = {1: 4, 2: 8, 3: 16}
+
+        def h_out(r, half, on_vector=False):
+            if half == 0:
+                h[r] = placed([P, S], F32, "h_%d" % r, h_place[r]) if r in h_place else sb([P, S], F32, "h_%d" % r)
+            dst = h[r][:, half * BANK : (half + 1) * BANK]
+            bias = b1_lo[:, r // 2, r % 2 : r % 2 + 1] if r < PACK else b1_hi[:, r - PACK : r - PACK + 1]
+            if on_vector:
+                nc.vector.tensor_scalar(dst, h_ps[r, half][:], bias, 0.0, ALU.add, ALU.max)
+            else:
+                nc.scalar.activation(dst, h_ps[r, half][:], ACT.Relu, bias=bias)
+
+        def h_passes(r, first):
+            for half in range(2):
+                h_pass(first, r, half, True)
+                h_pass(1 - first, r, half, False)
+
+        def h_outs(r):
+            for half in range(2):
+                h_out(r, half)
+
+        run = (2 * PACK - 1) * PAIRS
+        row = sb([P, 2 * run], F32, "picked")
+        picked = {}
+        for side in range(2):
+            picked[1, side] = row[:, side * run : side * run + PACK * PAIRS]
+            picked[0, side] = row[:, side * run + (PACK - 1) * PAIRS : (side + 1) * run]
+        early = [sb([P, 2 * 2 * PAIRS], F32, "early_%d" % g) for g in range(2)]
+
+        def pick(r, side, q0=0, qn=PAIRS):
+            if r < PACK:
+                base = (2 * side + r % 2) * PAIRS + q0
+                dst = early[r // 2][:, base : base + qn]
+            else:
+                base = (r - PACK) * PAIRS + q0
+                dst = picked[1, side][:, base : base + qn]
+            nc.vector.tensor_copy(
+                dst, h[r][:].indirect(pos_sb[side][:, q0 // LIST_ROWS : (q0 + qn) // LIST_ROWS])
+            )
+
+        def deal(g, u0, un):
+            for e in range(2):
+                src = early[g][e:P:2, :].rearrange("p (s c) -> p s c", s=2)
+                dst = row[HALF * g : HALF * (g + 1), :].rearrange("p (s c) -> p s c", s=2)
+                slot = PACK - 1 + 2 * e + u0
+                nc.sync.dma_start(
+                    out=dst[:, :, slot * PAIRS : (slot + un) * PAIRS],
+                    in_=src[:, :, u0 * PAIRS : (u0 + un) * PAIRS],
+                )
+
+        z_g, z_c, z_s = {}, {}, {}
+
+        def pair_max(b, part):
+            q0, qn = PARTS[part]
+            z_g[b, part] = sb([P, qn * PACK], BF16, "z_g_%d_%s" % (b, part))
+            sides = [picked[b, side].rearrange("p (t c i) -> p c t i", t=PACK, i=4) for side in range(2)]
+            nc.vector.tensor_tensor(
+                z_g[b, part][:].rearrange("p (c i t) -> p c t i", i=4, t=PACK),
+                sides[0][:, q0 // 4 : (q0 + qn) // 4, :, :],
+                sides[1][:, q0 // 4 : (q0 + qn) // 4, :, :],
+                ALU.max,
+            )
+
+        def quantize_z(b, part):
+            qn = PARTS[part][1]
+            z_c[b, part] = sb([P, qn], U32, "z_c_%d_%s" % (b, part))
+            z_s[b, part] = sb([P, qn], U8, "z_s_%d_%s" % (b, part))
+            nc.vector.quantize_mx(out=z_c[b, part][:].bitcast(FP8X4), scales=z_s[b, part][:], in_=z_g[b, part][:])
+
+        gather_words(0, 0, S)
+        load_w1(1, NARROW, NARROW, 0)
+        load_w1(0, NARROW, NARROW, 4)
+        load_w1(0, K_PASS, K_PASS, 8)
+        cast_narrow(0, 0)
+        quantize_w1(0, 0)
+        w2_s = placed([P, 2, N], U8, "w2_s", 36)
+        nc.vector.memset(w2_s[:].rearrange("p b n -> p (b n)").bitcast(I32), 0)
+        for r in range(2):
+            for half in range(2):
+                h_pass(0, r, half, True)
+        gather_words(1, 0, BANK)
+        gather_words(1, BANK, BANK)
+        b1_hi = placed([P, PACK], F32, "b1_hi", 28)
+        w2_w = placed([P, 2, 2 * N], U8, "w2_w", 24)
+        b2_sb = placed([P, N_TILES], F32, "b2_sb", 27)
+        load_w1(1, K_PASS, K_PASS, 16)
+        nc.sync.dma_start(out=b1_hi[:], in_=b1[K_PASS:].rearrange("(p t) -> p t", t=PACK))
         nc.sync.dma_start(out=w2_w[:].bitcast(I32), in_=w2_words.rearrange("b p n -> p b n").bitcast(I32))
         for q in range(4):
             nc.sync.dma_start(
@@ -114,266 +253,110 @@ def tile_list_point_pair_max_kernel(
         with nc.allow_non_contiguous_dma(reason="one bias value to a partition"):
             nc.sync.dma_start(out=b2_sb[:], in_=b2.rearrange("(c p) -> p c", p=P))
 
-        v_w = {}
-
-        def gather_words(a, j0, jn, tag=""):
-            if j0 == 0:
-                v_w[a] = sb([P, S], U32, "v_w%d" % a, tag)
-            nc.vector.tensor_copy(
-                v_w[a][:, j0 : j0 + jn],
-                tab_w[a][:].bitcast(U32).indirect(offs_sb[:, j0 // LIST_ROWS : (j0 + jn) // LIST_ROWS]),
-            )
-
-        grouped, codes, planes, where = {}, {}, {}, {}
-
-        def open_batch(name, operands, tag=""):
-            grouped[name] = sb([P, len(operands), P, PACK], BF16, "w1_g_" + name, tag)
-            for i, operand in enumerate(operands):
-                where[operand] = (name, i)
-
-        def cast_w1(a, b, u):
-            name, i = where[a, b, 2 * u]
-            nc.scalar.copy(
-                out=grouped[name][:, i : i + 2, :, :].rearrange("p t m j -> p m j t"),
-                in_=raw[a, b][:].rearrange("p j (m t) -> p m j t", t=PACK)[:, :, :, 2 * u : 2 * u + 2],
-            )
-
-        def cast_all(a, b, m0=0, m1=P, on_vector=False):
-            name, i = where[a, b, 0]
-            dst = grouped[name][:].rearrange("p t m j -> p m j t")[:, m0:m1, :, :]
-            src = raw[a, b][:].rearrange("p j (m t) -> p m j t", t=PACK)[:, m0:m1, :, :]
-            if on_vector:
-                nc.vector.tensor_copy(dst, src)
-            else:
-                nc.scalar.copy(out=dst, in_=src)
-
-        def quantize_w1(name, i0=0, n=0, tag=""):
-            count = grouped[name].shape[1]
-            n = n or count
-            if i0 == 0:
-                codes[name] = sb([P, count * P], U32, "w1_c_" + name, tag)
-                planes[name] = sb([P, count * P], U8, "w1_s_" + name)
-            cols = slice(i0 * P, (i0 + n) * P)
-            nc.vector.quantize_mx(
-                out=codes[name][:, cols].bitcast(FP8X4),
-                scales=planes[name][:, cols],
-                in_=grouped[name][:, i0 : i0 + n, :, :].rearrange("p t m j -> p (t m j)"),
-            )
-
-        h_ps = {}
-
-        def h_pass(a, b, t, half):
-            opens = a == 1 - b
-            if opens:
-                first_bank = 2 * (t % 2) if b == 0 else (2 * t + 4) % 8
-                h_ps[b, t, half] = bank(first_bank + half, "h_ps_%d_%d_%d" % (b, t, half))
-            name, i = where[a, b, t]
-            m_cols = slice(i * P, (i + 1) * P)
-            j_cols = slice(half * BANK, (half + 1) * BANK)
-            nc.tensor.matmul_mx(
-                out=h_ps[b, t, half][:],
-                lhsT=codes[name][:, m_cols].bitcast(FP8X4),
-                lhsT_scale=planes[name][:, m_cols],
-                rhs=v_w[a][:, j_cols].bitcast(FP8X4),
-                rhs_scale=v_s[4 * a :, j_cols],
-                start=opens,
-                stop=not opens,
-            )
-
-        own_tile = [(0, 0), (0, 1), (0, 2), (1, 0), (1, 1)]
-        h = {(b, t): sb([P, S], F32, "h_%d_%d" % (b, t)) for b, t in own_tile}
-        row = sb([P, 6528], F32, "tail_row")
-        h[1, 2] = row[:, 2304:3328]
-        h[1, 3] = row[:, 3328:4352]
-
-        def h_out(b, t, half, on_vector=False):
-            dst = h[b, t][:, half * BANK : (half + 1) * BANK]
-            bias = b1_sb[:, b, t : t + 1]
-            if on_vector:
-                nc.vector.tensor_scalar(dst, h_ps[b, t, half][:], bias, 0.0, ALU.add, ALU.max)
-            else:
-                nc.scalar.activation(dst, h_ps[b, t, half][:], ACT.Relu, bias=bias)
-
-        def h_tile(b, t):
+        cast_narrow(1, 0, 0, 1)
+        quantize_w1(1, 0, 0, 1)
+        cast_narrow(1, 0, 1, 1)
+        quantize_w1(1, 0, 1, 1)
+        for r in range(2):
             for half in range(2):
-                for a in (1 - b, b):
-                    h_pass(a, b, t, half)
-                h_out(b, t, half)
-
-        def pick(dst, b, t, side, q0, qn):
-            nc.vector.tensor_copy(
-                dst, h[b, t][:, 0:S].indirect(pos_sb[side][:, q0 // LIST_ROWS : (q0 + qn) // LIST_ROWS])
-            )
-
-        picked, z_g, z_c, z_s = {}, {}, {}, {}
-
-        def open_picked(b, side, q0, qn, tag=""):
-            tile = sb([P, PACK, qn], F32, "picked_%d_%d_%d" % (b, q0, side), tag)
-            for q in range(q0, q0 + qn, GROUP):
-                picked[b, q, side] = tile[:, :, q - q0 :]
-
-        def pick_pairs(b, t, side, q0, qn):
-            pick(picked[b, q0, side][:, t, 0:qn], b, t, side, q0, qn)
-
-        def pair_max(b, q0, qn, tag=""):
-            if (b, q0) not in z_g:
-                rounded = sb([P, qn, PACK], BF16, "z_g_%d_%d" % (b, q0), tag)
-                z_g[b, q0] = rounded[:]
-            nc.vector.tensor_tensor(
-                z_g[b, q0].rearrange("p (c i) t -> p c t i", i=4),
-                picked[b, q0, 0][:, :, 0:qn].rearrange("p t (c i) -> p c t i", i=4),
-                picked[b, q0, 1][:, :, 0:qn].rearrange("p t (c i) -> p c t i", i=4),
-                ALU.max,
-            )
-
-        def quantize_z(b, q0, qn, tag="", z0=-1):
-            z0 = q0 if z0 < 0 else z0
-            z_c[b, q0] = sb([P, qn], U32, "z_c_%d_%d" % (b, q0), tag)
-            z_s[b, q0] = sb([P, qn], U8, "z_s_%d_%d" % (b, q0))
-            nc.vector.quantize_mx(
-                out=z_c[b, q0][:].bitcast(FP8X4),
-                scales=z_s[b, q0][:],
-                in_=z_g[b, z0][:, q0 - z0 : q0 - z0 + qn, :].rearrange("p q t -> p (q t)"),
-            )
-
-        def out_pass(b, c, q, z0, start, stop):
-            z_cols = slice(q - z0, q - z0 + GROUP)
-            nc.tensor.matmul_mx(
-                out=o_ps[c, q],
-                lhsT=w2_w[:, b, 2 * P * c : 2 * P * (c + 1)].bitcast(FP4X4),
-                lhsT_scale=w2_s[:, b, P * c : P * (c + 1)],
-                rhs=z_c[b, z0][:, z_cols].bitcast(FP8X4),
-                rhs_scale=z_s[b, z0][:, z_cols],
-                start=start,
-                stop=stop,
-            )
-
-        gather_words(0, 0, S)
-        for a in range(2):
-            open_batch("%d_0" % a, [(a, 0, t) for t in range(PACK)])
-        cast_all(1, 0)
-        quantize_w1("1_0")
+                h_pass(1, r, half, False)
+        for a in (1, 0):
+            for u in range(2):
+                cast_narrow(a, 1, u, 1)
         for half in range(2):
-            gather_words(1, half * BANK, BANK)
-            for t in range(2):
-                h_pass(1, 0, t, half)
-        cast_all(0, 0, 0, 48)
-        cast_all(0, 0, 48, P, True)
-        quantize_w1("0_0", 0, 1)
-        quantize_w1("0_0", 1, 1)
-        for half in range(2):
-            h_pass(0, 0, 0, half)
-        h_out(0, 0, 0, on_vector=True)
-        h_out(0, 0, 1)
-        quantize_w1("0_0", 2, 2)
-        for half in range(2):
-            h_pass(0, 0, 1, half)
-            h_out(0, 1, half)
+            h_out(0, half, on_vector=True)
+        quantize_w1(1, 1)
+        quantize_w1(0, 1)
+        h_passes(2, 1)
+        h_passes(3, 1)
         for side in range(2):
-            open_picked(0, side, 0, PAIRS)
-            pick_pairs(0, 0, side, 0, PAIRS)
-        h_tile(0, 2)
-        for half in range(2):
-            for a in (1, 0):
-                h_pass(a, 0, 3, half)
-        open_batch("a0", [(0, 1, t) for t in range(PACK)], "w1_s_0_0")
-        cast_all(0, 1)
-        h[0, 3] = placed([P, S], F32, "h_0_3", 0)
-        for half in range(2):
-            h_out(0, 3, half)
-        open_batch("u0", [(1, 1, t) for t in (0, 1)])
-        open_batch("u1", [(1, 1, t) for t in (2, 3)], "w1_c_0_0")
-        for u in range(2):
-            cast_w1(1, 1, u)
-        for t in range(1, PACK):
-            if t == 3:
-                quantize_w1("a0")
+            pick(0, side)
+        h_outs(1)
+        for side in range(2):
+            pick(1, side)
+        deal(0, 0, 2)
+        for a in range(2):
+            cast_wide(a)
+            quantize_w1(a, 2, 0, PACK)
+            h_outs(2 + a)
             for side in range(2):
-                pick_pairs(0, t, side, 0, PAIRS)
-        quantize_w1("u0")
-        h_tile(1, 0)
-        h_tile(1, 1)
-        quantize_w1("u1")
-        h_tile(1, 2)
-        h_tile(1, 3)
-        pair_max(0, 0, PAIRS, "w1_c_0_0")
+                pick(2 + a, side)
+            deal(1, a, 1)
+        h_passes(4, 0)
+        h_passes(5, 0)
+        for r in (4, 5):
+            h_outs(r)
+            h_passes(r + 2, 0)
+            for side in range(2):
+                pick(r, side)
 
-        own = [bank(c, "o_own_%d" % c) for c in range(N_TILES)]
-        shared = [bank(N_TILES + i, "o_shared_%d" % i) for i in range(2)]
-        o_ps = {}
-        for c in range(N_TILES):
-            for q in (0, 128, 384):
-                o_ps[c, q] = own[c][:, q : q + GROUP]
-            o_ps[c, 256] = shared[c // 3][:, (c % 3) * GROUP : (c % 3 + 1) * GROUP]
+        banks_of = {"A": (4, 4, 5, 5, 6, 6), "B": (7, 7, 7, 0, 0, 0), "C": (1, 1, 2, 2, 3, 3)}
+        o_bank, o_ps, staged = {}, {}, {}
         out_v = out.rearrange("(c p) q -> p c q", p=P)
 
-        def add_bias(dst, src, c, on_vector=False):
-            if on_vector:
-                nc.vector.tensor_scalar_add(dst, src, b2_sb[:, c : c + 1])
-            else:
-                nc.scalar.activation(dst, src, ACT.Identity, bias=b2_sb[:, c : c + 1])
+        def out_passes(b, part):
+            qn = PARTS[part][1]
+            mine = banks_of[part]
+            for c in range(N_TILES):
+                first = mine.index(mine[c])
+                last = first + len([i for i in mine if i == mine[c]]) - 1
+                if b == 0:
+                    if c == first:
+                        o_bank[mine[c]] = bank(mine[c], "o_%s_%d" % (part, c))
+                    o_ps[part, c] = o_bank[mine[c]][:, (c - first) * qn : (c - first + 1) * qn]
+                nc.tensor.matmul_mx(
+                    out=o_ps[part, c],
+                    lhsT=w2_w[:, b, 2 * P * c : 2 * P * (c + 1)].bitcast(FP4X4),
+                    lhsT_scale=w2_s[:, b, P * c : P * (c + 1)],
+                    rhs=z_c[b, part][:].bitcast(FP8X4),
+                    rhs_scale=z_s[b, part][:],
+                    start=(b == 0 and c == first),
+                    stop=(b == 1 and c == last),
+                )
 
-        def store(staged, c0, cn, q0, qn):
-            nc.sync.dma_start(out=out_v[:, c0 : c0 + cn, q0 : q0 + qn], in_=staged[:, c0 : c0 + cn, :])
+        def finish(part, on_vector=()):
+            q0, qn = PARTS[part]
+            mine = banks_of[part]
+            staged[part] = sb([P, N_TILES, qn], F32, "staged_" + part)
+            for c in range(N_TILES):
+                if c in on_vector:
+                    nc.vector.tensor_scalar_add(staged[part][:, c, :], o_ps[part, c], b2_sb[:, c : c + 1])
+                else:
+                    nc.scalar.activation(staged[part][:, c, :], o_ps[part, c], ACT.Identity, bias=b2_sb[:, c : c + 1])
+                if c == N_TILES - 1 or mine[c + 1] != mine[c]:
+                    first = mine.index(mine[c])
+                    nc.sync.dma_start(
+                        out=out_v[:, first : c + 1, q0 : q0 + qn], in_=staged[part][:, first : c + 1, :]
+                    )
 
-        picked[1, 0, 0] = row[:, 0:1024].rearrange("p (t q) -> p t q", t=PACK)
-        picked[1, 256, 0] = row[:, 256:1280].rearrange("p (t q) -> p t q", t=PACK)
-        picked[1, 384, 0] = picked[1, 256, 0][:, :, GROUP:]
-        picked[1, 0, 1] = row[:, 1280:2304].rearrange("p (t q) -> p t q", t=PACK)
-        picked[1, 256, 1] = row[:, 128:6528].rearrange("p (r q) -> p r q", q=256)[:, ::8, :]
-        picked[1, 384, 1] = picked[1, 256, 1][:, :, GROUP:]
-        z_g[1, 0] = row[:, 4352:4864].bitcast(BF16).rearrange("p (q t) -> p q t", t=PACK)
-
-        pick_pairs(1, 0, 0, 0, 256)
-        quantize_z(0, 0, 256)
-        quantize_z(0, 256, GROUP, z0=0)
-        for c in range(N_TILES):
-            out_pass(0, c, 0, 0, True, False)
-            out_pass(0, c, 128, 0, False, False)
-        for c in range(N_TILES):
-            out_pass(0, c, 256, 256, c % 3 == 0, False)
-        pick_pairs(1, 0, 1, 0, 256)
-        for t in (1, 2):
-            for side in range(2):
-                pick_pairs(1, t, side, 0, 256)
-        pick(row[:, 768:1280], 1, 3, 0, 0, PAIRS)
-        pick_pairs(1, 3, 1, 0, 256)
-        pick_pairs(1, 3, 1, 256, 256)
-        pair_max(1, 0, 256)
-        pick_pairs(1, 2, 1, 256, GROUP)
-        quantize_z(1, 0, 256)
-        staged = sb([P, N_TILES, 256], F32, "staged_first")
-        for c in range(N_TILES):
-            out_pass(1, c, 0, 0, False, False)
-            out_pass(1, c, 128, 0, False, True)
-            add_bias(staged[:, c, :], own[c][:, 0:256], c)
-            if c % 2 == 1:
-                store(staged, c - 1, 2, 0, 256)
-        for t in range(3):
-            pick_pairs(1, t, 0, 256, 256)
-        for t in range(2):
-            pick_pairs(1, t, 1, 256, GROUP)
-        pick_pairs(1, 2, 1, 384, GROUP)
-        pair_max(1, 256, GROUP)
-        pick_pairs(1, 1, 1, 384, GROUP)
-        quantize_z(1, 256, GROUP)
-        staged = sb([P, N_TILES, GROUP], F32, "staged_middle")
-        for c in range(N_TILES):
-            out_pass(1, c, 256, 256, False, c % 3 == 2)
-            if c % 3 == 2:
-                for done in range(c - 2, c + 1):
-                    add_bias(staged[:, done, :], o_ps[done, 256], done)
-                store(staged, c - 2, 3, 256, GROUP)
-        pick_pairs(1, 0, 1, 384, GROUP)
-        quantize_z(0, 384, GROUP, "z_g_1_256", z0=0)
-        for c in range(N_TILES):
-            out_pass(0, c, 384, 384, True, False)
-        pair_max(1, 384, GROUP)
-        quantize_z(1, 384, GROUP)
-        staged = sb([P, N_TILES, GROUP], F32, "staged_last")
-        for c in range(N_TILES):
-            out_pass(1, c, 384, 384, False, True)
-            add_bias(staged[:, c, :], o_ps[c, 384], c, on_vector=(c % 2 == 1))
-        store(staged, 0, 3, 384, GROUP)
-        store(staged, 3, 2, 384, GROUP)
-        store(staged, 5, 1, 384, GROUP)
+        for r in (6, 7):
+            h_outs(r)
+        for side in range(2):
+            pick(6, side)
+        pair_max(0, "A")
+        pair_max(0, "B")
+        for side in range(2):
+            pick(7, side, *PARTS["A"])
+        quantize_z(0, "A")
+        out_passes(0, "A")
+        pair_max(1, "A")
+        pick(7, 0, *PARTS["B"])
+        quantize_z(1, "A")
+        out_passes(1, "A")
+        finish("A")
+        pick(7, 1, *PARTS["B"])
+        pair_max(0, "C")
+        pair_max(1, "B")
+        quantize_z(0, "B")
+        out_passes(0, "B")
+        pick(7, 0, *PARTS["C"])
+        quantize_z(1, "B")
+        out_passes(1, "B")
+        finish("B")
+        pick(7, 1, *PARTS["C"])
+        quantize_z(0, "C")
+        out_passes(0, "C")
+        pair_max(1, "C")
+        quantize_z(1, "C")
+        out_passes(1, "C")
+        finish("C", on_vector=(2, 3))

@@ -1,6 +1,7 @@
 from contextlib import ExitStack
 
 import concourse.mybir as mybir
+from concourse.masks import make_identity
 
 K, T, S, PAIRS, H, N = 1024, 4096, 1024, 512, 1024, 768
 FLOPS = 2 * K * H * S + 2 * H * N * PAIRS
@@ -42,7 +43,7 @@ def tile_list_point_pair_max_kernel(
             return keep.tile(shape, dtype, name=name, tag=tag or name, align_bytes=64)
 
         def placed(shape, dtype, name, kib):
-            return reused.tile(shape, dtype, name=name, tag=name, offset=kib * 1024, align_bytes=64)
+            return reused.tile(shape, dtype, name=name, tag=name, offset=int(kib * 1024), align_bytes=64)
 
         def bank(i, name):
             return psum.tile([P, BANK], F32, name=name, tag="bank%d" % i)
@@ -55,6 +56,8 @@ def tile_list_point_pair_max_kernel(
         g_s = sb([P, S], U8, "g_s")
         v_s = sb([P, S], U8, "v_s")
 
+        ident = sb([P, P], F32, "ident")
+        make_identity(nc, ident[:])
         nc.vector.memset(tab_s[QUAD : 2 * QUAD, :].bitcast(I32), 0)
         nc.vector.memset(tab_s[2 * QUAD :, :].bitcast(I32), 0)
         nc.vector.memset(v_s[:].bitcast(I32), 0)
@@ -82,10 +85,8 @@ def tile_list_point_pair_max_kernel(
         nc.sync.dma_start(offs_sb[:], offs)
         nc.sync.dma_start(pos_sb[0][:], pos1)
         nc.sync.dma_start(pos_sb[1][:], pos2)
-        b1_lo = sb([P, 2, 2], F32, "b1_lo")
-        nc.sync.dma_start(out=b1_lo[:], in_=b1[0:K_PASS].rearrange("(g m u) -> m g u", g=2, u=2))
         load_table(0)
-        load_w1(0, 0, NARROW, 36)
+        load_w1(0, 0, NARROW, 37)
 
         nc.vector.tensor_copy(g_s[:], tab_s[:].indirect(offs_sb[:]))
         moves = [(a, q) for a in range(2) for q in range(4)]
@@ -94,7 +95,9 @@ def tile_list_point_pair_max_kernel(
         load_table(1)
         for a, q in moves[5:]:
             move_scales(nc.sync, a, q)
-        load_w1(1, 0, NARROW, 32)
+        load_w1(1, 0, NARROW, 32.0625)
+        b1_lo = placed([P, 2, 2], F32, "b1_lo", 32)
+        nc.sync.dma_start(out=b1_lo[:], in_=b1[0:K_PASS].rearrange("(g m u) -> m g u", g=2, u=2))
 
         v_w = [sb([P, S], U32, "v_w%d" % a) for a in range(2)]
 
@@ -111,13 +114,10 @@ def tile_list_point_pair_max_kernel(
                 grouped[a, g] = sb([P, (2, 2, PACK)[g] * K_PASS], BF16, "w1_g_%d_%d" % (a, g))
             return grouped[a, g][:]
 
-        def cast_narrow(a, g, u0=0, un=2):
+        def cast_narrow(a, g):
             dst = grouped_of(a, g).rearrange("p (u w e j) -> p w j e u", u=2, e=2, j=PACK)
             src = raw[a, g * NARROW][:].rearrange("p j (w e u) -> p w j e u", e=2, u=2)
-            if un == 1:
-                nc.scalar.copy(out=dst[:, :, :, :, u0], in_=src[:, :, :, :, u0])
-            else:
-                nc.scalar.copy(out=dst, in_=src)
+            nc.scalar.copy(out=dst, in_=src)
 
         def cast_wide(a):
             nc.scalar.copy(
@@ -163,7 +163,7 @@ def tile_list_point_pair_max_kernel(
             if half == 0:
                 h[r] = placed([P, S], F32, "h_%d" % r, h_place[r]) if r in h_place else sb([P, S], F32, "h_%d" % r)
             dst = h[r][:, half * BANK : (half + 1) * BANK]
-            bias = b1_lo[:, r // 2, r % 2 : r % 2 + 1] if r < PACK else b1_hi[:, r - PACK : r - PACK + 1]
+            bias = b1_lo[:, r // 2, r % 2 : r % 2 + 1] if r < PACK else b1_hi[r // 2 - 2][:, r % 2 : r % 2 + 1]
             if on_vector:
                 nc.vector.tensor_scalar(dst, h_ps[r, half][:], bias, 0.0, ALU.add, ALU.max)
             else:
@@ -178,12 +178,11 @@ def tile_list_point_pair_max_kernel(
             for half in range(2):
                 h_out(r, half)
 
-        run = (2 * PACK - 1) * PAIRS
-        row = sb([P, 2 * run], F32, "picked")
-        picked = {}
-        for side in range(2):
-            picked[1, side] = row[:, side * run : side * run + PACK * PAIRS]
-            picked[0, side] = row[:, side * run + (PACK - 1) * PAIRS : (side + 1) * run]
+        late = [sb([P, PACK * PAIRS], F32, "late_%d" % side) for side in range(2)]
+
+        def late_slot(side, t):
+            return late[side][:].rearrange("p (n t q) -> p t n q", n=2, t=PACK)[:, t, :, :]
+
         early = [sb([P, 2 * 2 * PAIRS], F32, "early_%d" % g) for g in range(2)]
 
         def pick(r, side, q0=0, qn=PAIRS):
@@ -191,32 +190,59 @@ def tile_list_point_pair_max_kernel(
                 base = (2 * side + r % 2) * PAIRS + q0
                 dst = early[r // 2][:, base : base + qn]
             else:
-                base = (r - PACK) * PAIRS + q0
-                dst = picked[1, side][:, base : base + qn]
+                dst = late_slot(side, r - PACK)
+                if qn < PAIRS:
+                    dst = dst[:, q0 // 256, q0 % 256 : q0 % 256 + qn]
             nc.vector.tensor_copy(
                 dst, h[r][:].indirect(pos_sb[side][:, q0 // LIST_ROWS : (q0 + qn) // LIST_ROWS])
             )
 
-        def deal(g, u0, un):
-            for e in range(2):
-                src = early[g][e:P:2, :].rearrange("p (s c) -> p s c", s=2)
-                dst = row[HALF * g : HALF * (g + 1), :].rearrange("p (s c) -> p s c", s=2)
-                slot = PACK - 1 + 2 * e + u0
-                nc.sync.dma_start(
-                    out=dst[:, :, slot * PAIRS : (slot + un) * PAIRS],
-                    in_=src[:, :, u0 * PAIRS : (u0 + un) * PAIRS],
-                )
-
+        turned = sb([P, PACK * 2 * P], F32, "turned")
         z_g, z_c, z_s = {}, {}, {}
 
-        def pair_max(b, part):
-            q0, qn = PARTS[part]
-            z_g[b, part] = sb([P, qn * PACK], BF16, "z_g_%d_%s" % (b, part))
-            sides = [picked[b, side].rearrange("p (t c i) -> p c t i", t=PACK, i=4) for side in range(2)]
+        def early_max(g, kib, i):
+            words = placed([P, 2 * PAIRS], BF16, "z_pairs_%d" % g, kib)
+            sides = early[g][:].rearrange("p (s u c i) -> p s c u i", s=2, u=2, i=4)
             nc.vector.tensor_tensor(
-                z_g[b, part][:].rearrange("p (c i t) -> p c t i", i=4, t=PACK),
-                sides[0][:, q0 // 4 : (q0 + qn) // 4, :, :],
-                sides[1][:, q0 // 4 : (q0 + qn) // 4, :, :],
+                words[:].rearrange("p (c i u) -> p c u i", i=4, u=2), sides[:, 0, :, :, :], sides[:, 1, :, :, :], ALU.max
+            )
+            ps = bank(i, "turn_%d" % g)
+            for j in range(PACK):
+                nc.tensor.transpose(ps[:, j * P : (j + 1) * P], words[:].bitcast(F32)[:, j * P : (j + 1) * P], ident[:])
+            return ps
+
+        def turn_out(g, ps):
+            nc.scalar.copy(
+                out=turned[:].rearrange("p (j e g w) -> p j e g w", j=PACK, e=2, g=2)[:, :, :, g, :],
+                in_=ps[:].rearrange("p (j w e) -> p j e w", j=PACK, e=2),
+            )
+
+        def turn_back(i, jj):
+            ps = bank(i, "back_%d" % jj)
+            for n in range(PACK):
+                col = (PACK * jj + n) * P
+                nc.tensor.transpose(ps[:, n * P : (n + 1) * P], turned[:, col : col + P], ident[:])
+            return ps
+
+        def back_out(part, words, ps):
+            nc.scalar.copy(
+                out=words.rearrange("p (j q e) -> p j q e", q=P, e=2),
+                in_=ps.rearrange("p (j e q) -> p j q e", q=P, e=2),
+            )
+            z_g[0, part] = words.bitcast(BF16)
+
+        def late_max(part, words):
+            q0, qn = PARTS[part]
+            z_g[1, part] = words.bitcast(BF16)
+            sides = [
+                late[side][:].rearrange("p (n t c i) -> p n c t i", n=2, t=PACK, i=4)[:, q0 // 256, :, :, :]
+                for side in range(2)
+            ]
+            c0 = q0 % 256 // 4
+            nc.vector.tensor_tensor(
+                z_g[1, part].rearrange("p (c i t) -> p c t i", i=4, t=PACK),
+                sides[0][:, c0 : c0 + qn // 4, :, :],
+                sides[1][:, c0 : c0 + qn // 4, :, :],
                 ALU.max,
             )
 
@@ -224,7 +250,7 @@ def tile_list_point_pair_max_kernel(
             qn = PARTS[part][1]
             z_c[b, part] = sb([P, qn], U32, "z_c_%d_%s" % (b, part))
             z_s[b, part] = sb([P, qn], U8, "z_s_%d_%s" % (b, part))
-            nc.vector.quantize_mx(out=z_c[b, part][:].bitcast(FP8X4), scales=z_s[b, part][:], in_=z_g[b, part][:])
+            nc.vector.quantize_mx(out=z_c[b, part][:].bitcast(FP8X4), scales=z_s[b, part][:], in_=z_g[b, part])
 
         gather_words(0, 0, S)
         load_w1(1, NARROW, NARROW, 0)
@@ -232,18 +258,19 @@ def tile_list_point_pair_max_kernel(
         load_w1(0, K_PASS, K_PASS, 8)
         cast_narrow(0, 0)
         quantize_w1(0, 0)
-        w2_s = placed([P, 2, N], U8, "w2_s", 36)
+        w2_s = placed([P, 2, N], U8, "w2_s", 37)
         nc.vector.memset(w2_s[:].rearrange("p b n -> p (b n)").bitcast(I32), 0)
         for r in range(2):
             for half in range(2):
                 h_pass(0, r, half, True)
         gather_words(1, 0, BANK)
         gather_words(1, BANK, BANK)
-        b1_hi = placed([P, PACK], F32, "b1_hi", 28)
+        b1_hi = [placed([P, 2], F32, "b1_hi%d" % i, 28 + 2 * i) for i in range(2)]
         w2_w = placed([P, 2, 2 * N], U8, "w2_w", 24)
         b2_sb = placed([P, N_TILES], F32, "b2_sb", 27)
         load_w1(1, K_PASS, K_PASS, 16)
-        nc.sync.dma_start(out=b1_hi[:], in_=b1[K_PASS:].rearrange("(p t) -> p t", t=PACK))
+        for i in range(2):
+            nc.sync.dma_start(out=b1_hi[i][:], in_=b1[K_PASS:].rearrange("(p t) -> p t", t=PACK)[:, 2 * i : 2 * i + 2])
         nc.sync.dma_start(out=w2_w[:].bitcast(I32), in_=w2_words.rearrange("b p n -> p b n").bitcast(I32))
         for q in range(4):
             nc.sync.dma_start(
@@ -253,16 +280,14 @@ def tile_list_point_pair_max_kernel(
         with nc.allow_non_contiguous_dma(reason="one bias value to a partition"):
             nc.sync.dma_start(out=b2_sb[:], in_=b2.rearrange("(c p) -> p c", p=P))
 
-        cast_narrow(1, 0, 0, 1)
+        cast_narrow(1, 0)
         quantize_w1(1, 0, 0, 1)
-        cast_narrow(1, 0, 1, 1)
         quantize_w1(1, 0, 1, 1)
         for r in range(2):
             for half in range(2):
                 h_pass(1, r, half, False)
         for a in (1, 0):
-            for u in range(2):
-                cast_narrow(a, 1, u, 1)
+            cast_narrow(a, 1)
         for half in range(2):
             h_out(0, half, on_vector=True)
         quantize_w1(1, 1)
@@ -274,21 +299,37 @@ def tile_list_point_pair_max_kernel(
         h_outs(1)
         for side in range(2):
             pick(1, side)
-        deal(0, 0, 2)
-        for a in range(2):
-            cast_wide(a)
-            quantize_w1(a, 2, 0, PACK)
-            h_outs(2 + a)
-            for side in range(2):
-                pick(2 + a, side)
-            deal(1, a, 1)
+        cast_wide(0)
+        quantize_w1(0, 2, 0, PACK)
+        h_outs(2)
+        turn_ps = early_max(0, 12, 4)
+        for side in range(2):
+            pick(2, side)
+        cast_wide(1)
+        quantize_w1(1, 2, 0, PACK)
+        h_outs(3)
+        for side in range(2):
+            pick(3, side)
         h_passes(4, 0)
         h_passes(5, 0)
-        for r in (4, 5):
-            h_outs(r)
-            h_passes(r + 2, 0)
-            for side in range(2):
-                pick(r, side)
+        h_outs(4)
+        h_passes(6, 0)
+        for side in range(2):
+            pick(4, side)
+        h_outs(5)
+        h_passes(7, 0)
+        turn_out(0, turn_ps)
+        turn_ps = early_max(1, 28, 5)
+        for side in range(2):
+            pick(5, side)
+        h_outs(6)
+        turn_out(1, turn_ps)
+        h_outs(7)
+        spare = {part: sb([P, 2 * P], F32, "z_words_" + part) for part in ("0C", "1B", "1C")}
+        back_out("A", late[1][:, 3 * PAIRS :], turn_back(6, 0)[:])
+        rest = turn_back(7, 1)
+        back_out("B", late[0][:, 3 * PAIRS : 3 * PAIRS + 2 * P], rest[:, 0 : 2 * P])
+        back_out("C", spare["0C"][:], rest[:, 2 * P :])
 
         banks_of = {"A": (4, 4, 5, 5, 6, 6), "B": (7, 7, 7, 0, 0, 0), "C": (1, 1, 2, 2, 3, 3)}
         o_bank, o_ps, staged = {}, {}, {}
@@ -330,33 +371,28 @@ def tile_list_point_pair_max_kernel(
                     )
 
         for r in (6, 7):
-            h_outs(r)
-        for side in range(2):
-            pick(6, side)
-        pair_max(0, "A")
-        pair_max(0, "B")
-        for side in range(2):
-            pick(7, side, *PARTS["A"])
-        quantize_z(0, "A")
-        out_passes(0, "A")
-        pair_max(1, "A")
-        pick(7, 0, *PARTS["B"])
+            for side in range(2):
+                pick(r, side, *PARTS["A"])
+        for part in "ABC":
+            quantize_z(0, part)
+            out_passes(0, part)
+        pick(6, 1, *PARTS["B"])
+        late_max("A", late[0][:, 3 * PAIRS :])
+        pick(7, 1, *PARTS["B"])
         quantize_z(1, "A")
         out_passes(1, "A")
         finish("A")
-        pick(7, 1, *PARTS["B"])
-        pair_max(0, "C")
-        pair_max(1, "B")
-        quantize_z(0, "B")
-        out_passes(0, "B")
+        pick(6, 1, *PARTS["C"])
+        pick(6, 0, *PARTS["B"])
+        pick(7, 0, *PARTS["B"])
+        pick(7, 1, *PARTS["C"])
+        late_max("B", spare["1B"][:])
+        pick(6, 0, *PARTS["C"])
         pick(7, 0, *PARTS["C"])
         quantize_z(1, "B")
         out_passes(1, "B")
         finish("B")
-        pick(7, 1, *PARTS["C"])
-        quantize_z(0, "C")
-        out_passes(0, "C")
-        pair_max(1, "C")
+        late_max("C", spare["1C"][:])
         quantize_z(1, "C")
         out_passes(1, "C")
         finish("C", on_vector=(2, 3))

@@ -61,6 +61,8 @@ def tile_list_point_pair_max_kernel(
         nc.vector.memset(tab_s[QUAD : 2 * QUAD, :].bitcast(I32), 0)
         nc.vector.memset(tab_s[2 * QUAD :, :].bitcast(I32), 0)
         nc.vector.memset(v_s[:].bitcast(I32), 0)
+        minus_one = sb([P, PAIRS], F32, "minus_one")
+        nc.vector.memset(minus_one[:], -1.0)
 
         def move_scales(queue, a, q):
             queue.dma_start(
@@ -86,7 +88,7 @@ def tile_list_point_pair_max_kernel(
         nc.sync.dma_start(pos_sb[0][:], pos1)
         nc.sync.dma_start(pos_sb[1][:], pos2)
         load_table(0)
-        load_w1(0, 0, NARROW, 37)
+        load_w1(0, 0, NARROW, 44)
 
         nc.vector.tensor_copy(g_s[:], tab_s[:].indirect(offs_sb[:]))
         moves = [(a, q) for a in range(2) for q in range(4)]
@@ -157,17 +159,40 @@ def tile_list_point_pair_max_kernel(
             )
 
         h = {}
-        h_place = {1: 4, 2: 8, 3: 16}
+        h_place = {1: 2, 2: 8, 3: 24}
 
         def h_out(r, half, on_vector=False):
             if half == 0:
                 h[r] = placed([P, S], F32, "h_%d" % r, h_place[r]) if r in h_place else sb([P, S], F32, "h_%d" % r)
             dst = h[r][:, half * BANK : (half + 1) * BANK]
-            bias = b1_lo[:, r // 2, r % 2 : r % 2 + 1] if r < PACK else b1_hi[r // 2 - 2][:, r % 2 : r % 2 + 1]
+            bias = b1_lo[:, r // 2, r % 2 : r % 2 + 1] if r < PACK else b1_hi[:, r - PACK : r - PACK + 1]
             if on_vector:
                 nc.vector.tensor_scalar(dst, h_ps[r, half][:], bias, 0.0, ALU.add, ALU.max)
             else:
                 nc.scalar.activation(dst, h_ps[r, half][:], ACT.Relu, bias=bias)
+
+        quarter_ps = {}
+
+        def first_pass(a, n):
+            if a == 0:
+                quarter_ps[n] = bank((0, 1, 4, 5)[n], "h_ps_0_%d" % n)
+            j_cols = slice(n * 256, (n + 1) * 256)
+            nc.tensor.matmul_mx(
+                out=quarter_ps[n][:, 0:256],
+                lhsT=codes[a, 0][:, 0:P].bitcast(FP8X4),
+                lhsT_scale=planes[a, 0][:, 0:P],
+                rhs=v_w[a][:, j_cols].bitcast(FP8X4),
+                rhs_scale=v_s[4 * a :, j_cols],
+                start=(a == 0),
+                stop=(a == 1),
+            )
+
+        def first_out(n):
+            dst = h[0][:, n * 256 : (n + 1) * 256]
+            if n % 2 == 0:
+                nc.vector.tensor_scalar(dst, quarter_ps[n][:, 0:256], b1_lo[:, 0, 0:1], 0.0, ALU.add, ALU.max)
+            else:
+                nc.scalar.activation(dst, quarter_ps[n][:, 0:256], ACT.Relu, bias=b1_lo[:, 0, 0:1])
 
         def h_passes(r, first):
             for half in range(2):
@@ -183,53 +208,59 @@ def tile_list_point_pair_max_kernel(
         def late_slot(side, t):
             return late[side][:].rearrange("p (n t q) -> p t n q", n=2, t=PACK)[:, t, :, :]
 
-        early = [sb([P, 2 * 2 * PAIRS], F32, "early_%d" % g) for g in range(2)]
+        early = {}
 
         def pick(r, side, q0=0, qn=PAIRS):
             if r < PACK:
-                base = (2 * side + r % 2) * PAIRS + q0
-                dst = early[r // 2][:, base : base + qn]
+                name = "early_%d_%d" % (r, side)
+                early[r, side] = placed([P, PAIRS], F32, name, 6) if (r, side) == (0, 1) else sb([P, PAIRS], F32, name)
+                dst = early[r, side][:]
             else:
                 dst = late_slot(side, r - PACK)
                 if qn < PAIRS:
                     dst = dst[:, q0 // 256, q0 % 256 : q0 % 256 + qn]
-            nc.vector.tensor_copy(
-                dst, h[r][:].indirect(pos_sb[side][:, q0 // LIST_ROWS : (q0 + qn) // LIST_ROWS])
-            )
+            looked_up = h[r][:].indirect(pos_sb[side][:, q0 // LIST_ROWS : (q0 + qn) // LIST_ROWS])
+            if r < PACK and side == 1:
+                nc.vector.tensor_tensor(dst, looked_up, minus_one[:], ALU.mult)
+            else:
+                nc.vector.tensor_copy(dst, looked_up)
 
-        turned = sb([P, PACK * 2 * P], F32, "turned")
+        turned = {}
         z_g, z_c, z_s = {}, {}, {}
 
-        def early_max(g, kib, i):
-            words = placed([P, 2 * PAIRS], BF16, "z_pairs_%d" % g, kib)
-            sides = early[g][:].rearrange("p (s u c i) -> p s c u i", s=2, u=2, i=4)
-            nc.vector.tensor_tensor(
-                words[:].rearrange("p (c i u) -> p c u i", i=4, u=2), sides[:, 0, :, :, :], sides[:, 1, :, :, :], ALU.max
-            )
-            ps = bank(i, "turn_%d" % g)
-            for j in range(PACK):
-                nc.tensor.transpose(ps[:, j * P : (j + 1) * P], words[:].bitcast(F32)[:, j * P : (j + 1) * P], ident[:])
-            return ps
+        def turn_sum(dst, x, y):
+            nc.tensor.matmul(dst, lhsT=x, rhs=ident[:], is_transpose=True, start=True, stop=False)
+            nc.tensor.matmul(dst, lhsT=y, rhs=ident[:], is_transpose=True, start=False, stop=True)
 
-        def turn_out(g, ps):
+        def turn_early(j):
+            cols = slice(j * P, (j + 1) * P)
+            plain = bank(4 + 2 * (j % 2), "first_ps_%d" % j)
+            diff = bank(5 + 2 * (j % 2), "diff_ps_%d" % j)
+            places = [slice((2 * (r % 2) + r // 2) * P, (2 * (r % 2) + r // 2 + 1) * P) for r in range(PACK)]
+            for r in range(PACK):
+                nc.tensor.transpose(plain[:, places[r]], early[r, 0][:, cols], ident[:])
+            for r in range(PACK):
+                turn_sum(diff[:, places[r]], early[r, 0][:, cols], early[r, 1][:, cols])
+            turned[j] = sb([P, 2, K_PASS], F32, "turned_%d" % j)
             nc.scalar.copy(
-                out=turned[:].rearrange("p (j e g w) -> p j e g w", j=PACK, e=2, g=2)[:, :, :, g, :],
-                in_=ps[:].rearrange("p (j w e) -> p j e w", j=PACK, e=2),
+                out=turned[j][:, 0, :].rearrange("p (e n) -> p e n", e=2),
+                in_=plain[:].rearrange("p (n e) -> p e n", e=2),
+            )
+            nc.scalar.activation(
+                turned[j][:, 1, :].rearrange("p (e n) -> p e n", e=2),
+                diff[:].rearrange("p (n e) -> p e n", e=2),
+                ACT.Relu,
+                scale=-1.0,
             )
 
-        def turn_back(i, jj):
-            ps = bank(i, "back_%d" % jj)
-            for n in range(PACK):
-                col = (PACK * jj + n) * P
-                nc.tensor.transpose(ps[:, n * P : (n + 1) * P], turned[:, col : col + P], ident[:])
-            return ps
-
-        def back_out(part, words, ps):
+        def turn_back(j, rounded):
+            ps = bank(j, "back_%d" % j)
+            for t in range(PACK):
+                cols = slice(t * P, (t + 1) * P)
+                turn_sum(ps[:, cols], turned[j][:, 0, cols], turned[j][:, 1, cols])
             nc.scalar.copy(
-                out=words.rearrange("p (j q e) -> p j q e", q=P, e=2),
-                in_=ps.rearrange("p (j e q) -> p j q e", q=P, e=2),
+                out=rounded.rearrange("p (q t) -> p q t", t=PACK), in_=ps[:].rearrange("p (t q) -> p q t", t=PACK)
             )
-            z_g[0, part] = words.bitcast(BF16)
 
         def late_max(part, words):
             q0, qn = PARTS[part]
@@ -258,19 +289,19 @@ def tile_list_point_pair_max_kernel(
         load_w1(0, K_PASS, K_PASS, 8)
         cast_narrow(0, 0)
         quantize_w1(0, 0)
-        w2_s = placed([P, 2, N], U8, "w2_s", 37)
+        w2_s = placed([P, 2, N], U8, "w2_s", 44)
         nc.vector.memset(w2_s[:].rearrange("p b n -> p (b n)").bitcast(I32), 0)
-        for r in range(2):
-            for half in range(2):
-                h_pass(0, r, half, True)
+        for n in range(PACK):
+            first_pass(0, n)
+        for half in range(2):
+            h_pass(0, 1, half, True)
         gather_words(1, 0, BANK)
         gather_words(1, BANK, BANK)
-        b1_hi = [placed([P, 2], F32, "b1_hi%d" % i, 28 + 2 * i) for i in range(2)]
-        w2_w = placed([P, 2, 2 * N], U8, "w2_w", 24)
-        b2_sb = placed([P, N_TILES], F32, "b2_sb", 27)
-        load_w1(1, K_PASS, K_PASS, 16)
-        for i in range(2):
-            nc.sync.dma_start(out=b1_hi[i][:], in_=b1[K_PASS:].rearrange("(p t) -> p t", t=PACK)[:, 2 * i : 2 * i + 2])
+        b1_hi = placed([P, PACK], F32, "b1_hi", 20)
+        w2_w = placed([P, 2, 2 * N], U8, "w2_w", 16)
+        b2_sb = placed([P, N_TILES], F32, "b2_sb", 19)
+        load_w1(1, K_PASS, K_PASS, 24)
+        nc.sync.dma_start(out=b1_hi[:], in_=b1[K_PASS:].rearrange("(p t) -> p t", t=PACK))
         nc.sync.dma_start(out=w2_w[:].bitcast(I32), in_=w2_words.rearrange("b p n -> p b n").bitcast(I32))
         for q in range(4):
             nc.sync.dma_start(
@@ -283,26 +314,28 @@ def tile_list_point_pair_max_kernel(
         cast_narrow(1, 0)
         quantize_w1(1, 0, 0, 1)
         quantize_w1(1, 0, 1, 1)
-        for r in range(2):
-            for half in range(2):
-                h_pass(1, r, half, False)
-        for a in (1, 0):
-            cast_narrow(a, 1)
+        for n in range(PACK):
+            first_pass(1, n)
         for half in range(2):
-            h_out(0, half, on_vector=True)
+            h_pass(1, 1, half, False)
+        cast_narrow(1, 1)
+        h[0] = sb([P, S], F32, "h_0")
+        for n in range(PACK):
+            first_out(n)
+        cast_narrow(0, 1)
         quantize_w1(1, 1)
+        pick(0, 0)
         quantize_w1(0, 1)
         h_passes(2, 1)
         h_passes(3, 1)
-        for side in range(2):
-            pick(0, side)
-        h_outs(1)
+        h_out(1, 0, on_vector=True)
+        h_out(1, 1)
+        pick(0, 1)
         for side in range(2):
             pick(1, side)
         cast_wide(0)
         quantize_w1(0, 2, 0, PACK)
         h_outs(2)
-        turn_ps = early_max(0, 12, 4)
         for side in range(2):
             pick(2, side)
         cast_wide(1)
@@ -318,30 +351,32 @@ def tile_list_point_pair_max_kernel(
             pick(4, side)
         h_outs(5)
         h_passes(7, 0)
-        turn_out(0, turn_ps)
-        turn_ps = early_max(1, 28, 5)
         for side in range(2):
             pick(5, side)
         h_outs(6)
-        turn_out(1, turn_ps)
         h_outs(7)
-        spare = {part: sb([P, 2 * P], F32, "z_words_" + part) for part in ("0C", "1B", "1C")}
-        back_out("A", late[1][:, 3 * PAIRS :], turn_back(6, 0)[:])
-        rest = turn_back(7, 1)
-        back_out("B", late[0][:, 3 * PAIRS : 3 * PAIRS + 2 * P], rest[:, 0 : 2 * P])
-        back_out("C", spare["0C"][:], rest[:, 2 * P :])
+        spare = {name: sb([P, 2 * P], F32, "z_words_" + name) for name in ("0B", "0C", "1B", "1C")}
+        z_g[0, "A"] = late[1][:, 3 * PAIRS :].bitcast(BF16)
+        z_g[0, "B"] = spare["0B"][:].bitcast(BF16)
+        z_g[0, "C"] = spare["0C"][:].bitcast(BF16)
+        turn_early(0)
+        turn_early(1)
+        turn_back(0, z_g[0, "A"][:, 0:K_PASS])
+        turn_early(2)
+        turn_back(1, z_g[0, "A"][:, K_PASS:])
+        turn_early(3)
 
-        banks_of = {"A": (4, 4, 5, 5, 6, 6), "B": (7, 7, 7, 0, 0, 0), "C": (1, 1, 2, 2, 3, 3)}
+        banks_of = {"A": (4, 4, 5, 5, 6, 6), "B": (7, 7, 7, 0, 0, 0), "C": (1, 1, 1, 2, 2, 3)}
         o_bank, o_ps, staged = {}, {}, {}
         out_v = out.rearrange("(c p) q -> p c q", p=P)
 
-        def out_passes(b, part):
+        def out_passes(b, part, opens):
             qn = PARTS[part][1]
             mine = banks_of[part]
             for c in range(N_TILES):
                 first = mine.index(mine[c])
                 last = first + len([i for i in mine if i == mine[c]]) - 1
-                if b == 0:
+                if opens:
                     if c == first:
                         o_bank[mine[c]] = bank(mine[c], "o_%s_%d" % (part, c))
                     o_ps[part, c] = o_bank[mine[c]][:, (c - first) * qn : (c - first + 1) * qn]
@@ -351,8 +386,8 @@ def tile_list_point_pair_max_kernel(
                     lhsT_scale=w2_s[:, b, P * c : P * (c + 1)],
                     rhs=z_c[b, part][:].bitcast(FP8X4),
                     rhs_scale=z_s[b, part][:],
-                    start=(b == 0 and c == first),
-                    stop=(b == 1 and c == last),
+                    start=(opens and c == first),
+                    stop=(not opens and c == last),
                 )
 
         def finish(part, on_vector=()):
@@ -370,29 +405,33 @@ def tile_list_point_pair_max_kernel(
                         out=out_v[:, first : c + 1, q0 : q0 + qn], in_=staged[part][:, first : c + 1, :]
                     )
 
-        for r in (6, 7):
-            for side in range(2):
-                pick(r, side, *PARTS["A"])
-        for part in "ABC":
-            quantize_z(0, part)
-            out_passes(0, part)
-        pick(6, 1, *PARTS["B"])
-        late_max("A", late[0][:, 3 * PAIRS :])
-        pick(7, 1, *PARTS["B"])
+        for side in range(2):
+            pick(6, side, *PARTS["A"])
+        pick(6, 0, 256, 256)
+        for side in range(2):
+            pick(7, side, *PARTS["A"])
+        pick(7, 0, 256, 256)
+        quantize_z(0, "A")
+        out_passes(0, "A", True)
+        turn_back(2, z_g[0, "B"])
+        late_max("A", late[1][:, 3 * PAIRS :])
+        quantize_z(0, "B")
         quantize_z(1, "A")
-        out_passes(1, "A")
+        out_passes(1, "A", False)
+        turn_back(3, z_g[0, "C"])
         finish("A")
+        out_passes(0, "B", True)
+        pick(6, 1, *PARTS["B"])
+        pick(7, 1, *PARTS["B"])
         pick(6, 1, *PARTS["C"])
-        pick(6, 0, *PARTS["B"])
-        pick(7, 0, *PARTS["B"])
-        pick(7, 1, *PARTS["C"])
+        quantize_z(0, "C")
+        out_passes(0, "C", True)
         late_max("B", spare["1B"][:])
-        pick(6, 0, *PARTS["C"])
-        pick(7, 0, *PARTS["C"])
+        pick(7, 1, *PARTS["C"])
         quantize_z(1, "B")
-        out_passes(1, "B")
+        out_passes(1, "B", False)
         finish("B")
         late_max("C", spare["1C"][:])
         quantize_z(1, "C")
-        out_passes(1, "C")
-        finish("C", on_vector=(2, 3))
+        out_passes(1, "C", False)
+        finish("C", on_vector=(0, 1, 2, 5))

@@ -43,7 +43,7 @@ def tile_list_point_pair_max_kernel(
             return keep.tile(shape, dtype, name=name, tag=tag or name, align_bytes=64)
 
         def placed(shape, dtype, name, kib):
-            return reused.tile(shape, dtype, name=name, tag=name, offset=int(kib * 1024), align_bytes=64)
+            return reused.tile(shape, dtype, name=name, tag=name, offset=kib * 1024, align_bytes=64)
 
         def bank(i, name):
             return psum.tile([P, BANK], F32, name=name, tag="bank%d" % i)
@@ -52,7 +52,7 @@ def tile_list_point_pair_max_kernel(
         pos_sb = [lists.tile([P, PAIRS // LIST_ROWS], U16, name="pos%d_sb" % i) for i in (1, 2)]
 
         tab_w = {}
-        tab_s = placed([P, T], U8, "tab_s", 30)
+        tab_s = placed([P, T], U8, "tab_s", 31)
         g_s = sb([P, S], U8, "g_s")
         v_s = sb([P, S], U8, "v_s")
 
@@ -71,7 +71,7 @@ def tile_list_point_pair_max_kernel(
             )
 
         def load_table(a):
-            tab_w[a] = placed([P, T], I32, "tab_w%d" % a, 16 * a)
+            tab_w[a] = placed([P, T], I32, "tab_w%d" % a, 17 * a)
             nc.sync.dma_start(out=tab_w[a][:], in_=tab_words[a].rearrange("p t i -> p (t i)").bitcast(I32))
 
         raw = {}
@@ -97,9 +97,17 @@ def tile_list_point_pair_max_kernel(
         load_table(1)
         for a, q in moves[5:]:
             move_scales(nc.sync, a, q)
-        load_w1(1, 0, NARROW, 32.0625)
-        b1_lo = placed([P, 2, 2], F32, "b1_lo", 32)
-        nc.sync.dma_start(out=b1_lo[:], in_=b1[0:K_PASS].rearrange("(g m u) -> m g u", g=2, u=2))
+        load_w1(1, 0, NARROW, 34)
+        b1_pairs = b1[0:K_PASS].rearrange("(g m u) -> g m u", g=2, u=2)
+        bias = {}
+
+        def load_bias(r):
+            column = placed([P, 1], F32, "b1_%d" % r, (33, 8, 22, 23)[r])
+            with nc.allow_non_contiguous_dma(reason="one bias value to a partition"):
+                nc.sync.dma_start(out=column[:], in_=b1_pairs[r // 2][:, r % 2 : r % 2 + 1])
+            bias[r] = column[:]
+
+        load_bias(0)
 
         v_w = [sb([P, S], U32, "v_w%d" % a) for a in range(2)]
 
@@ -121,10 +129,10 @@ def tile_list_point_pair_max_kernel(
             src = raw[a, g * NARROW][:].rearrange("p j (w e u) -> p w j e u", e=2, u=2)
             nc.scalar.copy(out=dst, in_=src)
 
-        def cast_wide(a):
+        def cast_wide(a, t0, tn):
             nc.scalar.copy(
-                out=grouped_of(a, 2).rearrange("p (t m j) -> p m j t", t=PACK, j=PACK),
-                in_=raw[a, K_PASS][:].rearrange("p j (m t) -> p m j t", t=PACK),
+                out=grouped_of(a, 2).rearrange("p (t m j) -> p m j t", t=PACK, j=PACK)[:, :, :, t0 : t0 + tn],
+                in_=raw[a, K_PASS][:].rearrange("p j (m t) -> p m j t", t=PACK)[:, :, :, t0 : t0 + tn],
             )
 
         def quantize_w1(a, g, u0=0, un=2):
@@ -159,17 +167,16 @@ def tile_list_point_pair_max_kernel(
             )
 
         h = {}
-        h_place = {1: 2, 2: 8, 3: 24}
 
         def h_out(r, half, on_vector=False):
             if half == 0:
-                h[r] = placed([P, S], F32, "h_%d" % r, h_place[r]) if r in h_place else sb([P, S], F32, "h_%d" % r)
+                h[r] = sb([P, S], F32, "h_%d" % r)
             dst = h[r][:, half * BANK : (half + 1) * BANK]
-            bias = b1_lo[:, r // 2, r % 2 : r % 2 + 1] if r < PACK else b1_hi[:, r - PACK : r - PACK + 1]
+            column = bias[r] if r < PACK else b1_hi[:, r - PACK : r - PACK + 1]
             if on_vector:
-                nc.vector.tensor_scalar(dst, h_ps[r, half][:], bias, 0.0, ALU.add, ALU.max)
+                nc.vector.tensor_scalar(dst, h_ps[r, half][:], column, 0.0, ALU.add, ALU.max)
             else:
-                nc.scalar.activation(dst, h_ps[r, half][:], ACT.Relu, bias=bias)
+                nc.scalar.activation(dst, h_ps[r, half][:], ACT.Relu, bias=column)
 
         quarter_ps = {}
 
@@ -190,9 +197,9 @@ def tile_list_point_pair_max_kernel(
         def first_out(n):
             dst = h[0][:, n * 256 : (n + 1) * 256]
             if n % 2 == 0:
-                nc.vector.tensor_scalar(dst, quarter_ps[n][:, 0:256], b1_lo[:, 0, 0:1], 0.0, ALU.add, ALU.max)
+                nc.vector.tensor_scalar(dst, quarter_ps[n][:, 0:256], bias[0], 0.0, ALU.add, ALU.max)
             else:
-                nc.scalar.activation(dst, quarter_ps[n][:, 0:256], ACT.Relu, bias=b1_lo[:, 0, 0:1])
+                nc.scalar.activation(dst, quarter_ps[n][:, 0:256], ACT.Relu, bias=bias[0])
 
         def h_passes(r, first):
             for half in range(2):
@@ -208,22 +215,25 @@ def tile_list_point_pair_max_kernel(
         def late_slot(side, t):
             return late[side][:].rearrange("p (n t q) -> p t n q", n=2, t=PACK)[:, t, :, :]
 
-        early = {}
+        early, negated = {}, {}
+
+        def looked_up(r, side, q0, qn):
+            return h[r][:].indirect(pos_sb[side][:, q0 // LIST_ROWS : (q0 + qn) // LIST_ROWS])
+
+        def pick_first(r):
+            early[r] = sb([P, PAIRS], F32, "first_%d" % r)
+            nc.vector.tensor_copy(early[r][:], looked_up(r, 0, 0, PAIRS))
+
+        def pick_negated(r, dst, q0=0, qn=PAIRS):
+            nc.vector.tensor_tensor(dst[:], looked_up(r, 1, q0, qn), minus_one[:, 0:qn], ALU.mult)
+            for q in range(q0, q0 + qn, P):
+                negated[r, q // P] = dst[:, q - q0 : q - q0 + P]
 
         def pick(r, side, q0=0, qn=PAIRS):
-            if r < PACK:
-                name = "early_%d_%d" % (r, side)
-                early[r, side] = placed([P, PAIRS], F32, name, 6) if (r, side) == (0, 1) else sb([P, PAIRS], F32, name)
-                dst = early[r, side][:]
-            else:
-                dst = late_slot(side, r - PACK)
-                if qn < PAIRS:
-                    dst = dst[:, q0 // 256, q0 % 256 : q0 % 256 + qn]
-            looked_up = h[r][:].indirect(pos_sb[side][:, q0 // LIST_ROWS : (q0 + qn) // LIST_ROWS])
-            if r < PACK and side == 1:
-                nc.vector.tensor_tensor(dst, looked_up, minus_one[:], ALU.mult)
-            else:
-                nc.vector.tensor_copy(dst, looked_up)
+            dst = late_slot(side, r - PACK)
+            if qn < PAIRS:
+                dst = dst[:, q0 // 256, q0 % 256 : q0 % 256 + qn]
+            nc.vector.tensor_copy(dst, looked_up(r, side, q0, qn))
 
         turned = {}
         z_g, z_c, z_s = {}, {}, {}
@@ -238,9 +248,9 @@ def tile_list_point_pair_max_kernel(
             diff = bank(5 + 2 * (j % 2), "diff_ps_%d" % j)
             places = [slice((2 * (r % 2) + r // 2) * P, (2 * (r % 2) + r // 2 + 1) * P) for r in range(PACK)]
             for r in range(PACK):
-                nc.tensor.transpose(plain[:, places[r]], early[r, 0][:, cols], ident[:])
+                nc.tensor.transpose(plain[:, places[r]], early[r][:, cols], ident[:])
             for r in range(PACK):
-                turn_sum(diff[:, places[r]], early[r, 0][:, cols], early[r, 1][:, cols])
+                turn_sum(diff[:, places[r]], early[r][:, cols], negated[r, j])
             turned[j] = sb([P, 2, K_PASS], F32, "turned_%d" % j)
             nc.scalar.copy(
                 out=turned[j][:, 0, :].rearrange("p (e n) -> p e n", e=2),
@@ -286,7 +296,8 @@ def tile_list_point_pair_max_kernel(
         gather_words(0, 0, S)
         load_w1(1, NARROW, NARROW, 0)
         load_w1(0, NARROW, NARROW, 4)
-        load_w1(0, K_PASS, K_PASS, 8)
+        load_bias(1)
+        load_w1(0, K_PASS, K_PASS, 9)
         cast_narrow(0, 0)
         quantize_w1(0, 0)
         w2_s = placed([P, 2, N], U8, "w2_s", 44)
@@ -297,10 +308,12 @@ def tile_list_point_pair_max_kernel(
             h_pass(0, 1, half, True)
         gather_words(1, 0, BANK)
         gather_words(1, BANK, BANK)
-        b1_hi = placed([P, PACK], F32, "b1_hi", 20)
-        w2_w = placed([P, 2, 2 * N], U8, "w2_w", 16)
-        b2_sb = placed([P, N_TILES], F32, "b2_sb", 19)
-        load_w1(1, K_PASS, K_PASS, 24)
+        b1_hi = placed([P, PACK], F32, "b1_hi", 21)
+        w2_w = placed([P, 2, 2 * N], U8, "w2_w", 17)
+        b2_sb = placed([P, N_TILES], F32, "b2_sb", 20)
+        load_bias(2)
+        load_w1(1, K_PASS, K_PASS, 25)
+        load_bias(3)
         nc.sync.dma_start(out=b1_hi[:], in_=b1[K_PASS:].rearrange("(p t) -> p t", t=PACK))
         nc.sync.dma_start(out=w2_w[:].bitcast(I32), in_=w2_words.rearrange("b p n -> p b n").bitcast(I32))
         for q in range(4):
@@ -324,27 +337,29 @@ def tile_list_point_pair_max_kernel(
             first_out(n)
         cast_narrow(0, 1)
         quantize_w1(1, 1)
-        pick(0, 0)
+        pick_first(0)
         quantize_w1(0, 1)
         h_passes(2, 1)
         h_passes(3, 1)
-        h_out(1, 0, on_vector=True)
-        h_out(1, 1)
-        pick(0, 1)
-        for side in range(2):
-            pick(1, side)
-        cast_wide(0)
+        h_outs(1)
+        pick_negated(0, placed([P, PAIRS], F32, "negated_0", 6))
+        pick_first(1)
+        pick_negated(1, sb([P, PAIRS], F32, "negated_1"))
+        cast_wide(0, 0, PACK)
         quantize_w1(0, 2, 0, PACK)
         h_outs(2)
-        for side in range(2):
-            pick(2, side)
-        cast_wide(1)
-        quantize_w1(1, 2, 0, PACK)
+        pick_first(2)
+        pick_negated(2, sb([P, PAIRS], F32, "negated_2"))
+        cast_wide(1, 0, 2)
+        quantize_w1(1, 2, 0, 2)
         h_outs(3)
-        for side in range(2):
-            pick(3, side)
+        pick_first(3)
+        pick_negated(3, sb([P, 256], F32, "negated_3"), 0, 256)
         h_passes(4, 0)
         h_passes(5, 0)
+        cast_wide(1, 2, 2)
+        quantize_w1(1, 2, 2, 2)
+        pick_negated(3, placed([P, 256], F32, "negated_3_rest", 25), 256, 256)
         h_outs(4)
         h_passes(6, 0)
         for side in range(2):

@@ -119,27 +119,25 @@ def tile_list_point_pair_max_kernel(
 
         grouped, codes, planes = {}, {}, {}
 
-        def grouped_of(a, g):
-            if (a, g) not in grouped:
-                grouped[a, g] = sb([P, (2, 2, PACK)[g] * K_PASS], BF16, "w1_g_%d_%d" % (a, g))
-            return grouped[a, g][:]
-
         def cast_narrow(a, g):
-            dst = grouped_of(a, g).rearrange("p (u w e j) -> p w j e u", u=2, e=2, j=PACK)
-            src = raw[a, g * NARROW][:].rearrange("p j (w e u) -> p w j e u", e=2, u=2)
-            nc.scalar.copy(out=dst, in_=src)
-
-        def cast_wide(a, t0, tn):
+            grouped[a, g] = sb([P, 2 * K_PASS], BF16, "w1_g_%d_%d" % (a, g))
             nc.scalar.copy(
-                out=grouped_of(a, 2).rearrange("p (t m j) -> p m j t", t=PACK, j=PACK)[:, :, :, t0 : t0 + tn],
-                in_=raw[a, K_PASS][:].rearrange("p j (m t) -> p m j t", t=PACK)[:, :, :, t0 : t0 + tn],
+                out=grouped[a, g][:].rearrange("p (u w e j) -> p w j e u", u=2, e=2, j=PACK),
+                in_=raw[a, g * NARROW][:].rearrange("p j (w e u) -> p w j e u", e=2, u=2),
+            )
+
+        def cast_wide(a, g, dst):
+            grouped[a, g] = dst
+            t0 = 2 * (g - 2)
+            nc.scalar.copy(
+                out=dst[:].rearrange("p (t m j) -> p m j t", t=2, j=PACK),
+                in_=raw[a, K_PASS][:].rearrange("p j (m t) -> p m j t", t=PACK)[:, :, :, t0 : t0 + 2],
             )
 
         def quantize_w1(a, g, u0=0, un=2):
             if u0 == 0:
-                count = (2, 2, PACK)[g]
-                codes[a, g] = sb([P, count * P], U32, "w1_c_%d_%d" % (a, g))
-                planes[a, g] = sb([P, count * P], U8, "w1_s_%d_%d" % (a, g))
+                codes[a, g] = sb([P, 2 * P], U32, "w1_c_%d_%d" % (a, g))
+                planes[a, g] = sb([P, 2 * P], U8, "w1_s_%d_%d" % (a, g))
             cols = slice(u0 * P, (u0 + un) * P)
             nc.vector.quantize_mx(
                 out=codes[a, g][:, cols].bitcast(FP8X4),
@@ -153,7 +151,7 @@ def tile_list_point_pair_max_kernel(
         def h_pass(a, r, half, opens):
             if opens:
                 h_ps[r, half] = bank(first_bank[r] + half, "h_ps_%d_%d" % (r, half))
-            g = min(r // 2, 2)
+            g = r // 2
             m_cols = slice((r - 2 * g) * P, (r - 2 * g + 1) * P)
             j_cols = slice(half * BANK, (half + 1) * BANK)
             nc.tensor.matmul_mx(
@@ -345,21 +343,23 @@ def tile_list_point_pair_max_kernel(
         pick_negated(0, placed([P, PAIRS], F32, "negated_0", 6))
         pick_first(1)
         pick_negated(1, sb([P, PAIRS], F32, "negated_1"))
-        cast_wide(0, 0, PACK)
-        quantize_w1(0, 2, 0, PACK)
+        cast_wide(0, 2, sb([P, 2 * K_PASS], BF16, "w1_g_0_2"))
+        quantize_w1(0, 2)
         h_outs(2)
         pick_first(2)
         pick_negated(2, sb([P, PAIRS], F32, "negated_2"))
-        cast_wide(1, 0, 2)
-        quantize_w1(1, 2, 0, 2)
+        cast_wide(1, 2, sb([P, 2 * K_PASS], BF16, "w1_g_1_2"))
+        quantize_w1(1, 2)
         h_outs(3)
         pick_first(3)
         pick_negated(3, sb([P, 256], F32, "negated_3"), 0, 256)
         h_passes(4, 0)
         h_passes(5, 0)
-        cast_wide(1, 2, 2)
-        quantize_w1(1, 2, 2, 2)
-        pick_negated(3, placed([P, 256], F32, "negated_3_rest", 25), 256, 256)
+        cast_wide(1, 3, sb([P, 2 * K_PASS], BF16, "w1_g_1_3"))
+        quantize_w1(1, 3)
+        cast_wide(0, 3, placed([P, 2 * K_PASS], BF16, "w1_g_0_3", 23))
+        quantize_w1(0, 3)
+        pick_negated(3, placed([P, 256], F32, "negated_3_rest", 9), 256, 256)
         h_outs(4)
         h_passes(6, 0)
         for side in range(2):

@@ -24,8 +24,8 @@ BANK = 512
 LIST_ROWS = 16
 N_TILES = N // P
 QUAD = 32
-HALF = 64
-NARROW = 256
+QUARTER = 256
+SLOT = 256
 PARTS = {"A": (0, 256), "B": (256, 128), "C": (384, 128)}
 
 
@@ -39,11 +39,11 @@ def tile_list_point_pair_max_kernel(
         reused = ctx.enter_context(tc.tile_pool(name="reused", bufs=1))
         psum = ctx.enter_context(tc.psum_pool(name="psum", bufs=1))
 
-        def sb(shape, dtype, name, tag=""):
-            return keep.tile(shape, dtype, name=name, tag=tag or name, align_bytes=64)
+        def sb(shape, dtype, name):
+            return keep.tile(shape, dtype, name=name, tag=name, align_bytes=64)
 
         def placed(shape, dtype, name, kib):
-            return reused.tile(shape, dtype, name=name, tag=name, offset=kib * 1024, align_bytes=64)
+            return reused.tile(shape, dtype, name=name, tag=name, offset=int(kib * 1024), align_bytes=64)
 
         def bank(i, name):
             return psum.tile([P, BANK], F32, name=name, tag="bank%d" % i)
@@ -52,7 +52,7 @@ def tile_list_point_pair_max_kernel(
         pos_sb = [lists.tile([P, PAIRS // LIST_ROWS], U16, name="pos%d_sb" % i) for i in (1, 2)]
 
         tab_w = {}
-        tab_s = placed([P, T], U8, "tab_s", 31)
+        tab_s = placed([P, T], U8, "tab_s", 44.5)
         g_s = sb([P, S], U8, "g_s")
         v_s = sb([P, S], U8, "v_s")
 
@@ -61,17 +61,15 @@ def tile_list_point_pair_max_kernel(
         nc.vector.memset(tab_s[QUAD : 2 * QUAD, :].bitcast(I32), 0)
         nc.vector.memset(tab_s[2 * QUAD :, :].bitcast(I32), 0)
         nc.vector.memset(v_s[:].bitcast(I32), 0)
-        minus_one = sb([P, PAIRS], F32, "minus_one")
-        nc.vector.memset(minus_one[:], -1.0)
 
-        def move_scales(queue, a, q):
-            queue.dma_start(
+        def move_scales(a, q):
+            nc.sync.dma_start(
                 out=v_s[QUAD * q + 4 * a : QUAD * q + 4 * a + 4, :].bitcast(I32),
                 in_=g_s[16 * a + 4 * q : 16 * a + 4 * q + 4, :].bitcast(I32),
             )
 
         def load_table(a):
-            tab_w[a] = placed([P, T], I32, "tab_w%d" % a, 17 * a)
+            tab_w[a] = placed([P, T], I32, "tab_w%d" % a, 12 + 17 * a)
             nc.sync.dma_start(out=tab_w[a][:], in_=tab_words[a].rearrange("p t i -> p (t i)").bitcast(I32))
 
         raw = {}
@@ -81,6 +79,18 @@ def tile_list_point_pair_max_kernel(
             block = w1[a * K_PASS : (a + 1) * K_PASS, c0 : c0 + cn]
             nc.sync.dma_start(out=raw[a, c0][:], in_=block.rearrange("(p j) c -> p j c", j=PACK))
 
+        work = placed([P, 16 * SLOT], F32, "work", 60)
+
+        def slots(first, count):
+            return work[:, first * SLOT : (first + count) * SLOT]
+
+        bias = {}
+
+        def load_bias(r, column):
+            with nc.allow_non_contiguous_dma(reason="one bias value to a partition"):
+                nc.sync.dma_start(out=column, in_=b1[r * P : (r + 1) * P].rearrange("(p o) -> p o", o=1))
+            bias[r] = column
+
         nc.sync.dma_start(
             out=tab_s[0:QUAD, :].bitcast(I32), in_=tab_scales.rearrange("a q t -> (a q) t").bitcast(I32)
         )
@@ -88,230 +98,261 @@ def tile_list_point_pair_max_kernel(
         nc.sync.dma_start(pos_sb[0][:], pos1)
         nc.sync.dma_start(pos_sb[1][:], pos2)
         load_table(0)
-        load_w1(0, 0, NARROW, 44)
+        load_w1(0, 0, 2 * P, 82)
 
         nc.vector.tensor_copy(g_s[:], tab_s[:].indirect(offs_sb[:]))
         moves = [(a, q) for a in range(2) for q in range(4)]
         for a, q in moves[:5]:
-            move_scales(nc.sync, a, q)
+            move_scales(a, q)
         load_table(1)
         for a, q in moves[5:]:
-            move_scales(nc.sync, a, q)
-        load_w1(1, 0, NARROW, 34)
-        b1_pairs = b1[0:K_PASS].rearrange("(g m u) -> g m u", g=2, u=2)
-        bias = {}
+            move_scales(a, q)
+        load_w1(1, 0, P, 45.5)
+        load_bias(0, placed([P, 1], F32, "b1_0", 45)[:])
+        load_w1(1, P, P, 48)
 
-        def load_bias(r):
-            column = placed([P, 1], F32, "b1_%d" % r, (33, 8, 22, 23)[r])
-            with nc.allow_non_contiguous_dma(reason="one bias value to a partition"):
-                nc.sync.dma_start(out=column[:], in_=b1_pairs[r // 2][:, r % 2 : r % 2 + 1])
-            bias[r] = column[:]
+        v_w0 = sb([P, S], U32, "v_w0")
+        v_w1 = {}
 
-        load_bias(0)
-
-        v_w = [sb([P, S], U32, "v_w%d" % a) for a in range(2)]
-
-        def gather_words(a, j0, jn):
+        def gather_words(a, dst, j0, jn):
             nc.vector.tensor_copy(
-                v_w[a][:, j0 : j0 + jn],
-                tab_w[a][:].bitcast(U32).indirect(offs_sb[:, j0 // LIST_ROWS : (j0 + jn) // LIST_ROWS]),
+                dst, tab_w[a][:].bitcast(U32).indirect(offs_sb[:, j0 // LIST_ROWS : (j0 + jn) // LIST_ROWS])
             )
 
-        grouped, codes, planes = {}, {}, {}
+        def v_words(a, j0, jn):
+            if a == 0:
+                return v_w0[:, j0 : j0 + jn]
+            if j0 < 3 * QUARTER:
+                return v_w1[0][:, j0 : j0 + jn]
+            return v_w1[1][:, j0 - 3 * QUARTER : j0 - 3 * QUARTER + jn]
 
-        def cast_narrow(a, g):
-            grouped[a, g] = sb([P, 2 * K_PASS], BF16, "w1_g_%d_%d" % (a, g))
+        rounded, codes, planes = {}, {}, {}
+
+        def cast_plain(a, r, c0, dst):
+            rounded[r, a] = dst
+            m0 = r * P - c0
             nc.scalar.copy(
-                out=grouped[a, g][:].rearrange("p (u w e j) -> p w j e u", u=2, e=2, j=PACK),
-                in_=raw[a, g * NARROW][:].rearrange("p j (w e u) -> p w j e u", e=2, u=2),
+                out=dst.rearrange("p (c i j) -> p c j i", i=4, j=PACK),
+                in_=raw[a, c0][:, :, m0 : m0 + P].rearrange("p j (c i) -> p c j i", i=4),
             )
 
-        def cast_wide(a, g, dst):
-            grouped[a, g] = dst
-            t0 = 2 * (g - 2)
-            nc.scalar.copy(
-                out=dst[:].rearrange("p (t m j) -> p m j t", t=2, j=PACK),
-                in_=raw[a, K_PASS][:].rearrange("p j (m t) -> p m j t", t=PACK)[:, :, :, t0 : t0 + 2],
+        def by_tile(first_slot):
+            view = work[:].bitcast(BF16).rearrange("p (s x) -> p s x", x=K_PASS)
+            return view[:, first_slot : first_slot + 3 : 2, :]
+
+        def cast_pair(a, first_slot):
+            nc.gpsimd.tensor_scalar(
+                by_tile(first_slot).rearrange("p u (m j) -> p u m j", j=PACK),
+                raw[a, 2 * P][:].rearrange("p j (u m) -> p u m j", u=2),
+                1.0,
+                0.0,
+                ALU.mult,
+                ALU.add,
             )
 
-        def quantize_w1(a, g, u0=0, un=2):
-            if u0 == 0:
-                codes[a, g] = sb([P, 2 * P], U32, "w1_c_%d_%d" % (a, g))
-                planes[a, g] = sb([P, 2 * P], U8, "w1_s_%d_%d" % (a, g))
-            cols = slice(u0 * P, (u0 + un) * P)
-            nc.vector.quantize_mx(
-                out=codes[a, g][:, cols].bitcast(FP8X4),
-                scales=planes[a, g][:, cols],
-                in_=grouped[a, g][:, u0 * K_PASS : (u0 + un) * K_PASS],
+        def cast_dealt(a, r0, first_slot, on_gpsimd):
+            dst = by_tile(first_slot).rearrange("p t (m j) -> p m j t", j=PACK)
+            t0 = r0 - PACK
+            src = raw[a, K_PASS][:].rearrange("p j (m t) -> p m j t", t=PACK)[:, :, :, t0 : t0 + 2]
+            if on_gpsimd:
+                nc.gpsimd.tensor_scalar(
+                    dst.rearrange("p m j t -> p t m j"), src.rearrange("p m j t -> p t m j"), 1.0, 0.0, ALU.mult, ALU.add
+                )
+            else:
+                nc.scalar.copy(out=dst, in_=src)
+
+        def quantize_w1(operands, src):
+            n = len(operands) * P
+            c = sb([P, n], U32, "w1_c_%d_%d" % operands[0])
+            s = sb([P, n], U8, "w1_s_%d_%d" % operands[0])
+            nc.vector.quantize_mx(out=c[:].bitcast(FP8X4), scales=s[:], in_=src)
+            for i, key in enumerate(operands):
+                codes[key] = c[:, i * P : (i + 1) * P]
+                planes[key] = s[:, i * P : (i + 1) * P]
+
+        def quantize_slots(tiles, passes, first_slot):
+            operands = [(r, a) for a in passes for r in tiles]
+            quantize_w1(operands, slots(first_slot, len(operands)).bitcast(BF16))
+
+        def mx_pass(dst, r, a, j0, jn, start, stop):
+            nc.tensor.matmul_mx(
+                out=dst,
+                lhsT=codes[r, a].bitcast(FP8X4),
+                lhsT_scale=planes[r, a],
+                rhs=v_words(a, j0, jn).bitcast(FP8X4),
+                rhs_scale=v_s[4 * a :, j0 : j0 + jn],
+                start=start,
+                stop=stop,
             )
 
         h_ps = {}
-        first_bank = [0, 2, 4, 6, 0, 2, 0, 2]
+        first_bank = [0, 2, 4, 6, 2, 0, 0, 2]
 
-        def h_pass(a, r, half, opens):
-            if opens:
-                h_ps[r, half] = bank(first_bank[r] + half, "h_ps_%d_%d" % (r, half))
-            g = r // 2
-            m_cols = slice((r - 2 * g) * P, (r - 2 * g + 1) * P)
-            j_cols = slice(half * BANK, (half + 1) * BANK)
-            nc.tensor.matmul_mx(
-                out=h_ps[r, half][:],
-                lhsT=codes[a, g][:, m_cols].bitcast(FP8X4),
-                lhsT_scale=planes[a, g][:, m_cols],
-                rhs=v_w[a][:, j_cols].bitcast(FP8X4),
-                rhs_scale=v_s[4 * a :, j_cols],
-                start=opens,
-                stop=not opens,
-            )
+        def open_half(r, half):
+            h_ps[r, half] = bank(first_bank[r] + half, "h_ps_%d_%d" % (r, half))
+            mx_pass(h_ps[r, half][:], r, 0, half * BANK, BANK, True, False)
+
+        def close_half(r, half):
+            if half == 0:
+                mx_pass(h_ps[r, 0][:], r, 1, 0, BANK, False, True)
+            else:
+                mx_pass(h_ps[r, 1][:, 0:QUARTER], r, 1, 2 * QUARTER, QUARTER, False, False)
+                mx_pass(h_ps[r, 1][:, QUARTER:], r, 1, 3 * QUARTER, QUARTER, False, True)
+
+        def h_passes(r):
+            for half in range(2):
+                open_half(r, half)
+                close_half(r, half)
 
         h = {}
 
-        def h_out(r, half, on_vector=False):
-            if half == 0:
-                h[r] = sb([P, S], F32, "h_%d" % r)
-            dst = h[r][:, half * BANK : (half + 1) * BANK]
+        def h_outs(r):
+            h[r] = sb([P, S], F32, "h_%d" % r)
             column = bias[r] if r < PACK else b1_hi[:, r - PACK : r - PACK + 1]
-            if on_vector:
-                nc.vector.tensor_scalar(dst, h_ps[r, half][:], column, 0.0, ALU.add, ALU.max)
-            else:
-                nc.scalar.activation(dst, h_ps[r, half][:], ACT.Relu, bias=column)
+            for half in range(2):
+                nc.scalar.activation(
+                    h[r][:, half * BANK : (half + 1) * BANK], h_ps[r, half][:], ACT.Relu, bias=column
+                )
 
         quarter_ps = {}
 
         def first_pass(a, n):
             if a == 0:
                 quarter_ps[n] = bank((0, 1, 4, 5)[n], "h_ps_0_%d" % n)
-            j_cols = slice(n * 256, (n + 1) * 256)
-            nc.tensor.matmul_mx(
-                out=quarter_ps[n][:, 0:256],
-                lhsT=codes[a, 0][:, 0:P].bitcast(FP8X4),
-                lhsT_scale=planes[a, 0][:, 0:P],
-                rhs=v_w[a][:, j_cols].bitcast(FP8X4),
-                rhs_scale=v_s[4 * a :, j_cols],
-                start=(a == 0),
-                stop=(a == 1),
-            )
+            mx_pass(quarter_ps[n][:, 0:QUARTER], 0, a, n * QUARTER, QUARTER, a == 0, a == 1)
 
         def first_out(n):
-            dst = h[0][:, n * 256 : (n + 1) * 256]
-            if n % 2 == 0:
-                nc.vector.tensor_scalar(dst, quarter_ps[n][:, 0:256], bias[0], 0.0, ALU.add, ALU.max)
+            dst = h[0][:, n * QUARTER : (n + 1) * QUARTER]
+            if n == 1:
+                nc.vector.tensor_scalar(dst, quarter_ps[n][:, 0:QUARTER], bias[0], 0.0, ALU.add, ALU.max)
             else:
-                nc.scalar.activation(dst, quarter_ps[n][:, 0:256], ACT.Relu, bias=bias[0])
-
-        def h_passes(r, first):
-            for half in range(2):
-                h_pass(first, r, half, True)
-                h_pass(1 - first, r, half, False)
-
-        def h_outs(r):
-            for half in range(2):
-                h_out(r, half)
-
-        late = [sb([P, PACK * PAIRS], F32, "late_%d" % side) for side in range(2)]
-
-        def late_slot(side, t):
-            return late[side][:].rearrange("p (n t q) -> p t n q", n=2, t=PACK)[:, t, :, :]
-
-        early, negated = {}, {}
+                nc.scalar.activation(dst, quarter_ps[n][:, 0:QUARTER], ACT.Relu, bias=bias[0])
 
         def looked_up(r, side, q0, qn):
             return h[r][:].indirect(pos_sb[side][:, q0 // LIST_ROWS : (q0 + qn) // LIST_ROWS])
 
-        def pick_first(r):
-            early[r] = sb([P, PAIRS], F32, "first_%d" % r)
-            nc.vector.tensor_copy(early[r][:], looked_up(r, 0, 0, PAIRS))
+        early = {}
 
-        def pick_negated(r, dst, q0=0, qn=PAIRS):
-            nc.vector.tensor_tensor(dst[:], looked_up(r, 1, q0, qn), minus_one[:, 0:qn], ALU.mult)
-            for q in range(q0, q0 + qn, P):
-                negated[r, q // P] = dst[:, q - q0 : q - q0 + P]
+        def pick_early(r, side, dst=None):
+            early[r, side] = dst if dst is not None else sb([P, PAIRS], F32, "early_%d_%d" % (r, side))[:]
+            nc.vector.tensor_copy(early[r, side], looked_up(r, side, 0, PAIRS))
 
-        def pick(r, side, q0=0, qn=PAIRS):
-            dst = late_slot(side, r - PACK)
-            if qn < PAIRS:
-                dst = dst[:, q0 // 256, q0 % 256 : q0 % 256 + qn]
-            nc.vector.tensor_copy(dst, looked_up(r, side, q0, qn))
+        excess = {}
+
+        def subtract(dst, first, second):
+            nc.gpsimd.tensor_tensor(dst, first, second, ALU.subtract)
+
+        def clip(dst, src):
+            nc.scalar.activation(dst, src, ACT.Relu)
+
+        turned_ps = {}
+
+        def turn(r, j, src, start=False, stop=False):
+            if start:
+                turned_ps[j] = bank(4 + j, "turned_ps_%d" % j)
+            dst = turned_ps[j][:, r * P : (r + 1) * P]
+            nc.tensor.matmul(dst, lhsT=src, rhs=ident[:], is_transpose=True, start=start, stop=stop)
+
+        def turn_second(r):
+            for j in range(PACK):
+                turn(r, j, early[r, 1][:, j * P : (j + 1) * P], start=(r == 0))
+
+        def turn_excess(r, j, stop=False):
+            turn(r, j, excess[r, j // 2][:, j % 2 * P : (j % 2 + 1) * P], stop=stop)
 
         turned = {}
-        z_g, z_c, z_s = {}, {}, {}
 
-        def turn_sum(dst, x, y):
-            nc.tensor.matmul(dst, lhsT=x, rhs=ident[:], is_transpose=True, start=True, stop=False)
-            nc.tensor.matmul(dst, lhsT=y, rhs=ident[:], is_transpose=True, start=False, stop=True)
-
-        def turn_early(j):
-            cols = slice(j * P, (j + 1) * P)
-            plain = bank(4 + 2 * (j % 2), "first_ps_%d" % j)
-            diff = bank(5 + 2 * (j % 2), "diff_ps_%d" % j)
-            places = [slice((2 * (r % 2) + r // 2) * P, (2 * (r % 2) + r // 2 + 1) * P) for r in range(PACK)]
-            for r in range(PACK):
-                nc.tensor.transpose(plain[:, places[r]], early[r][:, cols], ident[:])
-            for r in range(PACK):
-                turn_sum(diff[:, places[r]], early[r][:, cols], negated[r, j])
-            turned[j] = sb([P, 2, K_PASS], F32, "turned_%d" % j)
+        def round_turned(j):
+            turned[j] = sb([P, 2 * P], F32, "turned_%d" % j)
             nc.scalar.copy(
-                out=turned[j][:, 0, :].rearrange("p (e n) -> p e n", e=2),
-                in_=plain[:].rearrange("p (n e) -> p e n", e=2),
-            )
-            nc.scalar.activation(
-                turned[j][:, 1, :].rearrange("p (e n) -> p e n", e=2),
-                diff[:].rearrange("p (n e) -> p e n", e=2),
-                ACT.Relu,
-                scale=-1.0,
+                out=turned[j][:].bitcast(BF16).rearrange("q (e p i) -> q e p i", e=2, i=2),
+                in_=turned_ps[j][:].rearrange("q (p e i) -> q e p i", e=2, i=2),
             )
 
-        def turn_back(j, rounded):
-            ps = bank(j, "back_%d" % j)
-            for t in range(PACK):
-                cols = slice(t * P, (t + 1) * P)
-                turn_sum(ps[:, cols], turned[j][:, 0, cols], turned[j][:, 1, cols])
-            nc.scalar.copy(
-                out=rounded.rearrange("p (q t) -> p q t", t=PACK), in_=ps[:].rearrange("p (t q) -> p q t", t=PACK)
-            )
+        def turn_back(j0, bank_no, pieces):
+            ps = bank(bank_no, "back_%d" % j0)
+            for jj in range(2):
+                for e in range(2):
+                    place = (2 * jj + e) * P
+                    nc.tensor.transpose(ps[:, place : place + P], turned[j0 + jj][:, e * P : (e + 1) * P], ident[:])
+            n = 2 // len(pieces)
+            for i, words in enumerate(pieces):
+                nc.scalar.copy(
+                    out=words.rearrange("p (n q e) -> p n q e", n=n, e=2),
+                    in_=ps[:, i * n * 256 : (i + 1) * n * 256].rearrange("p (n e q) -> p n q e", n=n, e=2),
+                )
+
+        late = placed([P, 17 * 256], F32, "late", 43)
+        late_at = {(1, 0): (0, 1), (1, 1): (5, 2), (0, 0): (9, 2), (0, 1): (10, 2)}
+        late_view = late[:].rearrange("p (s q) -> p s q", q=256)
+
+        def late_places(first, count):
+            return late[:, first * 256 : (first + count) * 256]
+
+        def pick_late(r, side, q0=0, qn=PAIRS):
+            at = [late_at[side, n][0] + late_at[side, n][1] * (r - PACK) for n in range(2)]
+            if qn == PAIRS:
+                dst = late_view[:, at[0] : at[1] + 1 : at[1] - at[0], :]
+            else:
+                dst = late_places(at[q0 // 256], 1)[:, q0 % 256 : q0 % 256 + qn]
+            nc.vector.tensor_copy(dst, looked_up(r, side, q0, qn))
+
+        z_c, z_s = {}, {}
 
         def late_max(part, words):
             q0, qn = PARTS[part]
-            z_g[1, part] = words.bitcast(BF16)
-            sides = [
-                late[side][:].rearrange("p (n t c i) -> p n c t i", n=2, t=PACK, i=4)[:, q0 // 256, :, :, :]
-                for side in range(2)
-            ]
-            c0 = q0 % 256 // 4
+            sides = []
+            for side in range(2):
+                first, step = late_at[side, q0 // 256]
+                tiles = late_view[:, first : first + 3 * step + 1 : step, q0 % 256 : q0 % 256 + qn]
+                sides.append(tiles.rearrange("p t (c i) -> p c t i", i=4))
             nc.vector.tensor_tensor(
-                z_g[1, part].rearrange("p (c i t) -> p c t i", i=4, t=PACK),
-                sides[0][:, c0 : c0 + qn // 4, :, :],
-                sides[1][:, c0 : c0 + qn // 4, :, :],
-                ALU.max,
+                words.bitcast(BF16).rearrange("p (c i t) -> p c t i", i=4, t=PACK), sides[0], sides[1], ALU.max
             )
 
-        def quantize_z(b, part):
-            qn = PARTS[part][1]
-            z_c[b, part] = sb([P, qn], U32, "z_c_%d_%s" % (b, part))
-            z_s[b, part] = sb([P, qn], U8, "z_s_%d_%s" % (b, part))
-            nc.vector.quantize_mx(out=z_c[b, part][:].bitcast(FP8X4), scales=z_s[b, part][:], in_=z_g[b, part])
+        def quantize_z(b, parts, pieces, kib=None):
+            qn = sum(PARTS[part][1] for part in parts)
+            name = "z_c_%d_%s" % (b, parts)
+            c = sb([P, qn], U32, name) if kib is None else placed([P, qn], U32, name, kib)
+            s = sb([P, qn], U8, "z_s_%d_%s" % (b, parts))
+            n = qn // len(pieces)
+            for i, words in enumerate(pieces):
+                cols = slice(i * n, (i + 1) * n)
+                nc.vector.quantize_mx(out=c[:, cols].bitcast(FP8X4), scales=s[:, cols], in_=words.bitcast(BF16))
+            for part in parts:
+                q0 = PARTS[part][0] - PARTS[parts[0]][0]
+                z_c[b, part] = c[:, q0 : q0 + PARTS[part][1]]
+                z_s[b, part] = s[:, q0 : q0 + PARTS[part][1]]
 
-        gather_words(0, 0, S)
-        load_w1(1, NARROW, NARROW, 0)
-        load_w1(0, NARROW, NARROW, 4)
-        load_bias(1)
-        load_w1(0, K_PASS, K_PASS, 9)
-        cast_narrow(0, 0)
-        quantize_w1(0, 0)
-        w2_s = placed([P, 2, N], U8, "w2_s", 44)
+        gather_words(0, v_w0[:], 0, S)
+        load_w1(1, 2 * P, 2 * P, 12.5)
+        load_w1(0, 2 * P, 2 * P, 16.5)
+        load_bias(1, placed([P, 1], F32, "b1_1", 20.5)[:])
+        load_w1(0, K_PASS, K_PASS, 21)
+        for r in range(2):
+            cast_plain(0, r, 0, sb([P, K_PASS], BF16, "w1_r_%d_0" % r)[:])
+            quantize_w1([(r, 0)], rounded[r, 0])
+        w2_s = placed([P, 2, N], U8, "w2_s", 82)
         nc.vector.memset(w2_s[:].rearrange("p b n -> p (b n)").bitcast(I32), 0)
         for n in range(PACK):
             first_pass(0, n)
         for half in range(2):
-            h_pass(0, 1, half, True)
-        gather_words(1, 0, BANK)
-        gather_words(1, BANK, BANK)
-        b1_hi = placed([P, PACK], F32, "b1_hi", 21)
-        w2_w = placed([P, 2, 2 * N], U8, "w2_w", 17)
-        b2_sb = placed([P, N_TILES], F32, "b2_sb", 20)
-        load_bias(2)
-        load_w1(1, K_PASS, K_PASS, 25)
-        load_bias(3)
+            open_half(1, half)
+        v_w1[0] = sb([P, 3 * QUARTER], U32, "v_w1_0")
+        gather_words(1, v_w1[0][:], 0, 3 * QUARTER)
+        cast_plain(1, 0, 0, placed([P, K_PASS], BF16, "w1_r_0_1", 80)[:])
+        quantize_w1([(0, 1)], rounded[0, 1])
+        v_w1[1] = placed([P, QUARTER], U32, "v_w1_1", 80)
+        gather_words(1, v_w1[1][:], 3 * QUARTER, QUARTER)
+        cast_plain(1, 1, P, sb([P, K_PASS], BF16, "w1_r_1_1")[:])
+        quantize_w1([(1, 1)], rounded[1, 1])
+
+        b1_hi = placed([P, PACK], F32, "b1_hi", 32.5)
+        w2_w = placed([P, 2, 2 * N], U8, "w2_w", 29)
+        b2_sb = placed([P, N_TILES], F32, "b2_sb", 32.25)
+        load_bias(2, placed([P, 1], F32, "b1_2", 32.75)[:])
+        load_w1(1, K_PASS, K_PASS, 36)
+        load_bias(3, placed([P, 1], F32, "b1_3", 33.5)[:])
         nc.sync.dma_start(out=b1_hi[:], in_=b1[K_PASS:].rearrange("(p t) -> p t", t=PACK))
         nc.sync.dma_start(out=w2_w[:].bitcast(I32), in_=w2_words.rearrange("b p n -> p b n").bitcast(I32))
         for q in range(4):
@@ -322,76 +363,97 @@ def tile_list_point_pair_max_kernel(
         with nc.allow_non_contiguous_dma(reason="one bias value to a partition"):
             nc.sync.dma_start(out=b2_sb[:], in_=b2.rearrange("(c p) -> p c", p=P))
 
-        cast_narrow(1, 0)
-        quantize_w1(1, 0, 0, 1)
-        quantize_w1(1, 0, 1, 1)
         for n in range(PACK):
             first_pass(1, n)
         for half in range(2):
-            h_pass(1, 1, half, False)
-        cast_narrow(1, 1)
+            close_half(1, half)
         h[0] = sb([P, S], F32, "h_0")
         for n in range(PACK):
             first_out(n)
-        cast_narrow(0, 1)
-        quantize_w1(1, 1)
-        pick_first(0)
-        quantize_w1(0, 1)
-        h_passes(2, 1)
-        h_passes(3, 1)
-        h_outs(1)
-        pick_negated(0, placed([P, PAIRS], F32, "negated_0", 6))
-        pick_first(1)
-        pick_negated(1, sb([P, PAIRS], F32, "negated_1"))
-        cast_wide(0, 2, sb([P, 2 * K_PASS], BF16, "w1_g_0_2"))
-        quantize_w1(0, 2)
-        h_outs(2)
-        pick_first(2)
-        pick_negated(2, sb([P, PAIRS], F32, "negated_2"))
-        cast_wide(1, 2, sb([P, 2 * K_PASS], BF16, "w1_g_1_2"))
-        quantize_w1(1, 2)
-        h_outs(3)
-        pick_first(3)
-        pick_negated(3, sb([P, 256], F32, "negated_3"), 0, 256)
-        h_passes(4, 0)
-        h_passes(5, 0)
-        cast_wide(1, 3, sb([P, 2 * K_PASS], BF16, "w1_g_1_3"))
-        quantize_w1(1, 3)
-        cast_wide(0, 3, placed([P, 2 * K_PASS], BF16, "w1_g_0_3", 23))
-        quantize_w1(0, 3)
-        pick_negated(3, placed([P, 256], F32, "negated_3_rest", 9), 256, 256)
-        h_outs(4)
-        h_passes(6, 0)
-        for side in range(2):
-            pick(4, side)
-        h_outs(5)
-        h_passes(7, 0)
-        for side in range(2):
-            pick(5, side)
-        h_outs(6)
-        h_outs(7)
-        spare = {name: sb([P, 2 * P], F32, "z_words_" + name) for name in ("0B", "0C", "1B", "1C")}
-        z_g[0, "A"] = late[1][:, 3 * PAIRS :].bitcast(BF16)
-        z_g[0, "B"] = spare["0B"][:].bitcast(BF16)
-        z_g[0, "C"] = spare["0C"][:].bitcast(BF16)
-        turn_early(0)
-        turn_early(1)
-        turn_back(0, z_g[0, "A"][:, 0:K_PASS])
-        turn_early(2)
-        turn_back(1, z_g[0, "A"][:, K_PASS:])
-        turn_early(3)
 
-        banks_of = {"A": (4, 4, 5, 5, 6, 6), "B": (7, 7, 7, 0, 0, 0), "C": (1, 1, 1, 2, 2, 3)}
+        cast_pair(1, 3)
+        cast_pair(0, 4)
+        h_outs(1)
+        pick_early(0, 0)
+        pick_early(0, 1)
+        quantize_slots([2], (1, 0), 3)
+        quantize_slots([3], (1, 0), 5)
+        h_passes(2)
+        h_passes(3)
+        turn_second(0)
+        cast_dealt(0, 6, 6, True)
+        subtract(slots(4, 2), early[0, 0], early[0, 1])
+        cast_dealt(0, 4, 9, False)
+        h_outs(2)
+        pick_early(1, 0, slots(2, 2))
+        pick_early(1, 1)
+        turn_second(1)
+        cast_dealt(1, 4, 10, False)
+        h_outs(3)
+        first_excess = placed([P, PAIRS], F32, "first_excess", 33.5)
+        clip(first_excess[:], slots(4, 2))
+        pick_early(2, 0, slots(14, 2))
+        quantize_slots([5], (0, 1), 11)
+        quantize_slots([4], (0, 1), 9)
+        h_passes(5)
+        h_passes(4)
+        cast_dealt(1, 6, 7, True)
+        pick_early(2, 1, slots(12, 2))
+        for n in range(2):
+            excess[0, n] = first_excess[:, n * 256 : (n + 1) * 256]
+        for j in range(PACK):
+            turn_excess(0, j)
+        turn_second(2)
+        pick_early(3, 0, slots(10, 2))
+        quantize_slots([6], (0, 1), 6)
+        quantize_slots([7], (0, 1), 8)
+        pick_early(3, 1, slots(6, 2))
+        h_outs(5)
+        h_passes(6)
+        h_outs(4)
+        h_passes(7)
+        turn_second(3)
+        for n in range(2):
+            for r in (1, 2, 3):
+                cols = slice(n * 256, (n + 1) * 256)
+                excess[r, n] = slots(((8, 9, 10), (2, 14, 11))[n][r - 1], 1)
+                subtract(excess[r, n], early[r, 0][:, cols], early[r, 1][:, cols])
+
+        def close_turns(n):
+            for x in [slots(8, 3)] if n == 0 else [excess[r, 1] for r in (1, 2, 3)]:
+                clip(x, x)
+            for j in (2 * n, 2 * n + 1):
+                for r in (1, 2, 3):
+                    turn_excess(r, j, stop=(r == 3))
+
+        for side in range(2):
+            pick_late(5, side)
+        h_outs(6)
+        close_turns(0)
+        for j in range(2):
+            round_turned(j)
+        h_outs(7)
+        close_turns(1)
+        first_words = placed([P, PAIRS], F32, "first_words", 76)
+        turn_back(0, 0, [first_words[:, 0:256], late_places(16, 1)])
+        for side in range(2):
+            pick_late(4, side)
+        for j in range(2, PACK):
+            round_turned(j)
+        rest_words = sb([P, PAIRS], F32, "rest_words")
+        turn_back(2, 2, [rest_words[:]])
+
+        banks_of = {"A": (4, 4, 5, 5, 1, 1), "B": (6, 6, 6, 7, 7, 7), "C": (3, 3, 3, 0, 0, 2)}
         o_bank, o_ps, staged = {}, {}, {}
         out_v = out.rearrange("(c p) q -> p c q", p=P)
 
-        def out_passes(b, part, opens):
+        def out_passes(b, part):
             qn = PARTS[part][1]
             mine = banks_of[part]
             for c in range(N_TILES):
                 first = mine.index(mine[c])
                 last = first + len([i for i in mine if i == mine[c]]) - 1
-                if opens:
+                if b == 0:
                     if c == first:
                         o_bank[mine[c]] = bank(mine[c], "o_%s_%d" % (part, c))
                     o_ps[part, c] = o_bank[mine[c]][:, (c - first) * qn : (c - first + 1) * qn]
@@ -399,10 +461,10 @@ def tile_list_point_pair_max_kernel(
                     out=o_ps[part, c],
                     lhsT=w2_w[:, b, 2 * P * c : 2 * P * (c + 1)].bitcast(FP4X4),
                     lhsT_scale=w2_s[:, b, P * c : P * (c + 1)],
-                    rhs=z_c[b, part][:].bitcast(FP8X4),
-                    rhs_scale=z_s[b, part][:],
-                    start=(opens and c == first),
-                    stop=(not opens and c == last),
+                    rhs=z_c[b, part].bitcast(FP8X4),
+                    rhs_scale=z_s[b, part],
+                    start=(b == 0 and c == first),
+                    stop=(b == 1 and c == last),
                 )
 
         def finish(part, on_vector=()):
@@ -420,33 +482,30 @@ def tile_list_point_pair_max_kernel(
                         out=out_v[:, first : c + 1, q0 : q0 + qn], in_=staged[part][:, first : c + 1, :]
                     )
 
-        for side in range(2):
-            pick(6, side, *PARTS["A"])
-        pick(6, 0, 256, 256)
-        for side in range(2):
-            pick(7, side, *PARTS["A"])
-        pick(7, 0, 256, 256)
-        quantize_z(0, "A")
-        out_passes(0, "A", True)
-        turn_back(2, z_g[0, "B"])
-        late_max("A", late[1][:, 3 * PAIRS :])
-        quantize_z(0, "B")
-        quantize_z(1, "A")
-        out_passes(1, "A", False)
-        turn_back(3, z_g[0, "C"])
+        spare = {part: sb([P, 2 * PARTS[part][1]], F32, "z_words_" + part) for part in "BC"}
+        pick_late(6, 1, *PARTS["A"])
+        pick_late(6, 0)
+        pick_late(7, 1, *PARTS["A"])
+        pick_late(7, 0, *PARTS["A"])
+        quantize_z(0, "A", [first_words[:, 0:256], late_places(16, 1)])
+        out_passes(0, "A")
+        late_max("A", first_words[:])
+        pick_late(7, 0, 256, 256)
+        quantize_z(1, "A", [first_words[:]])
+        out_passes(1, "A")
         finish("A")
-        out_passes(0, "B", True)
-        pick(6, 1, *PARTS["B"])
-        pick(7, 1, *PARTS["B"])
-        pick(6, 1, *PARTS["C"])
-        quantize_z(0, "C")
-        out_passes(0, "C", True)
-        late_max("B", spare["1B"][:])
-        pick(7, 1, *PARTS["C"])
-        quantize_z(1, "B")
-        out_passes(1, "B", False)
+        pick_late(6, 1, *PARTS["B"])
+        quantize_z(0, "BC", [rest_words[:]], 76)
+        out_passes(0, "B")
+        pick_late(7, 1, *PARTS["B"])
+        pick_late(6, 1, *PARTS["C"])
+        out_passes(0, "C")
+        late_max("B", spare["B"][:])
+        pick_late(7, 1, *PARTS["C"])
+        quantize_z(1, "B", [spare["B"][:]])
+        out_passes(1, "B")
         finish("B")
-        late_max("C", spare["1C"][:])
-        quantize_z(1, "C")
-        out_passes(1, "C", False)
+        late_max("C", spare["C"][:])
+        quantize_z(1, "C", [spare["C"][:]])
+        out_passes(1, "C")
         finish("C", on_vector=(0, 1, 2, 5))

@@ -54,17 +54,18 @@ def tile_list_point_pair_max_kernel(
         tab_w = {}
         tab_s = placed([P, T], U8, "tab_s", 44.5)
         g_s = sb([P, S], U8, "g_s")
-        v_s = sb([P, S], U8, "v_s")
+        v_s = [sb([P, S], U8, "v_s%d" % a) for a in range(2)]
 
         ident = sb([P, P], F32, "ident")
         make_identity(nc, ident[:])
         nc.vector.memset(tab_s[QUAD : 2 * QUAD, :].bitcast(I32), 0)
         nc.vector.memset(tab_s[2 * QUAD :, :].bitcast(I32), 0)
-        nc.vector.memset(v_s[:].bitcast(I32), 0)
+        for a in range(2):
+            nc.vector.memset(v_s[a][:].bitcast(I32), 0)
 
         def move_scales(a, q):
             nc.sync.dma_start(
-                out=v_s[QUAD * q + 4 * a : QUAD * q + 4 * a + 4, :].bitcast(I32),
+                out=v_s[a][QUAD * q : QUAD * q + 4, :].bitcast(I32),
                 in_=g_s[16 * a + 4 * q : 16 * a + 4 * q + 4, :].bitcast(I32),
             )
 
@@ -180,7 +181,7 @@ def tile_list_point_pair_max_kernel(
                 lhsT=codes[r, a].bitcast(FP8X4),
                 lhsT_scale=planes[r, a],
                 rhs=v_words(a, j0, jn).bitcast(FP8X4),
-                rhs_scale=v_s[4 * a :, j0 : j0 + jn],
+                rhs_scale=v_s[a][:, j0 : j0 + jn],
                 start=start,
                 stop=stop,
             )

@@ -26,6 +26,7 @@ N_TILES = N // P
 QUAD = 32
 QUARTER = 256
 SLOT = 256
+F32_MAX = 3.4028234663852886e38
 PARTS = {"A": (0, 256), "B": (256, 128), "C": (384, 128)}
 
 
@@ -137,13 +138,13 @@ def tile_list_point_pair_max_kernel(
                 in_=raw[a, c0][:, :, m0 : m0 + P].rearrange("p j (c i) -> p c j i", i=4),
             )
 
-        def by_tile(first_slot):
+        def by_tile(first_slot, step):
             view = work[:].bitcast(BF16).rearrange("p (s x) -> p s x", x=K_PASS)
-            return view[:, first_slot : first_slot + 3 : 2, :]
+            return view[:, first_slot : first_slot + step + 1 : step, :]
 
         def cast_pair(a, first_slot):
             nc.gpsimd.tensor_scalar(
-                by_tile(first_slot).rearrange("p u (m j) -> p u m j", j=PACK),
+                by_tile(first_slot, 3).rearrange("p u (m j) -> p u m j", j=PACK),
                 raw[a, 2 * P][:].rearrange("p j (u m) -> p u m j", u=2),
                 1.0,
                 0.0,
@@ -151,8 +152,8 @@ def tile_list_point_pair_max_kernel(
                 ALU.add,
             )
 
-        def cast_dealt(a, r0, first_slot, on_gpsimd):
-            dst = by_tile(first_slot).rearrange("p t (m j) -> p m j t", j=PACK)
+        def cast_dealt(a, r0, first_slot, step, on_gpsimd=False):
+            dst = by_tile(first_slot, step).rearrange("p t (m j) -> p m j t", j=PACK)
             t0 = r0 - PACK
             src = raw[a, K_PASS][:].rearrange("p j (m t) -> p m j t", t=PACK)[:, :, :, t0 : t0 + 2]
             if on_gpsimd:
@@ -187,7 +188,7 @@ def tile_list_point_pair_max_kernel(
             )
 
         h_ps = {}
-        first_bank = [0, 2, 4, 6, 2, 0, 0, 2]
+        first_bank = [0, 2, 4, 0, 0, 2, 2, 0]
 
         def open_half(r, half):
             h_ps[r, half] = bank(first_bank[r] + half, "h_ps_%d_%d" % (r, half))
@@ -378,37 +379,44 @@ def tile_list_point_pair_max_kernel(
         pick_early(0, 0)
         pick_early(0, 1)
         quantize_slots([2], (1, 0), 3)
-        quantize_slots([3], (1, 0), 5)
-        h_passes(2)
+        quantize_slots([3], (1, 0), 6)
+        for n in range(PACK):
+            quarter_ps[n] = bank(4 + n, "h_ps_2_%d" % n)
+            for a in range(2):
+                mx_pass(quarter_ps[n][:, 0:QUARTER], 2, a, n * QUARTER, QUARTER, a == 0, a == 1)
         h_passes(3)
         turn_second(0)
-        cast_dealt(0, 6, 6, True)
-        subtract(slots(4, 2), early[0, 0], early[0, 1])
-        cast_dealt(0, 4, 9, False)
-        h_outs(2)
+        cast_dealt(0, 6, 4, 3, on_gpsimd=True)
+        cast_dealt(0, 4, 9, 2)
+        h[2] = sb([P, S], F32, "h_2")
+        for n in range(PACK):
+            nc.scalar.activation(
+                h[2][:, n * QUARTER : (n + 1) * QUARTER], quarter_ps[n][:, 0:QUARTER], ACT.Relu, bias=bias[2]
+            )
         pick_early(1, 0, slots(2, 2))
         pick_early(1, 1)
         turn_second(1)
-        cast_dealt(1, 4, 10, False)
+        cast_dealt(1, 4, 10, 2)
         h_outs(3)
-        first_excess = placed([P, PAIRS], F32, "first_excess", 33.5)
-        clip(first_excess[:], slots(4, 2))
-        pick_early(2, 0, slots(14, 2))
+        cast_dealt(1, 6, 5, 3)
+        pick_early(2, 0)
         quantize_slots([5], (0, 1), 11)
         quantize_slots([4], (0, 1), 9)
         h_passes(5)
         h_passes(4)
-        cast_dealt(1, 6, 7, True)
+        subtract(slots(10, 2), early[0, 0], early[0, 1])
+        first_excess = placed([P, PAIRS], F32, "first_excess", 33.5)
+        clip(first_excess[:], slots(10, 2))
         pick_early(2, 1, slots(12, 2))
         for n in range(2):
             excess[0, n] = first_excess[:, n * 256 : (n + 1) * 256]
         for j in range(PACK):
             turn_excess(0, j)
         turn_second(2)
-        pick_early(3, 0, slots(10, 2))
-        quantize_slots([6], (0, 1), 6)
-        quantize_slots([7], (0, 1), 8)
-        pick_early(3, 1, slots(6, 2))
+        pick_early(3, 0)
+        quantize_slots([6], (0, 1), 4)
+        quantize_slots([7], (0, 1), 7)
+        pick_early(3, 1, slots(4, 2))
         h_outs(5)
         h_passes(6)
         h_outs(4)
@@ -417,12 +425,15 @@ def tile_list_point_pair_max_kernel(
         for n in range(2):
             for r in (1, 2, 3):
                 cols = slice(n * 256, (n + 1) * 256)
-                excess[r, n] = slots(((8, 9, 10), (2, 14, 11))[n][r - 1], 1)
+                if n == 0:
+                    excess[r, n] = slots({1: 9, 2: 8, 3: 10}[r], 1)
+                else:
+                    excess[r, n] = slots(7, 1) if r == 1 else early[r, 0][:, 0:256]
                 subtract(excess[r, n], early[r, 0][:, cols], early[r, 1][:, cols])
+        for r in (1, 2, 3):
+            nc.gpsimd.tensor_scalar(excess[r, 1], excess[r, 1], F32_MAX, 0.0, ALU.min, ALU.max)
 
         def close_turns(n):
-            for x in [slots(8, 3)] if n == 0 else [excess[r, 1] for r in (1, 2, 3)]:
-                clip(x, x)
             for j in (2 * n, 2 * n + 1):
                 for r in (1, 2, 3):
                     turn_excess(r, j, stop=(r == 3))
@@ -430,21 +441,22 @@ def tile_list_point_pair_max_kernel(
         for side in range(2):
             pick_late(5, side)
         h_outs(6)
+        clip(slots(8, 3), slots(8, 3))
         close_turns(0)
-        for j in range(2):
-            round_turned(j)
         h_outs(7)
         close_turns(1)
-        first_words = placed([P, PAIRS], F32, "first_words", 76)
-        turn_back(0, 0, [first_words[:, 0:256], late_places(16, 1)])
+        for j in range(2):
+            round_turned(j)
         for side in range(2):
             pick_late(4, side)
-        for j in range(2, PACK):
-            round_turned(j)
+        round_turned(2)
+        first_words = placed([P, PAIRS], F32, "first_words", 76)
+        turn_back(0, 2, [first_words[:, 0:256], late_places(16, 1)])
+        round_turned(3)
         rest_words = sb([P, PAIRS], F32, "rest_words")
-        turn_back(2, 2, [rest_words[:]])
+        turn_back(2, 0, [rest_words[:]])
 
-        banks_of = {"A": (4, 4, 5, 5, 1, 1), "B": (6, 6, 6, 7, 7, 7), "C": (3, 3, 3, 0, 0, 2)}
+        banks_of = {"A": (4, 4, 5, 5, 3, 3), "B": (6, 6, 6, 7, 7, 7), "C": (1, 1, 1, 2, 2, 0)}
         o_bank, o_ps, staged = {}, {}, {}
         out_v = out.rearrange("(c p) q -> p c q", p=P)
 

from contextlib import ExitStack

import concourse.mybir as mybir
from concourse.masks import make_identity

K, T, S, PAIRS, H, N = 1024, 4096, 1024, 512, 1024, 768
FLOPS = 2 * K * H * S + 2 * H * N * PAIRS

F32 = mybir.dt.float32
BF16 = mybir.dt.bfloat16
I32 = mybir.dt.int32
U32 = mybir.dt.uint32
U16 = mybir.dt.uint16
U8 = mybir.dt.uint8
FP8X4 = mybir.dt.float8_e4m3fn_x4
FP4X4 = mybir.dt.float4_e2m1fn_x4
ACT = mybir.ActivationFunctionType
ALU = mybir.AluOpType

P = 128
PACK = 4
K_PASS = P * PACK
BANK = 512
LIST_ROWS = 16
N_TILES = N // P
QUAD = 32
QUARTER = 256
SLOT = 256
F32_MAX = 3.4028234663852886e38
PARTS = {"A": (0, 256), "B": (256, 128), "C": (384, 128)}


def tile_list_point_pair_max_kernel(
    tc, tab_words, tab_scales, w1, b1, w2_words, w2_scales, b2, offs, pos1, pos2, out
):
    nc = tc.nc
    with ExitStack() as ctx:
        lists = ctx.enter_context(tc.tile_pool(name="lists", bufs=1))
        keep = ctx.enter_context(tc.tile_pool(name="keep", bufs=1))
        reused = ctx.enter_context(tc.tile_pool(name="reused", bufs=1))
        psum = ctx.enter_context(tc.psum_pool(name="psum", bufs=1))

        def sb(shape, dtype, name):
            return keep.tile(shape, dtype, name=name, tag=name, align_bytes=64)

        def placed(shape, dtype, name, kib):
            return reused.tile(shape, dtype, name=name, tag=name, offset=int(kib * 1024), align_bytes=64)

        def bank(i, name):
            return psum.tile([P, BANK], F32, name=name, tag="bank%d" % i)

        offs_sb = lists.tile([P, S // LIST_ROWS], U16, name="offs_sb")
        pos_sb = [lists.tile([P, PAIRS // LIST_ROWS], U16, name="pos%d_sb" % i) for i in (1, 2)]

        tab_w = {}
        tab_s = placed([P, T], U8, "tab_s", 44.5)
        g_s = sb([P, S], U8, "g_s")
        v_s = [sb([P, S], U8, "v_s%d" % a) for a in range(2)]

        ident = sb([P, P], F32, "ident")
        make_identity(nc, ident[:])
        nc.vector.memset(tab_s[QUAD : 2 * QUAD, :].bitcast(I32), 0)
        nc.vector.memset(tab_s[2 * QUAD :, :].bitcast(I32), 0)
        for a in range(2):
            nc.vector.memset(v_s[a][:].bitcast(I32), 0)

        def move_scales(a, q):
            nc.sync.dma_start(
                out=v_s[a][QUAD * q : QUAD * q + 4, :].bitcast(I32),
                in_=g_s[16 * a + 4 * q : 16 * a + 4 * q + 4, :].bitcast(I32),
            )

        def load_table(a):
            tab_w[a] = placed([P, T], I32, "tab_w%d" % a, 12 + 17 * a)
            nc.sync.dma_start(out=tab_w[a][:], in_=tab_words[a].rearrange("p t i -> p (t i)").bitcast(I32))

        raw = {}

        def load_w1(a, c0, cn, kib):
            raw[a, c0] = placed([P, PACK, cn], F32, "w1_raw_%d_%d" % (a, c0), kib)
            block = w1[a * K_PASS : (a + 1) * K_PASS, c0 : c0 + cn]
            nc.sync.dma_start(out=raw[a, c0][:], in_=block.rearrange("(p j) c -> p j c", j=PACK))

        work = placed([P, 16 * SLOT], F32, "work", 60)

        def slots(first, count):
            return work[:, first * SLOT : (first + count) * SLOT]

        bias = {}

        def load_bias(r, column):
            with nc.allow_non_contiguous_dma(reason="one bias value to a partition"):
                nc.sync.dma_start(out=column, in_=b1[r * P : (r + 1) * P].rearrange("(p o) -> p o", o=1))
            bias[r] = column

        nc.sync.dma_start(
            out=tab_s[0:QUAD, :].bitcast(I32), in_=tab_scales.rearrange("a q t -> (a q) t").bitcast(I32)
        )
        nc.sync.dma_start(offs_sb[:], offs)
        nc.sync.dma_start(pos_sb[0][:], pos1)
        nc.sync.dma_start(pos_sb[1][:], pos2)
        load_table(0)
        load_w1(0, 0, 2 * P, 82)

        nc.vector.tensor_copy(g_s[:], tab_s[:].indirect(offs_sb[:]))
        moves = [(a, q) for a in range(2) for q in range(4)]
        for a, q in moves[:5]:
            move_scales(a, q)
        load_table(1)
        for a, q in moves[5:]:
            move_scales(a, q)
        load_w1(1, 0, P, 45.5)
        load_bias(0, placed([P, 1], F32, "b1_0", 45)[:])
        load_w1(1, P, P, 48)

        v_w0 = sb([P, S], U32, "v_w0")
        v_w1 = {}

        def gather_words(a, dst, j0, jn):
            nc.vector.tensor_copy(
                dst, tab_w[a][:].bitcast(U32).indirect(offs_sb[:, j0 // LIST_ROWS : (j0 + jn) // LIST_ROWS])
            )

        def v_words(a, j0, jn):
            if a == 0:
                return v_w0[:, j0 : j0 + jn]
            if j0 < 3 * QUARTER:
                return v_w1[0][:, j0 : j0 + jn]
            return v_w1[1][:, j0 - 3 * QUARTER : j0 - 3 * QUARTER + jn]

        rounded, codes, planes = {}, {}, {}

        def cast_plain(a, r, c0, dst):
            rounded[r, a] = dst
            m0 = r * P - c0
            nc.scalar.copy(
                out=dst.rearrange("p (c i j) -> p c j i", i=4, j=PACK),
                in_=raw[a, c0][:, :, m0 : m0 + P].rearrange("p j (c i) -> p c j i", i=4),
            )

        def by_tile(first_slot, step):
            view = work[:].bitcast(BF16).rearrange("p (s x) -> p s x", x=K_PASS)
            return view[:, first_slot : first_slot + step + 1 : step, :]

        def cast_pair(a, first_slot):
            nc.gpsimd.tensor_scalar(
                by_tile(first_slot, 3).rearrange("p u (m j) -> p u m j", j=PACK),
                raw[a, 2 * P][:].rearrange("p j (u m) -> p u m j", u=2),
                1.0,
                0.0,
                ALU.mult,
                ALU.add,
            )

        def cast_dealt(a, r0, first_slot, step, on_gpsimd=False):
            dst = by_tile(first_slot, step).rearrange("p t (m j) -> p m j t", j=PACK)
            t0 = r0 - PACK
            src = raw[a, K_PASS][:].rearrange("p j (m t) -> p m j t", t=PACK)[:, :, :, t0 : t0 + 2]
            if on_gpsimd:
                nc.gpsimd.tensor_scalar(
                    dst.rearrange("p m j t -> p t m j"), src.rearrange("p m j t -> p t m j"), 1.0, 0.0, ALU.mult, ALU.add
                )
            else:
                nc.scalar.copy(out=dst, in_=src)

        def quantize_w1(operands, src):
            n = len(operands) * P
            c = sb([P, n], U32, "w1_c_%d_%d" % operands[0])
            s = sb([P, n], U8, "w1_s_%d_%d" % operands[0])
            nc.vector.quantize_mx(out=c[:].bitcast(FP8X4), scales=s[:], in_=src)
            for i, key in enumerate(operands):
                codes[key] = c[:, i * P : (i + 1) * P]
                planes[key] = s[:, i * P : (i + 1) * P]

        def quantize_slots(tiles, passes, first_slot):
            operands = [(r, a) for a in passes for r in tiles]
            quantize_w1(operands, slots(first_slot, len(operands)).bitcast(BF16))

        def mx_pass(dst, r, a, j0, jn, start, stop):
            nc.tensor.matmul_mx(
                out=dst,
                lhsT=codes[r, a].bitcast(FP8X4),
                lhsT_scale=planes[r, a],
                rhs=v_words(a, j0, jn).bitcast(FP8X4),
                rhs_scale=v_s[a][:, j0 : j0 + jn],
                start=start,
                stop=stop,
            )

        h_ps = {}
        first_bank = [0, 2, 4, 0, 0, 2, 2, 0]

        def open_half(r, half):
            h_ps[r, half] = bank(first_bank[r] + half, "h_ps_%d_%d" % (r, half))
            mx_pass(h_ps[r, half][:], r, 0, half * BANK, BANK, True, False)

        def close_half(r, half):
            if half == 0:
                mx_pass(h_ps[r, 0][:], r, 1, 0, BANK, False, True)
            else:
                mx_pass(h_ps[r, 1][:, 0:QUARTER], r, 1, 2 * QUARTER, QUARTER, False, False)
                mx_pass(h_ps[r, 1][:, QUARTER:], r, 1, 3 * QUARTER, QUARTER, False, True)

        def h_passes(r):
            for half in range(2):
                open_half(r, half)
                close_half(r, half)

        h = {}

        def h_outs(r):
            h[r] = sb([P, S], F32, "h_%d" % r)
            column = bias[r] if r < PACK else b1_hi[:, r - PACK : r - PACK + 1]
            for half in range(2):
                nc.scalar.activation(
                    h[r][:, half * BANK : (half + 1) * BANK], h_ps[r, half][:], ACT.Relu, bias=column
                )

        quarter_ps = {}

        def first_pass(a, n):
            if a == 0:
                quarter_ps[n] = bank((0, 1, 4, 5)[n], "h_ps_0_%d" % n)
            mx_pass(quarter_ps[n][:, 0:QUARTER], 0, a, n * QUARTER, QUARTER, a == 0, a == 1)

        def first_out(n):
            dst = h[0][:, n * QUARTER : (n + 1) * QUARTER]
            if n == 1:
                nc.vector.tensor_scalar(dst, quarter_ps[n][:, 0:QUARTER], bias[0], 0.0, ALU.add, ALU.max)
            else:
                nc.scalar.activation(dst, quarter_ps[n][:, 0:QUARTER], ACT.Relu, bias=bias[0])

        def looked_up(r, side, q0, qn):
            return h[r][:].indirect(pos_sb[side][:, q0 // LIST_ROWS : (q0 + qn) // LIST_ROWS])

        early = {}

        def pick_early(r, side, dst=None):
            early[r, side] = dst if dst is not None else sb([P, PAIRS], F32, "early_%d_%d" % (r, side))[:]
            nc.vector.tensor_copy(early[r, side], looked_up(r, side, 0, PAIRS))

        excess = {}

        def subtract(dst, first, second):
            nc.gpsimd.tensor_tensor(dst, first, second, ALU.subtract)

        def clip(dst, src):
            nc.scalar.activation(dst, src, ACT.Relu)

        turned_ps = {}

        def turn(r, j, src, start=False, stop=False):
            if start:
                turned_ps[j] = bank(4 + j, "turned_ps_%d" % j)
            dst = turned_ps[j][:, r * P : (r + 1) * P]
            nc.tensor.matmul(dst, lhsT=src, rhs=ident[:], is_transpose=True, start=start, stop=stop)

        def turn_second(r):
            for j in range(PACK):
                turn(r, j, early[r, 1][:, j * P : (j + 1) * P], start=(r == 0))

        def turn_excess(r, j, stop=False):
            turn(r, j, excess[r, j // 2][:, j % 2 * P : (j % 2 + 1) * P], stop=stop)

        turned = {}

        def round_turned(j):
            turned[j] = sb([P, 2 * P], F32, "turned_%d" % j)
            nc.scalar.copy(
                out=turned[j][:].bitcast(BF16).rearrange("q (e p i) -> q e p i", e=2, i=2),
                in_=turned_ps[j][:].rearrange("q (p e i) -> q e p i", e=2, i=2),
            )

        def turn_back(j0, bank_no, pieces):
            ps = bank(bank_no, "back_%d" % j0)
            for jj in range(2):
                for e in range(2):
                    place = (2 * jj + e) * P
                    nc.tensor.transpose(ps[:, place : place + P], turned[j0 + jj][:, e * P : (e + 1) * P], ident[:])
            n = 2 // len(pieces)
            for i, words in enumerate(pieces):
                nc.scalar.copy(
                    out=words.rearrange("p (n q e) -> p n q e", n=n, e=2),
                    in_=ps[:, i * n * 256 : (i + 1) * n * 256].rearrange("p (n e q) -> p n q e", n=n, e=2),
                )

        late = placed([P, 17 * 256], F32, "late", 43)
        late_at = {(1, 0): (0, 1), (1, 1): (5, 2), (0, 0): (9, 2), (0, 1): (10, 2)}
        late_view = late[:].rearrange("p (s q) -> p s q", q=256)

        def late_places(first, count):
            return late[:, first * 256 : (first + count) * 256]

        def pick_late(r, side, q0=0, qn=PAIRS):
            at = [late_at[side, n][0] + late_at[side, n][1] * (r - PACK) for n in range(2)]
            if qn == PAIRS:
                dst = late_view[:, at[0] : at[1] + 1 : at[1] - at[0], :]
            else:
                dst = late_places(at[q0 // 256], 1)[:, q0 % 256 : q0 % 256 + qn]
            nc.vector.tensor_copy(dst, looked_up(r, side, q0, qn))

        z_c, z_s = {}, {}

        def late_max(part, words):
            q0, qn = PARTS[part]
            sides = []
            for side in range(2):
                first, step = late_at[side, q0 // 256]
                tiles = late_view[:, first : first + 3 * step + 1 : step, q0 % 256 : q0 % 256 + qn]
                sides.append(tiles.rearrange("p t (c i) -> p c t i", i=4))
            nc.vector.tensor_tensor(
                words.bitcast(BF16).rearrange("p (c i t) -> p c t i", i=4, t=PACK), sides[0], sides[1], ALU.max
            )

        def quantize_z(b, parts, pieces, kib=None):
            qn = sum(PARTS[part][1] for part in parts)
            name = "z_c_%d_%s" % (b, parts)
            c = sb([P, qn], U32, name) if kib is None else placed([P, qn], U32, name, kib)
            s = sb([P, qn], U8, "z_s_%d_%s" % (b, parts))
            n = qn // len(pieces)
            for i, words in enumerate(pieces):
                cols = slice(i * n, (i + 1) * n)
                nc.vector.quantize_mx(out=c[:, cols].bitcast(FP8X4), scales=s[:, cols], in_=words.bitcast(BF16))
            for part in parts:
                q0 = PARTS[part][0] - PARTS[parts[0]][0]
                z_c[b, part] = c[:, q0 : q0 + PARTS[part][1]]
                z_s[b, part] = s[:, q0 : q0 + PARTS[part][1]]

        gather_words(0, v_w0[:], 0, S)
        load_w1(1, 2 * P, 2 * P, 12.5)
        load_w1(0, 2 * P, 2 * P, 16.5)
        load_bias(1, placed([P, 1], F32, "b1_1", 20.5)[:])
        load_w1(0, K_PASS, K_PASS, 21)
        for r in range(2):
            cast_plain(0, r, 0, sb([P, K_PASS], BF16, "w1_r_%d_0" % r)[:])
            quantize_w1([(r, 0)], rounded[r, 0])
        w2_s = placed([P, 2, N], U8, "w2_s", 82)
        nc.vector.memset(w2_s[:].rearrange("p b n -> p (b n)").bitcast(I32), 0)
        for n in range(PACK):
            first_pass(0, n)
        for half in range(2):
            open_half(1, half)
        v_w1[0] = sb([P, 3 * QUARTER], U32, "v_w1_0")
        gather_words(1, v_w1[0][:], 0, 3 * QUARTER)
        cast_plain(1, 0, 0, placed([P, K_PASS], BF16, "w1_r_0_1", 80)[:])
        quantize_w1([(0, 1)], rounded[0, 1])
        v_w1[1] = placed([P, QUARTER], U32, "v_w1_1", 80)
        gather_words(1, v_w1[1][:], 3 * QUARTER, QUARTER)
        cast_plain(1, 1, P, sb([P, K_PASS], BF16, "w1_r_1_1")[:])
        quantize_w1([(1, 1)], rounded[1, 1])

        b1_hi = placed([P, PACK], F32, "b1_hi", 32.5)
        w2_w = placed([P, 2, 2 * N], U8, "w2_w", 29)
        b2_sb = placed([P, N_TILES], F32, "b2_sb", 32.25)
        load_bias(2, placed([P, 1], F32, "b1_2", 32.75)[:])
        load_w1(1, K_PASS, K_PASS, 36)
        load_bias(3, placed([P, 1], F32, "b1_3", 33.5)[:])
        nc.sync.dma_start(out=b1_hi[:], in_=b1[K_PASS:].rearrange("(p t) -> p t", t=PACK))
        nc.sync.dma_start(out=w2_w[:].bitcast(I32), in_=w2_words.rearrange("b p n -> p b n").bitcast(I32))
        for q in range(4):
            nc.sync.dma_start(
                out=w2_s[QUAD * q : QUAD * q + 4, :, :].bitcast(I32),
                in_=w2_scales[:, 4 * q : 4 * q + 4, :].rearrange("b r n -> r b n").bitcast(I32),
            )
        with nc.allow_non_contiguous_dma(reason="one bias value to a partition"):
            nc.sync.dma_start(out=b2_sb[:], in_=b2.rearrange("(c p) -> p c", p=P))

        for n in range(PACK):
            first_pass(1, n)
        for half in range(2):
            close_half(1, half)
        h[0] = sb([P, S], F32, "h_0")
        for n in range(PACK):
            first_out(n)

        cast_pair(1, 3)
        cast_pair(0, 4)
        h_outs(1)
        pick_early(0, 0)
        pick_early(0, 1)
        quantize_slots([2], (1, 0), 3)
        quantize_slots([3], (1, 0), 6)
        for n in range(PACK):
            quarter_ps[n] = bank(4 + n, "h_ps_2_%d" % n)
            for a in range(2):
                mx_pass(quarter_ps[n][:, 0:QUARTER], 2, a, n * QUARTER, QUARTER, a == 0, a == 1)
        h_passes(3)
        turn_second(0)
        cast_dealt(0, 6, 4, 3, on_gpsimd=True)
        cast_dealt(0, 4, 9, 2)
        h[2] = sb([P, S], F32, "h_2")
        for n in range(PACK):
            nc.scalar.activation(
                h[2][:, n * QUARTER : (n + 1) * QUARTER], quarter_ps[n][:, 0:QUARTER], ACT.Relu, bias=bias[2]
            )
        pick_early(1, 0, slots(2, 2))
        pick_early(1, 1)
        turn_second(1)
        cast_dealt(1, 4, 10, 2)
        h_outs(3)
        cast_dealt(1, 6, 5, 3)
        pick_early(2, 0)
        quantize_slots([5], (0, 1), 11)
        quantize_slots([4], (0, 1), 9)
        h_passes(5)
        h_passes(4)
        subtract(slots(10, 2), early[0, 0], early[0, 1])
        first_excess = placed([P, PAIRS], F32, "first_excess", 33.5)
        clip(first_excess[:], slots(10, 2))
        pick_early(2, 1, slots(12, 2))
        for n in range(2):
            excess[0, n] = first_excess[:, n * 256 : (n + 1) * 256]
        for j in range(PACK):
            turn_excess(0, j)
        turn_second(2)
        pick_early(3, 0)
        quantize_slots([6], (0, 1), 4)
        quantize_slots([7], (0, 1), 7)
        pick_early(3, 1, slots(4, 2))
        h_outs(5)
        h_passes(6)
        h_outs(4)
        h_passes(7)
        turn_second(3)
        for n in range(2):
            for r in (1, 2, 3):
                cols = slice(n * 256, (n + 1) * 256)
                if n == 0:
                    excess[r, n] = slots({1: 9, 2: 8, 3: 10}[r], 1)
                else:
                    excess[r, n] = slots(7, 1) if r == 1 else early[r, 0][:, 0:256]
                subtract(excess[r, n], early[r, 0][:, cols], early[r, 1][:, cols])
        for r in (1, 2, 3):
            nc.gpsimd.tensor_scalar(excess[r, 1], excess[r, 1], F32_MAX, 0.0, ALU.min, ALU.max)

        def close_turns(n):
            for j in (2 * n, 2 * n + 1):
                for r in (1, 2, 3):
                    turn_excess(r, j, stop=(r == 3))

        for side in range(2):
            pick_late(5, side)
        h_outs(6)
        clip(slots(8, 3), slots(8, 3))
        close_turns(0)
        h_outs(7)
        close_turns(1)
        for j in range(2):
            round_turned(j)
        for side in range(2):
            pick_late(4, side)
        round_turned(2)
        first_words = placed([P, PAIRS], F32, "first_words", 76)
        turn_back(0, 2, [first_words[:, 0:256], late_places(16, 1)])
        round_turned(3)
        rest_words = sb([P, PAIRS], F32, "rest_words")
        turn_back(2, 0, [rest_words[:]])

        banks_of = {"A": (4, 4, 5, 5, 3, 3), "B": (6, 6, 6, 7, 7, 7), "C": (1, 1, 1, 2, 2, 0)}
        o_bank, o_ps, staged = {}, {}, {}
        out_v = out.rearrange("(c p) q -> p c q", p=P)

        def out_passes(b, part):
            qn = PARTS[part][1]
            mine = banks_of[part]
            for c in range(N_TILES):
                first = mine.index(mine[c])
                last = first + len([i for i in mine if i == mine[c]]) - 1
                if b == 0:
                    if c == first:
                        o_bank[mine[c]] = bank(mine[c], "o_%s_%d" % (part, c))
                    o_ps[part, c] = o_bank[mine[c]][:, (c - first) * qn : (c - first + 1) * qn]
                nc.tensor.matmul_mx(
                    out=o_ps[part, c],
                    lhsT=w2_w[:, b, 2 * P * c : 2 * P * (c + 1)].bitcast(FP4X4),
                    lhsT_scale=w2_s[:, b, P * c : P * (c + 1)],
                    rhs=z_c[b, part].bitcast(FP8X4),
                    rhs_scale=z_s[b, part],
                    start=(b == 0 and c == first),
                    stop=(b == 1 and c == last),
                )

        def finish(part, on_vector=()):
            q0, qn = PARTS[part]
            mine = banks_of[part]
            staged[part] = sb([P, N_TILES, qn], F32, "staged_" + part)
            for c in range(N_TILES):
                if c in on_vector:
                    nc.vector.tensor_scalar_add(staged[part][:, c, :], o_ps[part, c], b2_sb[:, c : c + 1])
                else:
                    nc.scalar.activation(staged[part][:, c, :], o_ps[part, c], ACT.Identity, bias=b2_sb[:, c : c + 1])
                if c == N_TILES - 1 or mine[c + 1] != mine[c]:
                    first = mine.index(mine[c])
                    nc.sync.dma_start(
                        out=out_v[:, first : c + 1, q0 : q0 + qn], in_=staged[part][:, first : c + 1, :]
                    )

        spare = {part: sb([P, 2 * PARTS[part][1]], F32, "z_words_" + part) for part in "BC"}
        pick_late(6, 1, *PARTS["A"])
        pick_late(6, 0)
        pick_late(7, 1, *PARTS["A"])
        pick_late(7, 0, *PARTS["A"])
        quantize_z(0, "A", [first_words[:, 0:256], late_places(16, 1)])
        out_passes(0, "A")
        late_max("A", first_words[:])
        pick_late(7, 0, 256, 256)
        quantize_z(1, "A", [first_words[:]])
        out_passes(1, "A")
        finish("A")
        pick_late(6, 1, *PARTS["B"])
        quantize_z(0, "BC", [rest_words[:]], 76)
        out_passes(0, "B")
        pick_late(7, 1, *PARTS["B"])
        pick_late(6, 1, *PARTS["C"])
        out_passes(0, "C")
        late_max("B", spare["B"][:])
        pick_late(7, 1, *PARTS["C"])
        quantize_z(1, "B", [spare["B"][:]])
        out_passes(1, "B")
        finish("B")
        late_max("C", spare["C"][:])
        quantize_z(1, "C", [spare["C"][:]])
        out_passes(1, "C")
        finish("C", on_vector=(0, 1, 2, 5))
